import numpy as np, ml_dtypes
CORES = [66,74,82,90,194,202,210,218]
N = 8
import mx_ref
BF = ml_dtypes.bfloat16
def gentries(a):
    return np.ascontiguousarray(a.reshape(8, 16, -1).transpose(0, 2, 1)).reshape(8, -1)
def gtable(e):
    e = np.asarray(e); return np.ascontiguousarray(e.reshape(8, -1, 16).transpose(0, 2, 1)).reshape(128, -1).astype(np.int32)
def gcols(t, e):
    v = np.concatenate([t.reshape(8, 16, -1, 4), np.zeros((8, 16, 1, 4), BF)], axis=2)
    return np.ascontiguousarray(np.stack([v[g][:, e[g]] for g in range(8)])).reshape(128, -1)
def gpick(z, e):
    return np.concatenate([z[16 * g:16 * g + 16][:, e[g]] for g in range(8)])
def tile(rs):
    return np.stack(rs, axis=2).reshape(128, -1).astype(BF)
def pick(q, e):
    c = np.concatenate([q[0].reshape(128, -1, 4), np.zeros((128, 1, 4), np.uint8)], axis=1); s = np.concatenate([q[1], np.ones((16, 1), np.uint8)], axis=1)
    return (np.ascontiguousarray(c[:, e].reshape(128, -1)), np.ascontiguousarray(s[:, e]))
def join(*qs):
    return (np.concatenate([q[0] for q in qs], axis=1), np.concatenate([q[1] for q in qs], axis=1))
def put(q, e, v):
    c, s = q[0].reshape(128, -1, 4).copy(), q[1].copy(); c[:, e] = v[0].reshape(128, -1, 4); s[:, e] = v[1]
    return (c.reshape(128, -1), s)
def pk(c, s):
    return (np.ascontiguousarray(c), mx_ref.live(s))
def emit(q):
    return q[0], q[1]
def packed(v, rng):
    q = [mx_ref.quantize(np.ascontiguousarray(v[r])) for r in range(N)]
    return np.stack([a for a, b in q]), np.stack([mx_ref.plane(b, rng) for a, b in q])
def values_of_codes():
    e, c = np.zeros((128, 128, 4), np.float32), np.zeros((128, 2, 4), np.uint8)
    e[np.arange(128), np.arange(128), 0] = 1
    c[:127, :, 0] = np.arange(256).reshape(2, 128).T[:127]
    return mx_ref.matmul(mx_ref.quantize(e.reshape(128, 512).astype(BF)), (c.reshape(128, 8), np.full((16, 2), 127, np.uint8))).T.reshape(-1).astype(np.float64)
CODE_VALUE, SCALE_VALUE = values_of_codes(), 2.0 ** (np.arange(256) - 127.0)
def decode(q):
    return (CODE_VALUE[q[0]].reshape(16, 8, -1, 4) * SCALE_VALUE[q[1]][:, None, :, None] + 0.0).reshape(128, -1).astype(np.float32)
def f(rng, *shape):
    return mx_ref.flush((rng.standard_normal(shape, dtype=np.float32) * np.exp2(rng.integers(-2, 3, shape[:-1] + (1,)))).astype(BF))
def wide(rng, *shape, cols=0):
    v = rng.standard_normal(shape, dtype=np.float32) * np.exp2(rng.integers(-12, 13, shape)).astype(np.float32)
    if cols: v *= np.repeat(np.exp2(rng.integers(-cols, cols + 1, shape[:-2] + (1, shape[-1] // 4))) * (rng.random(shape[:-2] + (1, shape[-1] // 4)) > 0.0625), 4, axis=-1).astype(np.float32)
    return mx_ref.flush(v.astype(BF))
C = 288
STEP = [4, 1, 2]
def numbers_of(rng):
    return {"x": np.array(f(rng, N, 128, 4 * C)), "u": np.array(f(rng, N, 128, 512)), "v": np.array(f(rng, N, 128, 512))}
def orders(rng):
    return rng.permuted(np.tile(np.arange(C), (N, 8, 1)), axis=2), rng.permuted(np.tile(np.arange(8)[:, None], (N, 1, C)), axis=1)
def stored(p, o):
    return {"pg": np.stack([gtable(p[r]) for r in range(N)]), "og": np.stack([gtable(o[r]) for r in range(N)])}
def layers(rng, still=[]):
    w = np.array(f(rng, N, 128, 2048)).reshape(N, 8, 16, 4, 8, 16, 4)
    for i in still:
        w[:, :, i] = 0
        w[:, :, :, :, :, i] = 0
    return w
def weights(rng, w):
    c, s = packed(np.ascontiguousarray(w).reshape(N, 128, 2048), rng)
    return {"wc": c, "ws": s}
def setup_inputs(rng):
    return {**numbers_of(rng), **stored(*orders(rng)), **weights(rng, layers(rng))}
def setup_inputs_ties(rng):
    d = numbers_of(rng)
    n = rng.permutation(N)
    k = rng.integers(0, 4, (N, 8, C))
    k[n[1]] -= 4
    k[n[2]] = np.arange(8)[:, None]
    x = d["x"].reshape(N, 8, 16, C, 4)
    x[:, :, 0] = 0
    x[:, :, 0, :, 0] = k.astype(np.float32).astype(BF)
    u = d["u"].reshape(N, 128, 128, 4)
    u[:, :, ::16] = 0
    for r in range(N):
        for h in range(0, 128, 16): u[r, h, h, 0] = 0.0 if r == n[0] else 1.0
    p, o = orders(rng)
    o[n[2]] = 7 - np.arange(8)[:, None]
    return {"x": x.reshape(N, 128, 4 * C), "u": u.reshape(N, 128, 512), "v": d["v"], **stored(p, o), **weights(rng, layers(rng, [0]))}
def setup_inputs_near(rng):
    d = numbers_of(rng)
    x = d["x"].astype(np.float32).reshape(N, 8, 16, C, 4)
    x[:, :, 0] = 0
    x[:, :, 8:] = 0
    u = d["u"].reshape(N, 128, 128, 4)
    u[:, :, ::16] = 0
    w = layers(rng, [0, 8, 9, 10, 11, 12, 13, 14, 15])
    kind, size, least = np.zeros(N, np.int64), np.ones(N), 2.0 ** -30
    turn = rng.integers(2)
    for i, r in enumerate(rng.permutation([r for r in range(N) if r < r ^ STEP[0]])):
        both = [r, r ^ STEP[0]]
        kind[both] = 2 if i == 0 else rng.permutation(2)
        size[both] = least if (i + turn) % 2 else 1.0
    for r in range(N):
        s = rng.integers(0, 16, (8, C))
        digits = ((s[:, :, None] >> np.arange(4)) & 1) * np.exp2(np.arange(4) - 23.0)
        if kind[r] == 0:
            x[r, :, 0, :, 0] = rng.choice([-1.0, 1.0])
            x[r, :, 8] = digits
            x[r, :, 11, :, 0] = 2.0 ** -10
        if kind[r] == 1: x[r, :, 8] = digits * rng.choice([-1.0, 1.0], (8, C, 1))
        if kind[r] == 2:
            e = rng.integers(-1, 2, (8, C)) * least
            x[r, :, 8, :, 0] = 1.25 * e
            x[r, :, 9, :, 0] = -1.125 * e
            x[r, :, 13, :, 0] = rng.choice([-1.0, 1.0], (8, C)) * least
            for g in range(8): w[r, g, 13, 0, g, 12, 0] = 2.0 ** -8
        for g, j in zip(rng.permutation(8)[:4], [0, C - 1, int(rng.integers(C)), int(rng.integers(C))]): x[r, g, 0, j, 0] = 2.0 ** 29 * rng.choice([-1.0, 1.0])
        k = size[r] if kind[r] == 0 else least
        for h in range(0, 128, 16):
            u[r, h, h, 0] = k if kind[r] == 0 else 1.0
            if kind[r] == 0: u[r, h + 11, h, 0] = k
            if kind[r] < 2: u[r, h + 8, h] = k
            else:
                u[r, h + 8, h, 0] = k
                u[r, h + 9, h, 0] = 1.125 * k
                u[r, h + 12, h, 0] = k
    return {"x": x.reshape(N, 128, 4 * C).astype(BF), "u": u.reshape(N, 128, 512), "v": d["v"], **stored(*orders(rng)), **weights(rng, w)}
def setup_inputs_odd(rng):
    d = numbers_of(rng)
    x = (1.0 + (2 * rng.integers(0, 64, (N, 16, 8, C, 4)) + 1) * 2.0 ** -7) * np.exp2(-rng.integers(0, 7, (N, 16, 8, C, 4)).astype(np.float64)) * rng.choice([-1.0, 1.0], (N, 16, 8, C, 4))
    x[:, :, 0, :, 0] = 1.96875 * 2.0 ** 8 * rng.choice([-1.0, 1.0], (16, 1))
    u = d["u"].reshape(N, 16, 8, 128, 4)
    u[:, :, 0, ::16] = 0
    w = layers(rng, [0, 8])
    for g in range(8):
        for i in (0, 8): w[:, g, i, 0, g, i, 0] = -0.5
    return {"x": x.astype(np.float32).reshape(N, 128, 4 * C).astype(BF), "u": u.reshape(N, 128, 512), "v": d["v"], **stored(*orders(rng)), **weights(rng, w)}
def setup_inputs_ends(rng):
    d = numbers_of(rng)
    n, e, c = [rng.permutation(N) % 4 for _ in range(3)]
    low, tiny = 2.0 ** 29, 2.0 ** -30
    def small(*s): return (1 + 0.125 * rng.integers(0, 8, s)) * tiny
    x = np.zeros((N, 8, 16, C, 4))
    u = d["u"].astype(np.float32).reshape(N, 8, 16, 128, 4)
    v = d["v"].astype(np.float32)
    w = np.zeros((N, 128, 4, 128, 4), np.float32)
    i = np.arange(128)
    p, o = orders(rng)
    for r in range(N):
        h = rng.permutation(8)
        a = np.where(h < 2, 0.0, h % 2 * 2.0 - 1.0)[:, None]
        k = np.full(16, 4.0)
        k[15] = 0
        if n[r] < 2:
            x[r] = -(1 + 0.125 * rng.integers(0, 4, (8, 16, C, 4))) * low
            if n[r] == 1: x[r] *= rng.choice([-1.0, 1.0], (C, 1))
            x[r, :, 15] = 2.0 ** 16 * rng.choice([-1.0, 1.0], (8, C, 4))
            u[r, :, :, ::16] = a * 2.0 ** 30
            v[r] = rng.choice([-1.0, 1.0], (128, 512)) * (1 + 0.125 * rng.integers(4, 9, (128, 512))) * low
        elif n[r] == 2:
            x[r] = -small(8, 16, C, 4)
            u[r, :, :, ::16] = a * small(8, 16, 8, 4)
            u[r, :, 14:, ::16] = 0
            v[r] = rng.choice([-1.0, 1.0], (128, 512)) * small(128, 512)
            k[:] = 0
            k[14], k[15] = 2.0 ** -8, 2.0 ** 8
        else:
            x[r] = d["x"][r].astype(np.float32).reshape(8, 16, C, 4)[:, :, :1]
            u[r, :, :, ::16] *= np.abs(a).astype(np.float32)
        for b in range(4): w[r, i, b, i, b] = np.tile(k, 8)
        if e[r] < 3: p[r] = [np.arange(C), np.arange(C)[::-1], (np.arange(C) + 1) % C][e[r]]
        up = np.arange(8)[:, None]
        if c[r] < 3: o[r] = np.where([np.ones(C, bool), np.zeros(C, bool), rng.random(C) < 0.5][c[r]], up, 7 - up)
    return {"x": x.astype(np.float32).reshape(N, 128, 4 * C).astype(BF), "u": u.reshape(N, 128, 512).astype(BF), "v": v.astype(BF), **stored(p, o), **weights(rng, w.astype(BF))}
def setup_inputs_spread(rng):
    d = setup_inputs(rng)
    d["x"] = wide(rng, N, 128, 4 * C, cols=6)
    return d
def check_inputs(d):
    b = []
    for k in ("x", "u", "v"):
        a = np.abs(d[k].astype(np.float32))
        if not (np.isfinite(a).all() and ((a == 0) | (a >= 2.0 ** -30) & (a <= 2.0 ** 30)).all()): b.append("a value of " + k)
    none, least, most = [emit(mx_ref.quantize(np.full((128, 16), k, np.float32).astype(BF)))[1][0, 0] for k in (0.0, 2.0 ** -8, 2.0 ** 8)]
    for r in range(N):
        if not (np.sort(gentries(d["pg"][r]), axis=1) == np.arange(C)).all(): b.append("pg: a group's entries aren't all columns")
        if not (np.sort(gentries(d["og"][r]), axis=0) == np.arange(8)[:, None]).all(): b.append("og: a column's entries aren't all groups")
        if ((d["wc"][r] == 0x7F) | (d["wc"][r] == 0xFF)).any(): b.append("wc: a code that is no number")
        s = mx_ref.live(d["ws"][r])
        if ((s != none) & ((s < least) | (s > most))).any(): b.append("ws: a scale out of range")
        if (((d["wc"][r].reshape(16, 8, 512, 4) & 0x7F) != 0) & (s == none)[:, None, :, None]).any(): b.append("wc: a code other than zero under the scale of zeros")
    return b
def walk(p, o):
    a, at = np.arange(C), np.zeros((8, C), np.int64)
    for k in range(8):
        a = p[o[k], a]
        at[o[k], np.arange(C)] = a
    return at
def reference(x, u, v, pg, og, wc, ws):
    qu = [mx_ref.quantize(u[r]) for r in range(N)]
    lay = [pk(wc[r], ws[r]) for r in range(N)]
    p, o = [np.array(gentries(pg[r])) for r in range(N)], [np.array(gentries(og[r])) for r in range(N)]
    at = [walk(p[r], o[r]) for r in range(N)]
    now = [x[r] for r in range(N)]
    for t, step in enumerate(STEP):
        held, z = [], []
        for r in range(N):
            q = mx_ref.quantize(now[r])
            held.append(decode(q))
            s = mx_ref.matmul(qu[r], q)[::16]
            c = s[o[r], at[r][o[r], np.arange(C)]]
            for k in range(t % 2, 7, 2):
                turn = c[k] > c[k + 1]
                o[r][k], o[r][k + 1] = np.where(turn, o[r][k + 1], o[r][k]), np.where(turn, o[r][k], o[r][k + 1])
            at[r] = walk(p[r], o[r])
            z.append(mx_ref.quantize(gcols(held[r].astype(BF), at[r])))
        for r in range(N):
            e = np.take_along_axis(p[r], at[r], axis=1)
            now[r] = tile([held[r][:, b::4] + gpick(mx_ref.matmul(pick(lay[r], np.arange(128 * b, 128 * b + 128)), z[r ^ step]) * np.float32(0.03125), e) for b in range(4)])
    y, ol = np.zeros((N, 128, C), np.float32), np.zeros((N, 8, C), np.float32)
    oc, osc = np.zeros((N, 128, 4 * C), np.uint8), np.zeros((N, 16, C), np.uint8)
    for r in range(N):
        q = mx_ref.quantize(now[r])
        y[r] = mx_ref.matmul(mx_ref.quantize(v[r]), q)
        ol[r] = o[r]
        oc[r], osc[r] = emit(q)
    return {"y": y, "ol": ol, "oc": oc, "osc": osc}

@@ -1,0 +1,426 @@
+import math
+from concourse.mybir import dt, AluOpType, ActivationFunctionType
+
+STEP = (4, 1, 2)
+NB = 9
+BL = 9
+PARTS = ((0, 4), (4, 5))
+
+
+def blk(k):
+    return k // 2 if k % 2 == 0 else 5 + k // 2
+
+
+BF, F32, I32, U16, F16 = "bfloat16", "float32", "int32", "uint16", "float16"
+SCRATCH = {}
+for _d, _names in (
+        (BF, "diag 384 keepb 384 keepl 288 et 2048 lt 512 ut 512 vt 512 pt 2304 gm 2880 oh 162 fg 288 ft 288 gb 288 sb 288 xb 512 "
+             "f0 288 f1 288 f2 288 f3 288 d0 288 d1 288 d2 288 d3 288 x0 1152 x1 1152 x2 1152 x3 1152 z0 1152 z1 1152 z2 1152"),
+        (F32, "pf 8 keepf 384 jm 9 o 81 od 72 dd 36 mm 36 ab 162 dv 72 sov 72 sw 2304 ge 384 ee 384 ok 96 ot 96 yt 288 "
+              "r0 288 r1 288 r2 288 r3 288 cx 9 cd 9 cv 9"),
+        (I32, "pi 8 io 128 ioa 128 ip 384 ipa 384 ie 384 iea 768 ji 9 cli 72 uli 64 raw 2304 oi 144"),
+        (U16, "cl 72 ul 64 uo 90 uf 18 ub 18 so 24 al0 18 al1 18 al2 18 bl0 18 bl1 18 bl2 18 ll0 18 ll1 18 ll2 18 cu 10"),
+        (F16, "sc 2880 pm 144 pq 126")):
+    _w = _names.split()
+    for _n, _c in zip(_w[0::2], _w[1::2]):
+        SCRATCH[_n] = ("sbuf", [128, int(_c)], _d)
+for _n, _c in (("e", 512), ("l", 128), ("u", 128), ("r", 1024), ("v", 128), ("w", 512), ("b", 128)) + tuple(
+        (_m, 288) for _m in ("x0", "x1", "x2", "x3", "p0", "p1", "p2", "z0", "z1", "z2")):
+    SCRATCH["C" + _n], SCRATCH["S" + _n] = ("sbuf", [128, _c], "float8_e4m3fn_x4"), ("sbuf", [128, _c], "uint8")
+SCRATCH["old"] = ("dram", [72, 32], F32)
+for _b in range(8):
+    SCRATCH["ps%d" % _b] = ("psum", [128, 512], F32)
+SEMAPHORES = ["vq_", "sq_", "tq_", "gq_"] + ["dm%d" % i for i in range(20)] + [
+    n + str(t) for t in range(3) for n in ("ca", "cb", "sa", "sb", "la", "lb")]
+ORDER = []
+WAKE, NEAR = 100.0, 40.0
+
+
+def rank_program(g, core, T, topo):
+    rank = T.rank_of(core)
+    if rank is None:
+        return
+    A, AF = AluOpType, ActivationFunctionType
+    queue = {"v": g.vector, "s": g.scalar, "t": g.tensor, "g": g, "y": g.sync}
+    ops, recs = [], {}
+
+    def L(name, lo, n, st=1, p0=0, p1=128):
+        return (name, lo, lo + st * (n - 1) + 1, st, p0, p1)
+
+    def W(name):
+        return (name, 0, SCRATCH[name][1][1], 1, 0, 128)
+
+    def ap(v, idx=None):
+        name, lo, hi, st, p0, p1 = v
+        a = T[name][p0:p1, lo:hi] if st == 1 else T[name][p0:p1, lo:hi:st]
+        return a.indirect(ap(idx)) if idx else a
+
+    def u8(v):
+        return ap(v).bitcast(dt.uint8)
+
+    def clash(a, b):
+        if a[0].startswith("ps"):
+            return True
+        if a[1] >= b[2] or b[1] >= a[2] or a[4] >= b[5] or b[4] >= a[5]:
+            return False
+        return (a[1] - b[1]) % math.gcd(a[3], b[3]) == 0
+
+    def rec(q, call, reads, writes, dur, sem, inc=1, lat=0.0, group=None):
+        n, wait = len(ops), set()
+        for acc, w in [(r, False) for r in reads] + [(r, True) for r in writes]:
+            for m, w2, acc2 in recs.get(acc[0], []):
+                bank = acc[0].startswith("ps") and ops[m]["q"] != q
+                if m != n and not (group and ops[m]["group"] == group) and (w or w2 or bank) and clash(acc, acc2):
+                    wait.update(ops[m]["mates"])
+        for acc in writes:
+            recs[acc[0]] = [r for r in recs.get(acc[0], []) for b in [r[2]] if not (
+                acc[1] <= b[1] and b[2] <= acc[2] and acc[4] <= b[4] and b[5] <= acc[5]
+                and (acc[3] == 1 or (acc[3] == b[3] and (acc[1] - b[1]) % acc[3] == 0)))]
+        for acc, w in [(r, False) for r in reads] + [(r, True) for r in writes]:
+            recs.setdefault(acc[0], []).append((n, w, acc))
+        ops.append(dict(q=q, call=call, dur=dur, lat=lat, wait=wait, sem=sem, inc=inc, group=group, mates=[n]))
+        return n
+
+    def size(v):
+        return (v[2] - v[1] - 1) // v[3] + 1
+
+    def cost(q, out, ins, idx, two=False):
+        n = size(out)
+        if idx:
+            return 60 + 1.4 * size(idx) * 16
+        two_byte = all(SCRATCH[v[0]][2] in (BF, F16, U16) for v in [out] + ins)
+        return 0.9 * max(64, n * (2 if two and not ins[0][0].startswith("ps") else 0.5 if two_byte and q == "v" and not two else 1))
+
+    def do(q, call, reads, writes, dur):
+        rec(q, lambda: call().then_inc(T.sem[q + "q_"], 1), reads, writes, dur, q + "q_")
+
+    nd = [0]
+
+    def dmas(jobs, lat=2500.0):
+        sem = "dm%d" % nd[0]
+        nd[0] += 1
+        ids = [rec(e, lambda e=e, o=o, i=i: queue[e].dma_start(o, i).then_inc(T.sem[sem], 16), rd, wr, 60.0, sem, 16 * len(jobs), lat, sem)
+               for e, o, i, rd, wr in jobs]
+        for i in ids:
+            ops[i]["mates"] = ids
+
+    def send(dst, out, in_, arr, loc, code=False, lat=2500.0):
+        rid, pid = topo.addr(dst, core)
+        n = len(topo.engines(core, dst))
+        f = u8 if code else ap
+        s = rec("g", lambda: g.remote_dma(f(out), f(in_), T.sem[arr], T.sem[loc], pid, rid, topo.mask(core, dst)), [in_], [], 100.0, loc, n, lat)
+        r = rec(None, None, [], [out], 0.0, arr, n, lat)
+        ops[r]["wait"].add(s)
+
+    def more(*vs):
+        return [v for v in vs if isinstance(v, tuple)]
+
+    def tt(out, a, b, op, idx=None):
+        do("v", lambda: g.vector.tensor_tensor(ap(out), ap(a, idx), ap(b), op), [a, b] + more(idx), [out], cost("v", out, [a, b], idx, True))
+
+    def ts(out, a, s1, op0, s2=None, op1=None, idx=None):
+        c = [ap(s) if isinstance(s, tuple) else s for s in (s1, s2)]
+        o2 = (op0,) if op1 is None else (op0, op1)
+        do("v", lambda: g.vector.tensor_scalar(ap(out), ap(a, idx), c[0], c[1], *o2), [a] + more(s1, s2, idx), [out], cost("v", out, [a], idx))
+
+    def copy(out, a, idx=None):
+        do("v", lambda: g.vector.tensor_copy(ap(out), ap(a, idx)), [a] + more(idx), [out], cost("v", out, [a], idx))
+
+    def scan(out, d0, d1):
+        do("v", lambda: g.vector.tensor_tensor_scan(ap(out), ap(d0), ap(d1), 0.0, A.mult, A.add), [d0, d1], [out], cost("v", out, [d0, d1], None))
+
+    def turn(out, a):
+        do("v", lambda: g.vector.transpose(ap(out), ap(a)), [a], [out], cost("v", out, [a], None))
+
+    def act(out, a, func, idx=None, **kw):
+        k2 = {k: ap(v) if isinstance(v, tuple) else v for k, v in kw.items()}
+        do("s", lambda: g.scalar.activation(ap(out), ap(a, idx), func, **k2), [a] + more(idx, *kw.values()), [out], cost("s", out, [a], idx))
+
+    def quant(n, name, x):
+        q, s, v = L("C" + name, 0, n), L("S" + name, 0, n), L(x, 0, 4 * n)
+        do("v", lambda: g.vector.quantize_mx(ap(q), ap(s), ap(v)), [v], [q, s], 12 + n)
+
+    def mm(bank, n, w, w0, x, x0=0):
+        a, b, c, d = L("C" + w, w0, 128), L("S" + w, w0, 128), L("C" + x, x0, n), L("S" + x, x0, n)
+        o = L("ps%d" % bank, 0, n)
+        do("t", lambda: g.tensor.matmul_mx(ap(o), ap(a), ap(b), ap(c), ap(d), True, True), [a, b, c, d], [o], 0.6 * (n + 16))
+
+    def fill(v, k):
+        do("v", lambda: g.vector.memset(ap(v), k), [], [v], cost("v", v, [], None))
+
+    def iota(v, pattern, base, cm):
+        do("g", lambda: g.iota(ap(v), pattern, base, cm), [], [v], 130 + 2 * size(v))
+
+    q2 = ("y", "s")
+    H = 1152
+    for h in range(2):
+        dmas([(q2[r % 2], T.raw[r:r + 1, H * h:H * h + H], T.pg[64 * h:64 * h + 64, :], [], [L("raw", H * h, H, 1, r, r + 1)])
+              for r in range(16)], 2500.0 + 400 * h)
+    dmas([(q2[k % 2], T.oi[0:16, c:c + 18], T.og[16 * k:16 * k + 16, :], [], [L("oi", c, 18, 1, 0, 16)])
+          for k in range(8) for c in [18 * (k // 2 + 4 * (k % 2))]], 3300.0)
+    dmas([("y", T.x0[:, :], T.x[:, :], [], [W("x0")])], 4000.0)
+    dmas([("s", T.ut[:, :], T.u[:, :], [], [W("ut")])], 4000.0)
+    for name, lo, n, lat in (("raw", 0, H, 8000.0), ("raw", H, H, 10000.0), ("oi", 0, 144, 5000.0)):
+        dmas([(q2[h % 2], T[name][16 * h:16 * h + 16, lo:lo + n], T[name][0:16, lo:lo + n], [L(name, lo, n, 1, 0, 16)],
+               [L(name, lo, n, 1, 16 * h, 16 * h + 16)]) for h in range(1, 8)], lat)
+    dmas([("y", u8(W("Cw")), T.wc[:, :], [], [W("Cw")]), ("y", T.Sw[:, :], T.ws[:, :], [], [W("Sw")]),
+          ("y", T.vt[:, :], T.v[:, :], [], [W("vt")])], 9000.0)
+
+    iota(L("pi", 0, 1), [[0, 1]], 0, 1)
+    iota(W("uli"), [[16, 8], [0, 8]], 0, 0)
+    iota(W("io"), [[-1, 128]], 128, 1)
+    iota(W("ip"), [[-1, 384]], 384, 1)
+    iota(W("ie"), [[1, 384]], 0, 0)
+    iota(W("ji"), [[32, NB]], -144, 0)
+    iota(W("cli"), [[288, 4], [1, 18]], 0, 0)
+    copy(W("ul"), W("uli"))
+    fill(W("et"), 0.0)
+    fill(W("lt"), 0.0)
+    for b in range(4):
+        ts(L("et", 512 * b + b, 128, 4), W("io"), 128, A.is_equal)
+    ts(W("ioa"), W("io"), 31, A.bitwise_and)
+    ts(L("lt", 0, 128, 4), W("ioa"), 0, A.is_equal)
+    quant(512, "e", "et")
+    quant(128, "l", "lt")
+    ts(W("ipa"), W("ip"), 15, A.bitwise_and)
+    ts(W("diag"), W("ipa"), 0, A.is_equal)
+    ts(L("iea", 0, 384), W("ie"), 15, A.bitwise_and)
+    ts(L("iea", 384, 384), W("ie"), 31, A.bitwise_and)
+    ts(W("keepf"), L("iea", 0, 384), 0, A.is_gt)
+    ts(W("keepb"), L("iea", 0, 384), 0, A.is_gt)
+    ts(W("keepl"), L("iea", 384, 288), 0, A.is_gt)
+    P = lambda j: L("pi", j, 1)
+    Q = lambda j: L("pf", j, 1)
+    ts(P(1), P(0), 15, A.bitwise_and)
+    ts(P(2), P(0), 31, A.bitwise_and)
+    ts(P(3), P(0), 4, A.arith_shift_right)
+    ts(P(4), P(0), 5, A.arith_shift_right)
+    ts(P(5), P(3), 1, A.bitwise_and)
+    ts(Q(1), P(1), 18, A.mult)
+    ts(Q(2), P(2), 0, A.add)
+    ts(Q(3), P(3), 288, A.mult, 144, A.add)
+    ts(Q(4), P(4), -2, A.mult)
+    ts(Q(5), P(4), -2, A.mult, -1, A.add)
+    ts(Q(6), P(5), 0, A.add)
+    ts(W("jm"), W("ji"), Q(2), A.add)
+    ts(W("cl"), W("cli"), Q(1), A.add)
+    fill(W("gm"), 0.0)
+    fill(W("xb"), 0.0)
+    fill(L("ok", 72, 24), 0.0)
+    fill(L("o", 36, 9), 8.0)
+    quant(128, "u", "ut")
+    do("v", lambda: g.vector.tensor_copy(ap(W("Cr")).bitcast(dt.uint32), ap(W("Cu")).bitcast(dt.uint32).indirect(ap(W("ul")))),
+       [W("Cu"), W("ul")], [W("Cr")], 1500.0)
+    act(W("Sr"), W("Su"), AF.Copy, idx=W("ul"))
+
+    EV, OD = 0, 45
+    base = lambda b0, n: L("gm", 288 * b0 + 1, NB * n, 32)
+    last = lambda b0, n, b1=0: L("sc", 288 * b0 + 32 * b1 + 31, n, 32)
+
+    def look(s, name, lo):
+        for b, n in PARTS:
+            c = 288 * s + 32 * b
+            tt(L("gm", c, 16 * n, 2), W("pt"), L("diag", 0, 16 * n), A.mult, idx=L(name, lo + b, n))
+            scan(L("sc", c, 32 * n), L("keepl", 0, 32 * n), L("gm", c, 32 * n))
+
+    def lists(k):
+        for b, n in PARTS:
+            ts(L("uo", 10 * k + b, n), last(blk(k), n, b), 1296, A.add)
+
+    def walk(k0):
+        for k in range(k0 + 1, 8):
+            look(blk(k), "uo", 10 * (k - 1))
+            lists(k)
+
+    def score_lists(t):
+        look(4, "uo", 70)
+        tt(W("dv"), last(1, 72), base(1, 8), A.subtract)
+        tt(L("sov", 0, 36), L("dv", 36, 36), base(0, 4), A.add)
+        tt(L("sov", 36, 36), L("dv", 0, 36), base(5, 4), A.add)
+        for a, (p0, p1) in enumerate(((0, 32), (32, 64), (64, 128))):
+            ts(L("so", 0, 24, 1, p0, p1), L("sov", a, 24, 3, p0, p1), 1296, A.add)
+        if t % 2 == 0:
+            tt(L("dd", 0, 36), L("o", OD, 36), L("o", EV, 36), A.subtract)
+            tt(W("cv"), base(5, 1), W("jm"), A.add)
+        else:
+            tt(L("dd", 0, 27), L("o", EV + 9, 27), L("o", OD, 27), A.subtract)
+            tt(W("cv"), base(1, 1), L("dv", 36, 9), A.add)
+        ts(L("cu", 0, 9), W("cv"), 1296, A.add)
+        ts(base(9, 1), L("o", EV if t % 2 == 0 else OD, 9), 288, A.mult, -1152, A.add)
+        look(9, "cu", 0)
+        tt(W("cd"), last(9, 9), last(blk(1 + t % 2), 9), A.subtract)
+
+    def products(t):
+        x = "x%d" % t
+        quant(288, x, x)
+        if t == 3:
+            return
+        dst = T.cores[rank ^ STEP[t]]
+        send(dst, W("Cp%d" % t), W("C" + x), "ca%d" % t, "cb%d" % t, True, 6000.0)
+        send(dst, W("Sp%d" % t), W("S" + x), "sa%d" % t, "sb%d" % t, False, 6000.0)
+        for i in range(8):
+            mm(i, 288, "r", 128 * i, x)
+            if i % 2 == 0:
+                copy(L("sw", 288 * i, 288), L("ps%d" % i, 0, 288))
+            else:
+                act(L("sw", 288 * i, 288), L("ps%d" % i, 0, 288), AF.Copy)
+        for b in range(4):
+            mm(b, 288, "e", 128 * b, x)
+            act(W("f%d" % b), L("ps%d" % b, 0, 288), AF.Copy)
+
+    products(0)
+    tt(W("od"), L("oi", 1, 72, 2), L("oi", 0, 72, 2), A.subtract)
+    ts(W("od"), W("od"), Q(6), A.mult)
+    tt(L("o", EV, 36), L("od", 0, 36), L("oi", 0, 36, 2), A.add)
+    tt(L("o", OD, 36), L("od", 36, 36), L("oi", 72, 36, 2), A.add)
+    ts(base(0, BL), W("o"), 288, A.mult, -1152, A.add)
+    for h in range(2):
+        ts(L("pt", H * h, H), L("raw", H * h, H), -144, A.add, idx=W("cl"))
+    tt(last(0, 9), base(0, 1), W("jm"), A.add)
+    lists(0)
+    walk(0)
+    score_lists(0)
+    quant(128, "v", "vt")
+
+    for t in range(3):
+        dst = T.cores[rank ^ STEP[t]]
+        for h in (0, 192):
+            tt(L("ge", h, 192), W("sw"), L("diag", 0, 192), A.mult, idx=L("so", h // 16, 12))
+            scan(L("ee", h, 192), L("keepf", 0, 192), L("ge", h, 192))
+        n = 12 if t % 2 == 0 else 9
+        for a in range(3):
+            p = (32 * a, 32 * a + 32)
+            ev, od = L("ee", 15 if n == 12 else 63, n, 16, *p), L("ee", 207, n, 16, *p)
+            tt(L("xb", 4 * a, n, 12, *p), *((ev, od) if n == 12 else (od, ev)), A.is_gt)
+        quant(128, "b", "xb")
+        mm(7, 128, "l", 0, "b")
+        k1 = 1 + t % 2
+        tt(W("cx"), L("ps7", 0, 9), W("cd"), A.mult)
+        tt(last(blk(k1), 9), last(blk(k1), 9), W("cx"), A.add)
+        lists(k1)
+        m = 3 * n
+        lo, hi = (L("o", EV, 36), L("o", OD, 36)) if n == 12 else (L("o", OD, 27), L("o", EV + 9, 27))
+        tt(L("mm", 0, m), L("ps7", 0, m), L("dd", 0, m), A.mult)
+        tt(lo, lo, L("mm", 0, m), A.add)
+        tt(hi, hi, L("mm", 0, m), A.subtract)
+        ts(base(0, 4), L("o", EV, 36), 288, A.mult, -1152, A.add)
+        ts(base(5, 4), L("o", OD, 36), 288, A.mult, -1152, A.add)
+        if n == 12:
+            tt(last(0, 9), base(0, 1), W("jm"), A.add)
+        else:
+            tt(last(5, 9), base(5, 1), L("dv", 36, 9), A.add)
+        for e in range(2):
+            act(L("ab", 81 * e, 81), W("o"), AF.Abs, bias=Q(4 + e))
+        for e in range(2):
+            act(L("oh", 81 * e, 81), L("ab", 81 * e, 81), AF.Relu, bias=1.0, scale=-1.0)
+        walk(k1)
+        for to, b0, nb in ((0, 0, 3), (54, 5, 3), (108, 3, 1), (126, 8, 1)):
+            for e in range(2):
+                tt(L("pm", to + e, NB * nb, 2), last(b0, NB * nb), L("oh", 81 * e + 9 * b0, NB * nb), A.mult)
+        tt(L("pq", 0, 54), L("pm", 0, 54), L("pm", 54, 54), A.add)
+        tt(L("pq", 54, 18), L("pq", 0, 18), L("pq", 18, 18), A.add)
+        tt(L("pq", 72, 18), L("pq", 54, 18), L("pq", 36, 18), A.add)
+        tt(L("pq", 90, 18), L("pq", 72, 18), L("pm", 108, 18), A.add)
+        tt(L("pq", 108, 18), L("pq", 90, 18), L("pm", 126, 18), A.add)
+        ts(W("uf"), L("pq", 108, 18), 1296, A.add)
+        al, bl, ll = "al%d" % t, W("bl%d" % t), W("ll%d" % t)
+        for b, n in PARTS:
+            c = L("fg", 32 * b, 32 * n), L("ft", 32 * b, 32 * n)
+            copy(c[0], W("pt"), idx=L("uf", 2 * b, 2 * n))
+            turn(c[1], c[0])
+            ts(L(al, 2 * b, 2 * n), L("ft", 32 * b, 2 * n, 16), 144, A.add)
+        send(dst, ll, W(al), "la%d" % t, "lb%d" % t)
+        ts(W("ub"), L("ft", 0, 18, 16), Q(3), A.add)
+        tt(W("gb"), W("pt"), L("diag", 0, 288), A.mult, idx=W("ub"))
+        scan(W("sb"), L("keepb", 0, 288), W("gb"))
+        ts(bl, L("sb", 15, 18, 16), 144, A.add)
+        for b in range(4):
+            bank = 4 + b if b < 3 else 0
+            mm(bank, 288, "e", 128 * b, "p%d" % t)
+            act(W("d%d" % b), L("ps%d" % bank, 0, 288), AF.Copy)
+        if t < 2:
+            score_lists(t + 1)
+        else:
+            for k in range(8):
+                act(L("ok", 9 * k, 9), L("o", 9 * blk(k), 9), AF.Copy)
+            turn(W("ot"), W("ok"))
+            dmas([("y", T.old[32 * i:32 * i + r, :], T.ot[0:r, 32 * i:32 * i + 32], [L("ot", 32 * i, 32, 1, 0, r)],
+                   [L("old", 0, 32, 1, 32 * i, 32 * i + r)]) for i, r in ((0, 32), (1, 32), (2, 8))])
+            dmas([("y", T.ol[:, :], T.old[:, :], [L("old", 0, 32, 1, 0, 72)], [])])
+        z = "z%d" % t
+        for b in (0, 2, 1, 3):
+            if b < 2:
+                copy(L(z, b, 288, 4), W("d%d" % b), idx=ll)
+            else:
+                act(L(z, b, 288, 4), W("d%d" % b), AF.Copy, idx=ll)
+        quant(288, z, z)
+        for b in range(4):
+            mm(1 + b, 288, "w", 128 * b, z)
+            act(W("r%d" % b), L("ps%d" % (1 + b), 0, 288), AF.Identity, scale=0.03125)
+        for b in range(4):
+            tt(L("x%d" % (t + 1), b, 288, 4), W("r%d" % b), W("f%d" % b), A.add, idx=bl)
+        products(t + 1)
+
+    for h in range(2):
+        mm(5 + h, 144, "v", 0, "x3", 144 * h)
+    copy(L("yt", 0, 144), L("ps5", 0, 144))
+    act(L("yt", 144, 144), L("ps6", 0, 144), AF.Copy)
+    dmas([("y", T.y[:, :], T.yt[:, :], [W("yt")], [])])
+    dmas([("y", T.oc[:, :], u8(W("Cx3")), [W("Cx3")], [])]
+         + [("s", T.osc[4 * k:4 * k + 4, :], T.Sx3[32 * k:32 * k + 4, 0:288], [W("Sx3")], []) for k in range(4)])
+
+    if not ORDER:
+        N = len(ops)
+        nxt, left, prio = [[] for _ in ops], [len(o["wait"]) for o in ops], [0.0] * N
+        for i, o in enumerate(ops):
+            for m in o["wait"]:
+                nxt[m].append(i)
+        span = lambda o: (o["lat"] if o["q"] else 0.0) or o["dur"]
+        for i in reversed(range(N)):
+            prio[i] = span(ops[i]) + max([0.0] + [WAKE + prio[k] for k in nxt[i]])
+        ready, free, done = {i: 0.0 for i in range(N) if not left[i]}, {q: 0.0 for q in list(queue) + [None]}, [0.0] * N
+        while ready:
+            begin = {i: max(r, free[ops[i]["q"]]) for i, r in ready.items()}
+            first = min(begin, key=lambda i: (begin[i], -prio[i]))
+            i = max((k for k in begin if ops[k]["q"] == ops[first]["q"] and begin[k] <= begin[first] + NEAR), key=lambda k: (prio[k], -k))
+            o = ops[i]
+            at = ready.pop(i)
+            if o["q"]:
+                free[o["q"]] = begin[i] + o["dur"]
+                done[i] = begin[i] + span(o)
+            else:
+                done[i] = at
+            ORDER.append(i)
+            for k in nxt[i]:
+                left[k] -= 1
+                if not left[k]:
+                    ready[k] = WAKE + max(done[m] for m in ops[k]["wait"])
+
+    known, total, waited, snap, token = {q: {} for q in queue}, {}, {}, {}, {}
+    for i in ORDER:
+        o = ops[i]
+        q, sem = o["q"], o["sem"]
+        if q is None:
+            total[sem], token[i] = o["inc"], (sem, o["inc"])
+            continue
+        want = {}
+        for m in o["wait"]:
+            s, v = token[m]
+            want[s] = max(want.get(s, 0), v)
+        for s, v in sorted(want.items(), key=lambda kv: -kv[1]):
+            if known[q].get(s, 0) >= v:
+                continue
+            queue[q].wait_ge(T.sem[s], v)
+            waited[s] = max(waited.get(s, 0), v)
+            known[q][s] = v
+            for s2, v2 in snap.get((s, v), {}).items():
+                known[q][s2] = max(known[q].get(s2, 0), v2)
+        o["call"]()
+        total[sem] = total.get(sem, 0) + 1 if not o["lat"] else o["inc"]
+        token[i] = (sem, total[sem])
+        seen = snap.setdefault(token[i], {})
+        for s2, v2 in known[q].items():
+            seen[s2] = max(seen.get(s2, 0), v2)
+    for sem in sorted(total):
+        if waited.get(sem, 0) < total[sem]:
+            g.sync.wait_ge(T.sem[sem], total[sem])

@@ -2,38 +2,40 @@ import math
 from concourse.mybir import dt, AluOpType, ActivationFunctionType
 
 STEP = (4, 1, 2)
-NB = 9
-BL = 9
-PARTS = ((0, 4), (4, 5))
-
-
-def blk(k):
-    return k // 2 if k % 2 == 0 else 5 + k // 2
-
+HALF = ((0, 160), (160, 128))
+UP, LOW, OUT = 1024, -768, -4096
+SHIFT = 1600
 
 BF, F32, I32, U16, F16 = "bfloat16", "float32", "int32", "uint16", "float16"
-SCRATCH = {}
+SCRATCH, PLACE = {}, {}
 for _d, _names in (
-        (BF, "diag 384 keepb 384 keepl 288 et 2048 lt 512 ut 512 vt 512 pt 2304 gm 2880 oh 162 fg 288 ft 288 gb 288 sb 288 xb 512 "
-             "f0 288 f1 288 f2 288 f3 288 d0 288 d1 288 d2 288 d3 288 x0 1152 x1 1152 x2 1152 x3 1152 z0 1152 z1 1152 z2 1152"),
-        (F32, "pf 8 keepf 384 jm 9 o 81 od 72 dd 36 mm 36 ab 162 dv 72 sov 72 sw 2304 ge 384 ee 384 ok 96 ot 96 yt 288 "
-              "r0 288 r1 288 r2 288 r3 288 cx 9 cd 9 cv 9"),
-        (I32, "pi 8 io 128 ioa 128 ip 384 ipa 384 ie 384 iea 768 ji 9 cli 72 uli 64 raw 2304 oi 144"),
-        (U16, "cl 72 ul 64 uo 90 uf 18 ub 18 so 24 al0 18 al1 18 al2 18 bl0 18 bl1 18 bl2 18 ll0 18 ll1 18 ll2 18 cu 10"),
-        (F16, "sc 2880 pm 144 pq 126")):
+        (BF, "one 520 et 520 lt 512 ut 512 vt 512 wx 320 tab 3168 tw 608 idm 320 dtab 80 pall 288 ra 640 rb 320 da 640 db 320 dg 288 "
+             "g0 320 t0 320 g1 160 t1 160 g2 160 t2 160 g3 160 t3 160 gf 288 tf 288 gl 320 tl 320 gb 288 rr 160 rt 176 fh 160 e1 160 "
+             "e2 160 xb 512 oh 160 bt 88 st 80 pr 320 ss 320 keep8 320 dq 48 cq 160 ct 80 cs 160 f0 288 f1 288 f2 288 d0 288 d1 288 "
+             "d2 288 d3 288 x0 1152 x1 1152 x2 1152 x3 1152 z0 1152 z1 1152 z2 1152"),
+        (F32, "pf 48 bias 10 o 168 o288 168 dd 80 mm 80 cp 80 ak 240 j0 10 j1 10 ix 320 bw 20 co 30 s3 30 k3 30 s3o 30 sg 32 sa 32 "
+              "sw 2304 eb 160 ot 96 yt 288 r0 288 r1 288 r2 288 r3 288 r4 288 ab 30 nf 30 ki 14 oi 10 ji 20 bi 16 wli 20 two 20"),
+        (I32, "pi 10 io 128 raw 288 pgn 18 ni 30"),
+        (U16, "wl 20 pl 144 pll 10 ol_ 10 ul 10 pgu 18 kl 14 ar 20 fl 2 il 18 uc 60 ub 20 u1 10 u2 10 u3 10 uf 18 ut_ 32 so 32 "
+              "al0 32 al1 32 al2 32 bl0 18 bl1 18 bl2 18 ll0 18 ll1 18 ll2 18"),
+        (F16, "c0 320 c1 160 c2 160 c3 160 cf 320 cb 288")):
     _w = _names.split()
     for _n, _c in zip(_w[0::2], _w[1::2]):
-        SCRATCH[_n] = ("sbuf", [128, int(_c)], _d)
-for _n, _c in (("e", 512), ("l", 128), ("u", 128), ("r", 1024), ("v", 128), ("w", 512), ("b", 128)) + tuple(
+        if _d != BF and _n[:2] not in ("ra", "pg", "ll", "al", "sw", "eb", "ot", "yt", "r0", "r1", "r2", "r3", "r4"):
+            _at = SCRATCH.get("all" + _d, ("", [0, 0]))[1][1]
+            SCRATCH["all" + _d] = ("sbuf", [128, _at + (int(_c) + 15) // 16 * 16], _d)
+            PLACE[_n] = ("all" + _d, _at, int(_c))
+        else:
+            SCRATCH[_n] = ("sbuf", [128, int(_c)], _d)
+for _n, _c in (("e", 512), ("l", 128), ("u", 128), ("r", 144), ("v", 128), ("w", 512), ("b", 128)) + tuple(
         (_m, 288) for _m in ("x0", "x1", "x2", "x3", "p0", "p1", "p2", "z0", "z1", "z2")):
     SCRATCH["C" + _n], SCRATCH["S" + _n] = ("sbuf", [128, _c], "float8_e4m3fn_x4"), ("sbuf", [128, _c], "uint8")
-SCRATCH["old"] = ("dram", [72, 32], F32)
-for _b in range(8):
-    SCRATCH["ps%d" % _b] = ("psum", [128, 512], F32)
+SCRATCH["ps"] = ("psum", [128, 4096], F32)
 SEMAPHORES = ["vq_", "sq_", "tq_", "gq_"] + ["dm%d" % i for i in range(20)] + [
     n + str(t) for t in range(3) for n in ("ca", "cb", "sa", "sb", "la", "lb")]
 ORDER = []
-WAKE, NEAR = 100.0, 40.0
+INFO = {}
+WAKE = 100.0
 
 
 def rank_program(g, core, T, topo):
@@ -45,10 +47,14 @@ def rank_program(g, core, T, topo):
     ops, recs = [], {}
 
     def L(name, lo, n, st=1, p0=0, p1=128):
-        return (name, lo, lo + st * (n - 1) + 1, st, p0, p1)
+        name, at = PLACE.get(name, (name, 0))[:2]
+        return (name, at + lo, at + lo + st * (n - 1) + 1, st, p0, p1)
 
     def W(name):
-        return (name, 0, SCRATCH[name][1][1], 1, 0, 128)
+        return L(name, 0, PLACE[name][2] if name in PLACE else SCRATCH[name][1][1])
+
+    def PS(bank, lo, n, st=1):
+        return L("ps", 512 * bank + lo, n, st)
 
     def ap(v, idx=None):
         name, lo, hi, st, p0, p1 = v
@@ -59,8 +65,8 @@ def rank_program(g, core, T, topo):
         return ap(v).bitcast(dt.uint8)
 
     def clash(a, b):
-        if a[0].startswith("ps"):
-            return True
+        if a[0] == "ps":
+            return a[1] // 512 == b[1] // 512
         if a[1] >= b[2] or b[1] >= a[2] or a[4] >= b[5] or b[4] >= a[5]:
             return False
         return (a[1] - b[1]) % math.gcd(a[3], b[3]) == 0
@@ -69,17 +75,25 @@ def rank_program(g, core, T, topo):
         n, wait = len(ops), set()
         for acc, w in [(r, False) for r in reads] + [(r, True) for r in writes]:
             for m, w2, acc2 in recs.get(acc[0], []):
-                bank = acc[0].startswith("ps") and ops[m]["q"] != q
+                bank = acc[0] == "ps" and (ops[m]["q"] != q or q == "f")
                 if m != n and not (group and ops[m]["group"] == group) and (w or w2 or bank) and clash(acc, acc2):
                     wait.update(ops[m]["mates"])
         for acc in writes:
             recs[acc[0]] = [r for r in recs.get(acc[0], []) for b in [r[2]] if not (
+                clash(acc, b) if acc[0] == "ps" else
                 acc[1] <= b[1] and b[2] <= acc[2] and acc[4] <= b[4] and b[5] <= acc[5]
-                and (acc[3] == 1 or (acc[3] == b[3] and (acc[1] - b[1]) % acc[3] == 0)))]
+                and (acc[3] == 1 or (b[3] % acc[3] == 0 and (acc[1] - b[1]) % acc[3] == 0)))]
         for acc, w in [(r, False) for r in reads] + [(r, True) for r in writes]:
             recs.setdefault(acc[0], []).append((n, w, acc))
-        ops.append(dict(q=q, call=call, dur=dur, lat=lat, wait=wait, sem=sem, inc=inc, group=group, mates=[n]))
+        ops.append(dict(q=q, call=call, dur=dur, lat=lat, wait=wait, sem=sem, inc=inc, group=group, mates=[n],
+                        what=named((writes or reads)[0])))
         return n
+
+    def named(v):
+        for k, (b, at, n) in PLACE.items():
+            if b == v[0] and at <= v[1] < at + n:
+                return k, v[1] - at
+        return v[:2]
 
     def size(v):
         return (v[2] - v[1] - 1) // v[3] + 1
@@ -87,16 +101,17 @@ def rank_program(g, core, T, topo):
     def cost(q, out, ins, idx, two=False):
         n = size(out)
         if idx:
-            return 60 + 1.4 * size(idx) * 16
+            return (50 if q == "v" else 65) + 1.6 * size(idx) * 16
         two_byte = all(SCRATCH[v[0]][2] in (BF, F16, U16) for v in [out] + ins)
-        return 0.9 * max(64, n * (2 if two and not ins[0][0].startswith("ps") else 0.5 if two_byte and q == "v" and not two else 1))
+        psum = any(v[0] == "ps" for v in ins)
+        return 1.04 * max(64, n * (2 if two and not psum else 0.5 if two_byte and q == "v" and not two else 1))
 
     def do(q, call, reads, writes, dur):
         rec(q, lambda: call().then_inc(T.sem[q + "q_"], 1), reads, writes, dur, q + "q_")
 
     nd = [0]
 
-    def dmas(jobs, lat=2500.0):
+    def dmas(jobs, lat=2200.0):
         sem = "dm%d" % nd[0]
         nd[0] += 1
         ids = [rec(e, lambda e=e, o=o, i=i: queue[e].dma_start(o, i).then_inc(T.sem[sem], 16), rd, wr, 60.0, sem, 16 * len(jobs), lat, sem)
@@ -104,7 +119,7 @@ def rank_program(g, core, T, topo):
         for i in ids:
             ops[i]["mates"] = ids
 
-    def send(dst, out, in_, arr, loc, code=False, lat=2500.0):
+    def send(dst, out, in_, arr, loc, code=False, lat=2200.0):
         rid, pid = topo.addr(dst, core)
         n = len(topo.engines(core, dst))
         f = u8 if code else ap
@@ -124,282 +139,488 @@ def rank_program(g, core, T, topo):
         do("v", lambda: g.vector.tensor_scalar(ap(out), ap(a, idx), c[0], c[1], *o2), [a] + more(s1, s2, idx), [out], cost("v", out, [a], idx))
 
     def copy(out, a, idx=None):
+        if all(SCRATCH[v[0]][2] in (BF, F32) for v in (out, a)):
+            return aff(out, a, idx=idx)
         do("v", lambda: g.vector.tensor_copy(ap(out), ap(a, idx)), [a] + more(idx), [out], cost("v", out, [a], idx))
 
-    def scan(out, d0, d1):
-        do("v", lambda: g.vector.tensor_tensor_scan(ap(out), ap(d0), ap(d1), 0.0, A.mult, A.add), [d0, d1], [out], cost("v", out, [d0, d1], None))
+    def scan(out, d0, d1, op0=A.add, op1=A.max):
+        do("v", lambda: g.vector.tensor_tensor_scan(ap(out), ap(d0), ap(d1), 0.0, op0, op1), [d0, d1], [out], cost("v", out, [d0, d1], None))
+
+    def sums(out, keep, d1):
+        scan(out, keep, d1, A.mult, A.add)
 
     def turn(out, a):
         do("v", lambda: g.vector.transpose(ap(out), ap(a)), [a], [out], cost("v", out, [a], None))
 
-    def act(out, a, func, idx=None, **kw):
+    def act(out, a, func=None, idx=None, **kw):
+        if func is None and out[0] != "Sr":
+            return aff(out, a, idx=idx)
+        func = func or AF.Copy
         k2 = {k: ap(v) if isinstance(v, tuple) else v for k, v in kw.items()}
         do("s", lambda: g.scalar.activation(ap(out), ap(a, idx), func, **k2), [a] + more(idx, *kw.values()), [out], cost("s", out, [a], idx))
 
-    def quant(n, name, x):
-        q, s, v = L("C" + name, 0, n), L("S" + name, 0, n), L(x, 0, 4 * n)
-        do("v", lambda: g.vector.quantize_mx(ap(q), ap(s), ap(v)), [v], [q, s], 12 + n)
+    def aff(out, a, scale=1, bias=0, idx=None):
+        k, c = [ap(s) if isinstance(s, tuple) else float(s) for s in (scale, bias)]
+        plain = scale == 1 and bias == 0
+        calls = {"v": lambda: g.vector.tensor_copy(ap(out), ap(a, idx)) if plain else g.vector.tensor_scalar(ap(out), ap(a, idx), k, c, A.mult, A.add),
+                 "s": lambda: g.scalar.activation(ap(out), ap(a, idx), AF.Copy) if plain else
+                 g.scalar.activation(ap(out), ap(a, idx), AF.Identity, bias=c, scale=k)}
+        rec("f", calls, [a] + more(scale, bias, idx), [out], {q: cost(q, out, [a], idx) for q in "vs"}, None)
+
+    def sfill(v, k):
+        aff(v, L("one", 0, size(v)), k, 0)
+
+    def quant(name, c0, n, x, x0=None):
+        q, s, v = L("C" + name, c0, n), L("S" + name, c0, n), L(x, 4 * c0 if x0 is None else x0, 4 * n)
+        do("v", lambda: g.vector.quantize_mx(ap(q), ap(s), ap(v)), [v], [q, s], 15 + 1.1 * n)
 
     def mm(bank, n, w, w0, x, x0=0):
         a, b, c, d = L("C" + w, w0, 128), L("S" + w, w0, 128), L("C" + x, x0, n), L("S" + x, x0, n)
-        o = L("ps%d" % bank, 0, n)
-        do("t", lambda: g.tensor.matmul_mx(ap(o), ap(a), ap(b), ap(c), ap(d), True, True), [a, b, c, d], [o], 0.6 * (n + 16))
+        o = PS(bank, 0, n)
+        do("t", lambda: g.tensor.matmul_mx(ap(o), ap(a), ap(b), ap(c), ap(d), True, True), [a, b, c, d], [o], 0.7 * (n + 16))
 
     def fill(v, k):
         do("v", lambda: g.vector.memset(ap(v), k), [], [v], cost("v", v, [], None))
 
-    def iota(v, pattern, base, cm):
-        do("g", lambda: g.iota(ap(v), pattern, base, cm), [], [v], 130 + 2 * size(v))
+    def iota(v, pattern, base, cm=0):
+        small = SCRATCH[v[0]][2] != I32
+        do("g", lambda: g.iota(ap(v), pattern, base, cm, allow_small_or_imprecise_dtypes=True) if small else g.iota(ap(v), pattern, base, cm),
+           [], [v], 160 + 2.1 * size(v))
 
-    q2 = ("y", "s")
-    H = 1152
-    for h in range(2):
-        dmas([(q2[r % 2], T.raw[r:r + 1, H * h:H * h + H], T.pg[64 * h:64 * h + 64, :], [], [L("raw", H * h, H, 1, r, r + 1)])
-              for r in range(16)], 2500.0 + 400 * h)
-    dmas([(q2[k % 2], T.oi[0:16, c:c + 18], T.og[16 * k:16 * k + 16, :], [], [L("oi", c, 18, 1, 0, 16)])
-          for k in range(8) for c in [18 * (k // 2 + 4 * (k % 2))]], 3300.0)
-    dmas([("y", T.x0[:, :], T.x[:, :], [], [W("x0")])], 4000.0)
-    dmas([("s", T.ut[:, :], T.u[:, :], [], [W("ut")])], 4000.0)
-    for name, lo, n, lat in (("raw", 0, H, 8000.0), ("raw", H, H, 10000.0), ("oi", 0, 144, 5000.0)):
-        dmas([(q2[h % 2], T[name][16 * h:16 * h + 16, lo:lo + n], T[name][0:16, lo:lo + n], [L(name, lo, n, 1, 0, 16)],
-               [L(name, lo, n, 1, 16 * h, 16 * h + 16)]) for h in range(1, 8)], lat)
+    def pick(out, win, idx, nv):
+        n = size(idx)
+        if nv:
+            copy(L(out[0], out[1], 16 * nv), win, idx=L(idx[0], idx[1], nv))
+        if n > nv:
+            act(L(out[0], out[1] + 16 * nv, 16 * (n - nv)), win, idx=L(idx[0], idx[1] + nv, n - nv))
+
+    fill(W("raw"), 0)
+    dmas([("y", T.x0[:, :], T.x[:, :], [], [W("x0")])], 3000.0)
+    dmas([("s", T.ut[:, :], T.u[:, :], [], [W("ut")])], 3000.0)
+    dmas([(("y", "s")[h % 2], T.raw[16 * h + 1:16 * h + 9, :], T.pg[:, :], [], [L("raw", 0, 288, 1, 16 * h + 1, 16 * h + 9)]) for h in range(8)]
+         + [(("s", "y")[h % 2], T.raw[16 * h + 9:16 * h + 13, :], T.og[64 * (h % 2):64 * (h % 2) + 64, :], [],
+             [L("raw", 0, 288, 1, 16 * h + 9, 16 * h + 13)]) for h in range(8)])
+    dmas([("y", T.pgn[:, :], T.pg[:, :], [], [W("pgn")])])
     dmas([("y", u8(W("Cw")), T.wc[:, :], [], [W("Cw")]), ("y", T.Sw[:, :], T.ws[:, :], [], [W("Sw")]),
-          ("y", T.vt[:, :], T.v[:, :], [], [W("vt")])], 9000.0)
+          ("y", T.vt[:, :], T.v[:, :], [], [W("vt")])], 5000.0)
 
-    iota(L("pi", 0, 1), [[0, 1]], 0, 1)
-    iota(W("uli"), [[16, 8], [0, 8]], 0, 0)
-    iota(W("io"), [[-1, 128]], 128, 1)
-    iota(W("ip"), [[-1, 384]], 384, 1)
-    iota(W("ie"), [[1, 384]], 0, 0)
-    iota(W("ji"), [[32, NB]], -144, 0)
-    iota(W("cli"), [[288, 4], [1, 18]], 0, 0)
-    copy(W("ul"), W("uli"))
-    fill(W("et"), 0.0)
-    fill(W("lt"), 0.0)
-    for b in range(4):
-        ts(L("et", 512 * b + b, 128, 4), W("io"), 128, A.is_equal)
-    ts(W("ioa"), W("io"), 31, A.bitwise_and)
-    ts(L("lt", 0, 128, 4), W("ioa"), 0, A.is_equal)
-    quant(512, "e", "et")
-    quant(128, "l", "lt")
-    ts(W("ipa"), W("ip"), 15, A.bitwise_and)
-    ts(W("diag"), W("ipa"), 0, A.is_equal)
-    ts(L("iea", 0, 384), W("ie"), 15, A.bitwise_and)
-    ts(L("iea", 384, 384), W("ie"), 31, A.bitwise_and)
-    ts(W("keepf"), L("iea", 0, 384), 0, A.is_gt)
-    ts(W("keepb"), L("iea", 0, 384), 0, A.is_gt)
-    ts(W("keepl"), L("iea", 384, 288), 0, A.is_gt)
     P = lambda j: L("pi", j, 1)
     Q = lambda j: L("pf", j, 1)
-    ts(P(1), P(0), 15, A.bitwise_and)
-    ts(P(2), P(0), 31, A.bitwise_and)
-    ts(P(3), P(0), 4, A.arith_shift_right)
-    ts(P(4), P(0), 5, A.arith_shift_right)
-    ts(P(5), P(3), 1, A.bitwise_and)
-    ts(Q(1), P(1), 18, A.mult)
-    ts(Q(2), P(2), 0, A.add)
-    ts(Q(3), P(3), 288, A.mult, 144, A.add)
-    ts(Q(4), P(4), -2, A.mult)
-    ts(Q(5), P(4), -2, A.mult, -1, A.add)
-    ts(Q(6), P(5), 0, A.add)
-    ts(W("jm"), W("ji"), Q(2), A.add)
-    ts(W("cl"), W("cli"), Q(1), A.add)
-    fill(W("gm"), 0.0)
-    fill(W("xb"), 0.0)
-    fill(L("ok", 72, 24), 0.0)
-    fill(L("o", 36, 9), 8.0)
-    quant(128, "u", "ut")
-    do("v", lambda: g.vector.tensor_copy(ap(W("Cr")).bitcast(dt.uint32), ap(W("Cu")).bitcast(dt.uint32).indirect(ap(W("ul")))),
-       [W("Cu"), W("ul")], [W("Cr")], 1500.0)
-    act(W("Sr"), W("Su"), AF.Copy, idx=W("ul"))
-
-    EV, OD = 0, 45
-    base = lambda b0, n: L("gm", 288 * b0 + 1, NB * n, 32)
-    last = lambda b0, n, b1=0: L("sc", 288 * b0 + 32 * b1 + 31, n, 32)
-
-    def look(s, name, lo):
-        for b, n in PARTS:
-            c = 288 * s + 32 * b
-            tt(L("gm", c, 16 * n, 2), W("pt"), L("diag", 0, 16 * n), A.mult, idx=L(name, lo + b, n))
-            scan(L("sc", c, 32 * n), L("keepl", 0, 32 * n), L("gm", c, 32 * n))
-
-    def lists(k):
-        for b, n in PARTS:
-            ts(L("uo", 10 * k + b, n), last(blk(k), n, b), 1296, A.add)
-
-    def walk(k0):
-        for k in range(k0 + 1, 8):
-            look(blk(k), "uo", 10 * (k - 1))
-            lists(k)
-
-    def score_lists(t):
-        look(4, "uo", 70)
-        tt(W("dv"), last(1, 72), base(1, 8), A.subtract)
-        tt(L("sov", 0, 36), L("dv", 36, 36), base(0, 4), A.add)
-        tt(L("sov", 36, 36), L("dv", 0, 36), base(5, 4), A.add)
-        for a, (p0, p1) in enumerate(((0, 32), (32, 64), (64, 128))):
-            ts(L("so", 0, 24, 1, p0, p1), L("sov", a, 24, 3, p0, p1), 1296, A.add)
-        if t % 2 == 0:
-            tt(L("dd", 0, 36), L("o", OD, 36), L("o", EV, 36), A.subtract)
-            tt(W("cv"), base(5, 1), W("jm"), A.add)
-        else:
-            tt(L("dd", 0, 27), L("o", EV + 9, 27), L("o", OD, 27), A.subtract)
-            tt(W("cv"), base(1, 1), L("dv", 36, 9), A.add)
-        ts(L("cu", 0, 9), W("cv"), 1296, A.add)
-        ts(base(9, 1), L("o", EV if t % 2 == 0 else OD, 9), 288, A.mult, -1152, A.add)
-        look(9, "cu", 0)
-        tt(W("cd"), last(9, 9), last(blk(1 + t % 2), 9), A.subtract)
+    iota(P(0), [[0, 1]], 0, 1)
+    for j, (sh, bits) in enumerate(((0, 15), (4, 1), (3, 1), (5, 3), (1, 3), (0, 1), (2, 1), (0, 3), (5, 1))):
+        ts(P(1 + j), P(0), sh, A.arith_shift_right, bits, A.bitwise_and)
+        copy(Q(1 + j), P(1 + j)) if j < 2 else None
+    copy(L("pf", 3, 7), L("pi", 3, 7))
+    I, S, HI, M, MI, OD, K4, K1, PAR = [Q(j) for j in range(1, 10)]
+    iota(W("one"), [[0, 520]], 1)
+    iota(W("wli"), [[1, 20]], -1)
+    ts(Q(10), I, 18, A.mult)
+    ts(W("nf")[:2] + (W("nf")[1] + 20, 1, 0, 128), W("wli"), 0, A.max, 17, A.min)
+    ts(W("wl"), L("nf", 0, 20), Q(10), A.add)
+    iota(W("ix"), [[1, 320]], -160)
+    ts(Q(11), I, 0, A.is_equal)
+    ts(Q(12), I, -4.5, A.add)
+    act(Q(12), Q(12), AF.Abs)
+    ts(Q(12), Q(12), 4, A.is_lt, -144, A.mult)
+    aff(W("idm"), W("ix"), Q(11), Q(12))
+    iota(L("ab", 0, 10), [[16, 10]], 0)
+    aff(L("ab", 10, 10), L("ab", 0, 10), 1, I)
+    ts(L("ni", 10, 10), L("ab", 10, 10), -8.5, A.add, 1.0 / 18, A.mult)
+    ts(L("ab", 20, 10), L("ni", 10, 10), -18, A.mult, S, A.add)
+    tt(L("ni", 0, 10), L("ab", 10, 10), L("ab", 20, 10), A.add)
+    ts(L("ni", 20, 10), L("ni", 0, 10), 1, A.bitwise_and)
+    aff(Q(14), S, -32, 1)
+    ts(L("ab", 20, 10), L("ni", 0, 10), 16, A.mult, Q(14), A.add)
+    tt(L("ab", 20, 10), L("ab", 20, 10), L("ni", 10, 10), A.add)
+    ts(L("ab", 10, 10), L("ni", 20, 10), 304, A.mult)
+    tt(L("ab", 0, 10), L("ab", 10, 10), L("ab", 20, 10), A.add)
+    copy(W("pll"), L("ab", 0, 10))
+    iota(W("oi"), [[0, 2], [64, 5]], 9)
+    aff(Q(15), K4, 16, K1)
+    aff(Q(16), HI, 32, Q(15))
+    ts(Q(17), S, HI, A.not_equal, 304, A.mult)
+    aff(Q(18), S, 16, Q(15))
+    aff(Q(18), HI, 16, Q(18))
+    ts(L("ol_", 0, 5), L("oi", 0, 5), Q(16), A.add)
+    ts(L("ol_", 5, 5), L("oi", 5, 5), Q(18), A.add, Q(17), A.add)
+    iota(W("bi"), [[1, 16]], 0)
+    ts(Q(19), I, 14, A.is_ge, OUT, A.mult)
+    ts(W("bias"), L("bi", 1, 10), I, A.is_equal, LOW, A.mult)
+    aff(W("bias"), W("bias"), 1, Q(19))
+    iota(L("fh", 0, 64), [[1, 8], [0, 8]], 1)
+    iota(L("fh", 64, 16), [[12, 2], [1, 8]], 1)
+    iota(L("fh", 80, 64), [[0, 8], [1, 8]], 1)
+    iota(L("fh", 144, 16), [[0, 16]], 30)
+    aff(Q(20), I, 1, -1)
+    ts(W("e1"), W("fh"), I, A.is_equal, -UP, A.mult)
+    ts(W("e2"), W("fh"), Q(20), A.is_equal, UP, A.mult)
+    ts(Q(21), I, 1, A.is_equal, UP, A.mult)
+    aff(L("e1", 64, 8), L("e1", 64, 8), (UP + 288.0) / UP, Q(21))
+    tt(L("e1", 0, 80), L("e1", 0, 80), L("e1", 80, 80), A.add)
+    tt(L("e2", 0, 80), L("e2", 0, 80), L("e2", 80, 80), A.add)
+    ts(Q(22), I, 14, A.is_equal, -UP, A.mult)
+    aff(Q(22), Q(11), OUT, Q(22))
+    aff(L("e2", 0, 80), L("e2", 0, 80), 1, Q(22))
+    tt(W("dtab"), L("e1", 0, 80), L("e2", 0, 80), A.add)
+    iota(L("ji", 0, 10), [[32, 10]], -144)
+    iota(L("ji", 10, 10), [[64, 5], [16, 2]], -144)
+    aff(Q(23), S, 16, I)
+    aff(Q(24), S, 32, I)
+    ts(W("j0"), L("ji", 0, 10), Q(23), A.add, 143, A.min)
+    ts(W("j1"), L("ji", 10, 10), Q(24), A.add, 143, A.min)
+    iota(W("keep8"), [[0, 40], [1, 8]], 0)
+    act(W("keep8"), W("keep8"), AF.Sign)
+    iota(W("k3"), [[0, 10], [1, 3]], 0)
+    act(W("k3"), W("k3"), AF.Sign)
+    sfill(W("ak"), 0)
+    sfill(L("o", 160, 8), 0)
+    sfill(L("rt", 160, 16), 0)
+    iota(W("xb"), [[0, 512]], 0)
+    iota(L("tab", 2592, 576), [[0, 2], [1, 288]], -144)
+    iota(L("two", 0, 2), [[256, 2]], 1)
+    iota(L("two", 2, 18), [[-1, 18]], 1)
+    aff(Q(33), M, 2, 0)
+    aff(Q(34), M, 2, 1)
+    aff(Q(32), PAR, -1, 1)
+    aff(Q(39), PAR, 80, Q(33))
+    aff(Q(40), PAR, 1, Q(34))
+    aff(Q(41), PAR, -1, Q(34))
+    aff(L("ki", 0, 2), L("bi", 0, 2), 1, Q(39))
+    iota(L("nf", 20, 8), [[-160, 2], [-1, 2], [1, 2]], 81)
+    aff(L("ki", 2, 8), L("nf", 20, 8), 1, Q(33))
+    aff(L("ki", 6, 2, 3), L("ki", 6, 2, 3), PAR, 160)
+    aff(L("ki", 7, 2), L("ki", 7, 2), Q(32), 160)
+    for c in range(2):
+        aff(L("ki", 10 + 2 * c, 2), L("two", 2, 2), Q(40 + c), 0)
+    ts(Q(25), I, 9, A.min, 8, A.mult)
+    ts(W("kl"), W("ki"), Q(25), A.add)
+    aff(Q(26), S, 1, Q(33))
+    aff(Q(26), I, 16, Q(26))
+    ts(W("fl"), L("two", 0, 2), Q(26), A.add, 287, A.min)
+    ts(Q(27), MI, M, A.is_equal)
+    ts(Q(28), OD, 0, A.is_equal, Q(27), A.mult)
+    ts(Q(29), HI, S, A.is_equal, Q(27), A.mult)
+    aff(Q(30), HI, 16, -160)
+    ts(Q(31), S, OD, A.not_equal, 16, A.mult)
+    aff(Q(31), Q(31), 1, -160)
+    for c in range(2):
+        ts(L("nf", 5 * c, 5), L("ji", 0, 5), 144, A.add, Q(30 + c), A.add)
+        aff(L("nf", 5 * c, 5), L("nf", 5 * c, 5), Q(28 + c), 160)
+    copy(L("ar", 10, 10), L("nf", 0, 10))
+    for c in range(2):
+        aff(L("nf", 10 + 5 * c, 5), L("nf", 5 * c, 5), PAR, 0)
+        ts(L("oi", 5 * c, 5), L("nf", 5 - 5 * c, 5), Q(32), A.mult)
+    tt(L("nf", 10, 10), L("nf", 10, 10), W("oi"), A.add)
+    copy(L("ar", 0, 10), L("nf", 10, 10))
+    aff(Q(35), I, 1, 1)
+    ts(L("dq", 16, 16), W("bi"), I, A.is_equal, OUT, A.mult)
+    ts(L("dq", 32, 16), W("bi"), Q(35), A.is_equal, UP, A.mult)
+    tt(L("dq", 0, 16), L("dq", 16, 16), L("dq", 32, 16), A.add)
+    ts(W("il"), L("two", 2, 18), 0, A.mult, I, A.add)
+    act(W("dg"), L("dq", 0, 16), idx=W("il"))
+    ts(Q(36), I, 15, A.is_lt, -UP, A.mult)
+    copy(W("pgu"), W("pgn"))
+    act(W("pall"), L("tab", 2592, 288), idx=W("pgu"))
+    do("g", lambda: g.affine_select(ap(W("et")), ap(W("one")), [[-1, 520]], A.is_equal, 0.0, 3, 4), [W("one")], [W("et")], 200 + 2.1 * 520)
+    for b in range(4):
+        quant("e", 128 * b, 128, "et", 3 - b)
+    iota(W("io"), [[-1, 128]], 128, 1)
+    iota(W("lt"), [[0, 512]], 0)
+    ts(W("io"), W("io"), 31, A.bitwise_and)
+    ts(L("lt", 0, 128, 4), W("io"), 0, A.is_equal)
+    ts(L("lt", 2, 128, 4), W("io"), 16, A.is_equal)
+    quant("l", 0, 128, "lt")
+    ts(Q(38), I, OD, A.subtract, 8, A.mult)
+    ts(W("ul"), L("two", 2, 10), 0, A.mult, Q(38), A.add)
+    quant("u", 0, 128, "ut")
+    ul = L("ul", 0, 9)
+    do("v", lambda: g.vector.tensor_copy(ap(W("Cr")).bitcast(dt.uint32), ap(W("Cu")).bitcast(dt.uint32).indirect(ap(ul))),
+       [W("Cu"), ul], [W("Cr")], 280.0)
+    act(W("Sr"), W("Su"), idx=ul)
 
     def products(t):
         x = "x%d" % t
-        quant(288, x, x)
+        for h, (c0, n) in enumerate(HALF):
+            quant(x, c0, n, x)
+            if t == 3:
+                continue
+            for i in range(8):
+                bank = (8 * h + i) % 7
+                mm(bank, n, "r", 2 * i, x, c0)
+                (copy if h == 1 and i % 2 == 0 else act)(L("sw", 288 * i + c0, n), PS(bank, 0, n))
         if t == 3:
             return
         dst = T.cores[rank ^ STEP[t]]
-        send(dst, W("Cp%d" % t), W("C" + x), "ca%d" % t, "cb%d" % t, True, 6000.0)
-        send(dst, W("Sp%d" % t), W("S" + x), "sa%d" % t, "sb%d" % t, False, 6000.0)
-        for i in range(8):
-            mm(i, 288, "r", 128 * i, x)
-            if i % 2 == 0:
-                copy(L("sw", 288 * i, 288), L("ps%d" % i, 0, 288))
-            else:
-                act(L("sw", 288 * i, 288), L("ps%d" % i, 0, 288), AF.Copy)
-        for b in range(4):
-            mm(b, 288, "e", 128 * b, x)
-            act(W("f%d" % b), L("ps%d" % b, 0, 288), AF.Copy)
+        send(dst, W("Cp%d" % t), W("C" + x), "ca%d" % t, "cb%d" % t, True, 5000.0)
+        send(dst, W("Sp%d" % t), W("S" + x), "sa%d" % t, "sb%d" % t, False, 5000.0)
+        for b in range(3):
+            mm(1 + b, 288, "e", 128 * b, x)
+            act(W("f%d" % b), PS(1 + b, 0, 288))
+        mm(7, 288, "e", 384, x)
+
+    O = lambda name, lay, k: L(name, 80 * lay + k, 10, 8)
+    run = lambda name, lo, slot, n=10: L(name, lo + slot, n, 16)
+
+    def prepare(t):
+        par = t % 2
+        first, second = L("o", par, 80, 2), L("o", par + 1, 80, 2)
+        tt(W("dd"), second, first, A.subtract)
+        if par:
+            sfill(L("dd", 3, 20, 4), 0)
+        aff(W("cp"), first, 8, 0)
+        tt(W("cp"), W("cp"), second, A.add)
+        if par:
+            aff(L("cp", 3, 10, 4), O("o", 0, 7), 1, 64)
+        for c, src in ((0, 40), (10, 42), (40, 1), (50, 3)):
+            if t < 2 or c < 50:
+                copy(L("uc", c, 10), L("cp", src, 10, 4))
+        sfill(W("ct"), 72)
+        for k in (4 + par, 5 + par):
+            aff(O("ct", 0, k), O("o", 1, k), 1, 64)
+        for k in range(6 + par, 8):
+            act(O("ct", 0, k), L("cp", 42, 10, 4))
+        for e in range(2):
+            ts(L("cq", 80 * e, 80), L("o", 80, 80), Q(33 + e), A.is_equal)
+            tt(L("cq", 80 * e, 80), L("cq", 80 * e, 80), W("ct"), A.mult)
+        sums(W("cs"), L("keep8", 0, 160), W("cq"))
+        copy(L("uc", 20, 20), L("cs", 7, 20, 8))
+        for r, d, lo, n, u0 in (("ra", "da", 0, 160, 0), ("rb", "db", 0, 160, 40), ("ra", "da", 160, 160, 10), ("rb", "db", 160, 160, 50),
+                                ("ra", "da", 320, 160, 20), ("ra", "da", 480, 160, 30)):
+            if (t == 2 and u0 == 50) or (t == 2 and u0 == 10):
+                continue
+            act(L(r, lo, n), W("dtab"), idx=L("uc", u0, n // 16))
+            turn(L(d, lo, n), L(r, lo, n))
+        s0 = O("ak", 1, 0) if par else W("j1")
+        for w in range(2):
+            tt(L("bw", 10 * w, 10), s0, O("o288", 1, par + w), A.add)
+            copy(L("ub", 10 * w, 10), L("bw", 10 * w, 10))
+            pick(L("g0", 160 * w, 160), W("tab"), L("ub", 10 * w, 10), 6 if t + w == 0 else 0)
+            turn(L("t0", 160 * w, 160), L("g0", 160 * w, 160))
+            scan(L("c0", 160 * w, 160), L("da", 0, 160), L("t0", 160 * w, 160))
+        tt(L("s3", 2, 10, 3), run("c0", 0, 15), O("o288", 0, 2 + par), A.add)
+        tt(L("co", 0, 10), run("c0", 160, 15), run("c0", 0, 15), A.subtract)
+        aff(L("co", 10, 10), L("dd", 1, 10, 4), 288, 0)
+        if t < 2:
+            tt(L("co", 20, 10), run("t0", 160, 0), run("t0", 0, 0), A.subtract)
+        sfill(W("st"), -UP)
+        for k in range(2 + par):
+            act(O("st", 0, k), O("ak", 0, 0) if par else W("j0"))
+
+    def bases(par, t):
+        aff(run("db", 0, 15), O("o", 1, 4 + par), 288, 144 - SHIFT)
+        if par:
+            sfill(run("da", 160, 15), 288 * 8 + 144 - SHIFT)
+        elif t < 2:
+            aff(run("da", 160, 15), O("o", 0, 6), 288, 144 - SHIFT)
+
+    def look(n, nv, d=None):
+        n = str(n)
+        pick(W("g" + n), W("tab"), W("u" + n), nv)
+        turn(W("t" + n), W("g" + n))
+        if d:
+            scan(W("c" + n), d, W("t" + n))
+
+    def rest(par, nv, last):
+        scan(W("c2"), L("da", 160, 160), W("t2"))
+        ts(W("u3"), run("c2", 0, 15), SHIFT, A.add)
+        look(3, nv, L("db", 160, 160) if last else None)
+        act(O("ak", 1, 2 + par), run("t1", 0, 0))
+        copy(O("ak", 1, 3 + par), run("c1", 0, 14))
+        act(O("ak", 0, 4 + par), run("t2", 0, 0))
+        copy(O("ak", 0, 5 + par), run("c2", 0, 14))
+        if not par:
+            act(O("ak", 1, 6), run("t3", 0, 0))
+        if last:
+            copy(O("ak", 1, 7), run("c3", 0, 14))
+
+    def score_lists(t):
+        if t:
+            ts(W("ut_"), W("ak"), 144 + 288 * 9, A.add, idx=L("kl", 8 + 2 * t, 2))
+            for c in range(3 - t):
+                act(L("gl", 160 * c, 160), W("tab"), idx=L("ut_", 16 * c, 10))
+                turn(L("tl", 160 * c, 160), L("gl", 160 * c, 160))
+                act(O("ak", 2 - c, 0), run("tl", 160 * c, 0))
+        act(W("sg"), L("o288", 0, 168), idx=L("kl", 2 * t, 2))
+        tt(W("sa"), W("ak"), W("sg"), A.add, idx=L("kl", 4 + 2 * t if t else 0, 2))
+        copy(W("so"), W("sa"))
 
     products(0)
-    tt(W("od"), L("oi", 1, 72, 2), L("oi", 0, 72, 2), A.subtract)
-    ts(W("od"), W("od"), Q(6), A.mult)
-    tt(L("o", EV, 36), L("od", 0, 36), L("oi", 0, 36, 2), A.add)
-    tt(L("o", OD, 36), L("od", 36, 36), L("oi", 72, 36, 2), A.add)
-    ts(base(0, BL), W("o"), 288, A.mult, -1152, A.add)
-    for h in range(2):
-        ts(L("pt", H * h, H), L("raw", H * h, H), -144, A.add, idx=W("cl"))
-    tt(last(0, 9), base(0, 1), W("jm"), A.add)
-    lists(0)
-    walk(0)
+    tt(W("wx"), W("raw"), W("idm"), A.add, idx=W("wl"))
+    turn(L("tw", 0, 288), L("wx", 16, 288))
+    turn(L("tw", 288, 320), W("wx"))
+    ts(W("pl"), W("tw"), 144, A.add, idx=L("pll", 0, 9))
+    act(L("o", 0, 160), W("tw"), idx=W("ol_"))
+    for r in range(8):
+        o, w, b, i = L("tab", 288 * r, 288), L("wx", 16, 288), L("bias", r, 1), L("pl", 18 * r, 18)
+        aff(o, w, 1, b, idx=i)
+    aff(L("tab", 2304, 288), L("wx", 16, 288), 1, Q(19))
+    aff(W("o288"), W("o"), 288, 144)
+    prepare(0)
+    bases(0, 0)
+    copy(W("u1"), L("s3", 2, 10, 3))
+    look(1, 6, L("db", 0, 160))
+    ts(W("u2"), run("c1", 0, 15), SHIFT, A.add)
+    look(2, 6)
+    act(O("ak", 0, 0), run("t0", 0, 0))
+    copy(O("ak", 0, 1), run("c0", 0, 15))
+    rest(0, 6, True)
     score_lists(0)
-    quant(128, "v", "vt")
+    quant("v", 0, 128, "vt")
 
     for t in range(3):
-        dst = T.cores[rank ^ STEP[t]]
-        for h in (0, 192):
-            tt(L("ge", h, 192), W("sw"), L("diag", 0, 192), A.mult, idx=L("so", h // 16, 12))
-            scan(L("ee", h, 192), L("keepf", 0, 192), L("ge", h, 192))
-        n = 12 if t % 2 == 0 else 9
-        for a in range(3):
-            p = (32 * a, 32 * a + 32)
-            ev, od = L("ee", 15 if n == 12 else 63, n, 16, *p), L("ee", 207, n, 16, *p)
-            tt(L("xb", 4 * a, n, 12, *p), *((ev, od) if n == 12 else (od, ev)), A.is_gt)
-        quant(128, "b", "xb")
-        mm(7, 128, "l", 0, "b")
-        k1 = 1 + t % 2
-        tt(W("cx"), L("ps7", 0, 9), W("cd"), A.mult)
-        tt(last(blk(k1), 9), last(blk(k1), 9), W("cx"), A.add)
-        lists(k1)
-        m = 3 * n
-        lo, hi = (L("o", EV, 36), L("o", OD, 36)) if n == 12 else (L("o", OD, 27), L("o", EV + 9, 27))
-        tt(L("mm", 0, m), L("ps7", 0, m), L("dd", 0, m), A.mult)
-        tt(lo, lo, L("mm", 0, m), A.add)
-        tt(hi, hi, L("mm", 0, m), A.subtract)
-        ts(base(0, 4), L("o", EV, 36), 288, A.mult, -1152, A.add)
-        ts(base(5, 4), L("o", OD, 36), 288, A.mult, -1152, A.add)
-        if n == 12:
-            tt(last(0, 9), base(0, 1), W("jm"), A.add)
-        else:
-            tt(last(5, 9), base(5, 1), L("dv", 36, 9), A.add)
-        for e in range(2):
-            act(L("ab", 81 * e, 81), W("o"), AF.Abs, bias=Q(4 + e))
-        for e in range(2):
-            act(L("oh", 81 * e, 81), L("ab", 81 * e, 81), AF.Relu, bias=1.0, scale=-1.0)
-        walk(k1)
-        for to, b0, nb in ((0, 0, 3), (54, 5, 3), (108, 3, 1), (126, 8, 1)):
-            for e in range(2):
-                tt(L("pm", to + e, NB * nb, 2), last(b0, NB * nb), L("oh", 81 * e + 9 * b0, NB * nb), A.mult)
-        tt(L("pq", 0, 54), L("pm", 0, 54), L("pm", 54, 54), A.add)
-        tt(L("pq", 54, 18), L("pq", 0, 18), L("pq", 18, 18), A.add)
-        tt(L("pq", 72, 18), L("pq", 54, 18), L("pq", 36, 18), A.add)
-        tt(L("pq", 90, 18), L("pq", 72, 18), L("pm", 108, 18), A.add)
-        tt(L("pq", 108, 18), L("pq", 90, 18), L("pm", 126, 18), A.add)
-        ts(W("uf"), L("pq", 108, 18), 1296, A.add)
-        al, bl, ll = "al%d" % t, W("bl%d" % t), W("ll%d" % t)
-        for b, n in PARTS:
-            c = L("fg", 32 * b, 32 * n), L("ft", 32 * b, 32 * n)
-            copy(c[0], W("pt"), idx=L("uf", 2 * b, 2 * n))
-            turn(c[1], c[0])
-            ts(L(al, 2 * b, 2 * n), L("ft", 32 * b, 2 * n, 16), 144, A.add)
-        send(dst, ll, W(al), "la%d" % t, "lb%d" % t)
-        ts(W("ub"), L("ft", 0, 18, 16), Q(3), A.add)
-        tt(W("gb"), W("pt"), L("diag", 0, 288), A.mult, idx=W("ub"))
-        scan(W("sb"), L("keepb", 0, 288), W("gb"))
-        ts(bl, L("sb", 15, 18, 16), 144, A.add)
-        for b in range(4):
-            bank = 4 + b if b < 3 else 0
-            mm(bank, 288, "e", 128 * b, "p%d" % t)
-            act(W("d%d" % b), L("ps%d" % bank, 0, 288), AF.Copy)
+        dst, par = T.cores[rank ^ STEP[t]], t % 2
+        act(L("eb", 0, 96), W("sw"), idx=L("so", 16, 6))
+        copy(L("eb", 96, 64), W("sw"), idx=L("so", 22, 4))
+        tt(L("rr", 96, 64), W("sw"), L("eb", 96, 64), A.is_gt, idx=L("so", 6, 4))
+        tt(L("rr", 0, 96), W("sw"), L("eb", 0, 96), A.is_gt, idx=L("so", 0, 6))
+        turn(L("rt", 0, 160), W("rr"))
+        ar = 10 if t else 0
+        copy(L("xb", 0, 96, 2), W("rt"), idx=L("ar", ar, 6))
+        act(L("xb", 192, 64, 2), W("rt"), idx=L("ar", ar + 6, 4))
+        quant("b", 0, 128, "xb")
+        mm(0, 128, "l", 0, "b")
+        for m in range(2):
+            tt(L("s3", m, 10, 3), PS(0, m, 10, 4), L("co", 10 * m, 10), A.mult)
+        sums(W("s3o"), W("k3"), W("s3"))
+        copy(W("u1"), L("s3o", 2, 10, 3))
+        tt(W("mm"), PS(0, 0, 80), W("dd"), A.mult)
         if t < 2:
+            tt(L("bw", 0, 10), PS(0, 0, 10, 4), L("co", 20, 10), A.mult)
+        for lay in range(2):
+            first, second, d = L("o", 80 * lay + par, 40, 2), L("o", 80 * lay + par + 1, 40, 2), L("mm", 40 * lay, 40)
+            tt(first, first, d, A.add)
+            if t < 2 or not lay:
+                tt(second, second, d, A.subtract)
+        bases(par, t)
+        tt(O("st", 0, 2 + par), L("s3", 0, 10, 3), run("c0", 0, 15), A.add)
+        act(O("st", 0, 3 + par), O("st", 0, 2 + par))
+        sfill(L("bt", par, 40, 2), 288 * 8 + 144 - SHIFT)
+        aff(L("bt", par + 1, 40, 2), L("o", par, 40, 2), 288, 144 - SHIFT)
+        for k in (4 + par, 5 + par):
+            sfill(O("bt", 0, k), 288 * 10 + 144 - SHIFT)
+        if par:
+            sfill(O("bt", 0, 0), 288 * 9 + 144 - SHIFT)
+        for e in range(2):
+            ts(L("oh", 80 * e, 80), L("o", 0, 80), Q(33 + e), A.is_equal)
+            tt(L("pr", 80 * e, 72), L("oh", 80 * e, 72), L("st", 0, 72), A.mult)
+            tt(L("pr", 160 + 80 * e, 72), L("oh", 80 * e, 72), L("bt", 0, 72), A.mult)
+        if t == 0:
+            sfill(L("pr", 72, 8), 0), sfill(L("pr", 152, 8), 0), sfill(L("pr", 232, 8), 0), sfill(L("pr", 312, 8), 0)
+        for c in range(2):
+            sums(L("ss", 160 * c, 160), L("keep8", 0, 160), L("pr", 160 * c, 160))
+            act(run("da", 320, 14 + c, 20), L("ss", 160 * c + 7, 20, 8))
+        look(1, 6, L("db", 0, 160))
+        ts(W("u2"), run("c1", 0, 15), SHIFT, A.add)
+        look(2, 6)
+        for e in range(2):
+            scan(L("cf", 160 * e, 144), L("da", 320 + 160 * e, 144), L("t2", 0, 144))
+            ts(L("uf", e, 9, 2), run("cf", 160 * e, 15, 9), SHIFT, A.add)
+        pick(W("gf"), W("tab"), W("uf"), 10)
+        turn(W("tf"), W("gf"))
+        al, bl, ll = "al%d" % t, "bl%d" % t, W("ll%d" % t)
+        ts(W(al), W("tf"), 144, A.add, idx=W("fl"))
+        send(dst, ll, L(al, 0, 18), "la%d" % t, "lb%d" % t)
+        act(W("gb"), W("pall"), idx=L(al, 0, 18))
+        scan(W("cb"), W("dg"), W("gb"))
+        ts(W(bl), run("cb", 0, 15, 18), Q(36), A.add, 144, A.add)
+        for b in range(4):
+            bank = 5 + b % 2
+            mm(bank, 288, "e", 128 * b, "p%d" % t)
+            act(W("d%d" % b), PS(bank, 0, 288))
+        if t < 2:
+            tt(O("ak", 0, par), L("bw", 0, 10), run("t0", 0, 0), A.add)
+            act(O("ak", 0, par + 1), O("st", 0, 2 + par))
+            aff(W("o288"), W("o"), 288, 144)
+            rest(par, 0, t == 1)
             score_lists(t + 1)
+            prepare(t + 1)
         else:
-            for k in range(8):
-                act(L("ok", 9 * k, 9), L("o", 9 * blk(k), 9), AF.Copy)
-            turn(W("ot"), W("ok"))
-            dmas([("y", T.old[32 * i:32 * i + r, :], T.ot[0:r, 32 * i:32 * i + 32], [L("ot", 32 * i, 32, 1, 0, r)],
-                   [L("old", 0, 32, 1, 32 * i, 32 * i + r)]) for i, r in ((0, 32), (1, 32), (2, 8))])
-            dmas([("y", T.ol[:, :], T.old[:, :], [L("old", 0, 32, 1, 0, 72)], [])])
+            turn(W("ot"), L("o", 0, 96))
+            dmas([("y", T.ol[:, 32 * c:32 * c + 32], T.ot[8 * (c % 4):8 * (c % 4) + 8, 32 * (c // 4):32 * (c // 4) + 32], [W("ot")], [])
+                  for c in range(9)])
         z = "z%d" % t
         for b in (0, 2, 1, 3):
-            if b < 2:
-                copy(L(z, b, 288, 4), W("d%d" % b), idx=ll)
-            else:
-                act(L(z, b, 288, 4), W("d%d" % b), AF.Copy, idx=ll)
-        quant(288, z, z)
+            (copy if b < 2 else act)(L(z, b, 288, 4), W("d%d" % b), idx=ll)
+        quant(z, 0, 288, z)
         for b in range(4):
             mm(1 + b, 288, "w", 128 * b, z)
-            act(W("r%d" % b), L("ps%d" % (1 + b), 0, 288), AF.Identity, scale=0.03125)
-        for b in range(4):
-            tt(L("x%d" % (t + 1), b, 288, 4), W("r%d" % b), W("f%d" % b), A.add, idx=bl)
+            aff(W("r%d" % b), PS(1 + b, 0, 288), 0.03125)
+        for c0, n in HALF:
+            x, i = "x%d" % (t + 1), L(bl, c0 // 16, n // 16)
+            for b in range(3):
+                tt(L(x, 4 * c0 + b, n, 4), W("r%d" % b), L("f%d" % b, c0, n), A.add, idx=i)
+            act(L("r4", c0, n), W("r3"), idx=i)
+            tt(L(x, 4 * c0 + 3, n, 4), PS(7, c0, n), L("r4", c0, n), A.add)
         products(t + 1)
 
-    for h in range(2):
-        mm(5 + h, 144, "v", 0, "x3", 144 * h)
-    copy(L("yt", 0, 144), L("ps5", 0, 144))
-    act(L("yt", 144, 144), L("ps6", 0, 144), AF.Copy)
+    for h, (c0, n) in enumerate(HALF):
+        mm(5 + h, n, "v", 0, "x3", c0)
+        (copy if h else act)(L("yt", c0, n), PS(5 + h, 0, n))
     dmas([("y", T.y[:, :], T.yt[:, :], [W("yt")], [])])
     dmas([("y", T.oc[:, :], u8(W("Cx3")), [W("Cx3")], [])]
          + [("s", T.osc[4 * k:4 * k + 4, :], T.Sx3[32 * k:32 * k + 4, 0:288], [W("Sx3")], []) for k in range(4)])
 
     if not ORDER:
         N = len(ops)
-        nxt, left, prio = [[] for _ in ops], [len(o["wait"]) for o in ops], [0.0] * N
+        nxt, prio = [[] for _ in ops], [0.0] * N
         for i, o in enumerate(ops):
             for m in o["wait"]:
                 nxt[m].append(i)
-        span = lambda o: (o["lat"] if o["q"] else 0.0) or o["dur"]
+        span = lambda o: o["dur"]["v"] if o["q"] == "f" else (o["lat"] if o["q"] else 0.0) or o["dur"]
         for i in reversed(range(N)):
             prio[i] = span(ops[i]) + max([0.0] + [WAKE + prio[k] for k in nxt[i]])
-        ready, free, done = {i: 0.0 for i in range(N) if not left[i]}, {q: 0.0 for q in list(queue) + [None]}, [0.0] * N
-        while ready:
-            begin = {i: max(r, free[ops[i]["q"]]) for i, r in ready.items()}
-            first = min(begin, key=lambda i: (begin[i], -prio[i]))
-            i = max((k for k in begin if ops[k]["q"] == ops[first]["q"] and begin[k] <= begin[first] + NEAR), key=lambda k: (prio[k], -k))
-            o = ops[i]
-            at = ready.pop(i)
-            if o["q"]:
-                free[o["q"]] = begin[i] + o["dur"]
-                done[i] = begin[i] + span(o)
-            else:
-                done[i] = at
-            ORDER.append(i)
-            for k in nxt[i]:
-                left[k] -= 1
-                if not left[k]:
-                    ready[k] = WAKE + max(done[m] for m in ops[k]["wait"])
+
+        def place(key, before, after, on, back):
+            left, start, end, on = [len(b) for b in before], [0.0] * N, [0.0] * N, dict(on)
+            busy = {q: [] for q in queue}
+            ready = [(key[i], i) for i in range(N) if not left[i]]
+            while ready:
+                ready.sort(reverse=True)
+                i = ready.pop()[1]
+                o = ops[i]
+                at0 = max([0.0] + [end[m] + WAKE for m in before[i]])
+                best = None
+                for q in ([on[i]] if back or o["q"] != "f" else ["v", "s"]):
+                    dur = o["dur"][q] if o["q"] == "f" else o["dur"]
+                    lat = o["lat"] if q and o["lat"] else dur
+                    at, n = at0 + (lat - dur if back else 0.0), 0
+                    for n, (a, b) in enumerate(busy.get(q, []) + [(1e18, 1e18)]):
+                        if b > at:
+                            if a >= at + dur:
+                                break
+                            at = b
+                    if best is None or at + dur < best[0] + best[1]:
+                        best = (at, dur, lat, q, n)
+                at, dur, lat, q, n = best
+                if q:
+                    busy[q].insert(n, (at, at + dur))
+                    start[i], end[i] = at, at + (dur if back else lat)
+                else:
+                    start[i], end[i] = at0, at0 - WAKE
+                on[i] = q
+                for k in after[i]:
+                    left[k] -= 1
+                    if not left[k]:
+                        ready.append((key[k], k))
+            return start, end, on
+
+        pre = [sorted(o["wait"]) for o in ops]
+        key, on, kept = [-p for p in prio], {i: o["q"] for i, o in enumerate(ops)}, None
+        for _ in range(6):
+            start, end, on = place(key, pre, nxt, on, False)
+            if kept is None or max(end) < max(kept[1]):
+                kept = (start, end, on)
+            key = [-e for e in place([-e for e in end], nxt, pre, on, True)[1]]
+        ORDER.extend((i, kept[2][i]) for i in sorted(range(N), key=lambda i: (kept[0][i], i)))
+        INFO.update(ops=ops, start=kept[0], done=kept[1], on=kept[2])
 
     known, total, waited, snap, token = {q: {} for q in queue}, {}, {}, {}, {}
-    for i in ORDER:
+    for i, q in ORDER:
         o = ops[i]
-        q, sem = o["q"], o["sem"]
+        sem = o["sem"]
+        if o["q"] == "f":
+            sem = q + "q_"
+            o["call"] = lambda o=o, c=o["call"][q], sem=sem: c().then_inc(T.sem[sem], 1)
         if q is None:
             total[sem], token[i] = o["inc"], (sem, o["inc"])
             continue

@@ -9,14 +9,14 @@ SHIFT = 1600
 BF, F32, I32, U16, F16 = "bfloat16", "float32", "int32", "uint16", "float16"
 SCRATCH, PLACE = {}, {}
 for _d, _names in (
-        (BF, "one 520 et 520 lt 512 ut 512 vt 512 wx 320 tab 3168 tw 608 idm 320 dtab 80 pall 288 ra 640 rb 320 da 640 db 320 dg 288 "
-             "g0 320 t0 320 g1 160 t1 160 g2 160 t2 160 g3 160 t3 160 gf 288 tf 288 gl 320 tl 320 gb 288 rr 160 rt 176 fh 160 e1 160 "
-             "e2 160 xb 512 oh 160 bt 88 st 80 pr 320 ss 320 keep8 320 dq 48 cq 160 ct 80 cs 160 f0 288 f1 288 f2 288 d0 288 d1 288 "
+        (BF, "one 520 et 520 lt 512 ut 512 vt 512 tab 2880 tw 608 ix 320 idm 320 dtab 80 pall 288 ra 320 rb 320 da 640 db 320 dg 288 "
+             "g0 320 g1 160 g2 160 g3 160 cw 1120 gf 288 tf 288 gl 320 gb 288 rr 160 rt 176 fh 160 e1 160 "
+             "e2 160 xb 512 oh 160 bt 88 st 80 pr 320 ss 320 keep8 160 dq 48 aa 20 f0 288 f1 288 f2 288 f3 288 d0 288 d1 288 "
              "d2 288 d3 288 x0 1152 x1 1152 x2 1152 x3 1152 z0 1152 z1 1152 z2 1152"),
-        (F32, "pf 48 bias 10 o 168 o288 168 dd 80 mm 80 cp 80 ak 240 j0 10 j1 10 ix 320 bw 20 co 30 s3 30 k3 30 s3o 30 sg 32 sa 32 "
-              "sw 2304 eb 160 ot 96 yt 288 r0 288 r1 288 r2 288 r3 288 r4 288 ab 30 nf 30 ki 14 oi 10 ji 20 bi 16 wli 20 two 20"),
+        (F32, "pf 48 bias 10 o 168 o288 168 dd 80 mm 80 cp 80 j0 10 j1 10 bw 20 co 30 s3 30 k3 30 s3o 30 sg 32 sa 32 "
+              "sw 2304 eb 160 ot 96 yt 288 r0 288 r1 288 r2 288 r3 288 r4 288 ab 30 nf 30 ki 16 oi 10 ji 20 bi 16 wli 20 two 20"),
         (I32, "pi 10 io 128 raw 288 pgn 18 ni 30"),
-        (U16, "wl 20 pl 144 pll 10 ol_ 10 ul 10 pgu 18 kl 14 ar 20 fl 2 il 18 uc 60 ub 20 u1 10 u2 10 u3 10 uf 18 ut_ 32 so 32 "
+        (U16, "wl 20 pl 144 pll 10 ol_ 10 ul 10 pgu 18 kl 16 ar 20 fl 2 il 18 uc 40 ub 20 u1 10 u2 10 u3 10 uf 18 ut_ 32 so 32 "
               "al0 32 al1 32 al2 32 bl0 18 bl1 18 bl2 18 ll0 18 ll1 18 ll2 18"),
         (F16, "c0 320 c1 160 c2 160 c3 160 cf 320 cb 288")):
     _w = _names.split()
@@ -36,6 +36,7 @@ SEMAPHORES = ["vq_", "sq_", "tq_", "gq_"] + ["dm%d" % i for i in range(20)] + [
 ORDER = []
 INFO = {}
 WAKE = 100.0
+FAVOUR = 100.0
 
 
 def rank_program(g, core, T, topo):
@@ -107,17 +108,18 @@ def rank_program(g, core, T, topo):
         return 1.04 * max(64, n * (2 if two and not psum else 0.5 if two_byte and q == "v" and not two else 1))
 
     def do(q, call, reads, writes, dur):
-        rec(q, lambda: call().then_inc(T.sem[q + "q_"], 1), reads, writes, dur, q + "q_")
+        return rec(q, lambda: call().then_inc(T.sem[q + "q_"], 1), reads, writes, dur, q + "q_")
 
     nd = [0]
 
-    def dmas(jobs, lat=2200.0):
+    def dmas(jobs, lat=2200.0, after=()):
         sem = "dm%d" % nd[0]
         nd[0] += 1
         ids = [rec(e, lambda e=e, o=o, i=i: queue[e].dma_start(o, i).then_inc(T.sem[sem], 16), rd, wr, 60.0, sem, 16 * len(jobs), lat, sem)
                for e, o, i, rd, wr in jobs]
         for i in ids:
             ops[i]["mates"] = ids
+            ops[i]["wait"].update(after)
 
     def send(dst, out, in_, arr, loc, code=False, lat=2200.0):
         rid, pid = topo.addr(dst, core)
@@ -131,17 +133,16 @@ def rank_program(g, core, T, topo):
         return [v for v in vs if isinstance(v, tuple)]
 
     def tt(out, a, b, op, idx=None):
-        do("v", lambda: g.vector.tensor_tensor(ap(out), ap(a, idx), ap(b), op), [a, b] + more(idx), [out], cost("v", out, [a, b], idx, True))
+        return do("v", lambda: g.vector.tensor_tensor(ap(out), ap(a, idx), ap(b), op), [a, b] + more(idx), [out],
+                  cost("v", out, [a, b], idx, True))
 
     def ts(out, a, s1, op0, s2=None, op1=None, idx=None):
         c = [ap(s) if isinstance(s, tuple) else s for s in (s1, s2)]
         o2 = (op0,) if op1 is None else (op0, op1)
         do("v", lambda: g.vector.tensor_scalar(ap(out), ap(a, idx), c[0], c[1], *o2), [a] + more(s1, s2, idx), [out], cost("v", out, [a], idx))
 
-    def copy(out, a, idx=None):
-        if all(SCRATCH[v[0]][2] in (BF, F32) for v in (out, a)):
-            return aff(out, a, idx=idx)
-        do("v", lambda: g.vector.tensor_copy(ap(out), ap(a, idx)), [a] + more(idx), [out], cost("v", out, [a], idx))
+    def cast(out, a):
+        do("v", lambda: g.vector.tensor_copy(ap(out), ap(a)), [a], [out], cost("v", out, [a], None))
 
     def scan(out, d0, d1, op0=A.add, op1=A.max):
         do("v", lambda: g.vector.tensor_tensor_scan(ap(out), ap(d0), ap(d1), 0.0, op0, op1), [d0, d1], [out], cost("v", out, [d0, d1], None))
@@ -152,23 +153,24 @@ def rank_program(g, core, T, topo):
     def turn(out, a):
         do("v", lambda: g.vector.transpose(ap(out), ap(a)), [a], [out], cost("v", out, [a], None))
 
-    def act(out, a, func=None, idx=None, **kw):
-        if func is None and out[0] != "Sr":
-            return aff(out, a, idx=idx)
-        func = func or AF.Copy
-        k2 = {k: ap(v) if isinstance(v, tuple) else v for k, v in kw.items()}
-        do("s", lambda: g.scalar.activation(ap(out), ap(a, idx), func, **k2), [a] + more(idx, *kw.values()), [out], cost("s", out, [a], idx))
+    def act(out, a, func, idx=None):
+        do("s", lambda: g.scalar.activation(ap(out), ap(a, idx), func), [a] + more(idx), [out], cost("s", out, [a], idx))
 
-    def aff(out, a, scale=1, bias=0, idx=None):
+    def aff(out, a, scale=1, bias=0, idx=None, spread=False):
         k, c = [ap(s) if isinstance(s, tuple) else float(s) for s in (scale, bias)]
         plain = scale == 1 and bias == 0
         calls = {"v": lambda: g.vector.tensor_copy(ap(out), ap(a, idx)) if plain else g.vector.tensor_scalar(ap(out), ap(a, idx), k, c, A.mult, A.add),
                  "s": lambda: g.scalar.activation(ap(out), ap(a, idx), AF.Copy) if plain else
                  g.scalar.activation(ap(out), ap(a, idx), AF.Identity, bias=c, scale=k)}
-        rec("f", calls, [a] + more(scale, bias, idx), [out], {q: cost(q, out, [a], idx) for q in "vs"}, None)
+        dur = {q: cost(q, out, [a], idx) for q in "vs"}
+        if spread:
+            calls["g"], dur["g"] = lambda: g.partition_broadcast(ap(out), ap(a[:5] + (1,)), 128), 180 + 4.2 * size(out)
+        rec("f", calls, [a] + more(scale, bias, idx), [out], dur, None)
 
-    def sfill(v, k):
-        aff(v, L("one", 0, size(v)), k, 0)
+    def fill(v, k):
+        calls = {"v": lambda: g.vector.memset(ap(v), float(k)),
+                 "g": lambda: g.iota(ap(v), [[0, size(v)]], k, 0, allow_small_or_imprecise_dtypes=True)}
+        rec("f", calls, [], [v], {"g": 160 + 2.1 * size(v), "v": cost("v", v, [], None)}, None)
 
     def quant(name, c0, n, x, x0=None):
         q, s, v = L("C" + name, c0, n), L("S" + name, c0, n), L(x, 4 * c0 if x0 is None else x0, 4 * n)
@@ -179,49 +181,43 @@ def rank_program(g, core, T, topo):
         o = PS(bank, 0, n)
         do("t", lambda: g.tensor.matmul_mx(ap(o), ap(a), ap(b), ap(c), ap(d), True, True), [a, b, c, d], [o], 0.7 * (n + 16))
 
-    def fill(v, k):
-        do("v", lambda: g.vector.memset(ap(v), k), [], [v], cost("v", v, [], None))
-
     def iota(v, pattern, base, cm=0):
         small = SCRATCH[v[0]][2] != I32
         do("g", lambda: g.iota(ap(v), pattern, base, cm, allow_small_or_imprecise_dtypes=True) if small else g.iota(ap(v), pattern, base, cm),
            [], [v], 160 + 2.1 * size(v))
 
-    def pick(out, win, idx, nv):
-        n = size(idx)
-        if nv:
-            copy(L(out[0], out[1], 16 * nv), win, idx=L(idx[0], idx[1], nv))
-        if n > nv:
-            act(L(out[0], out[1] + 16 * nv, 16 * (n - nv)), win, idx=L(idx[0], idx[1] + nv, n - nv))
+    def pick(out, win, idx, cut):
+        for a, b in ((0, cut), (cut, size(idx))):
+            if b > a:
+                aff(L(out[0], out[1] + 16 * a, 16 * (b - a)), win, idx=L(idx[0], idx[1] + a, b - a))
 
-    fill(W("raw"), 0)
-    dmas([("y", T.x0[:, :], T.x[:, :], [], [W("x0")])], 3000.0)
-    dmas([("s", T.ut[:, :], T.u[:, :], [], [W("ut")])], 3000.0)
+    zero = do("v", lambda: g.vector.memset(ap(W("raw")), 0), [], [W("raw")], 300.0)
     dmas([(("y", "s")[h % 2], T.raw[16 * h + 1:16 * h + 9, :], T.pg[:, :], [], [L("raw", 0, 288, 1, 16 * h + 1, 16 * h + 9)]) for h in range(8)]
          + [(("s", "y")[h % 2], T.raw[16 * h + 9:16 * h + 13, :], T.og[64 * (h % 2):64 * (h % 2) + 64, :], [],
              [L("raw", 0, 288, 1, 16 * h + 9, 16 * h + 13)]) for h in range(8)])
-    dmas([("y", T.pgn[:, :], T.pg[:, :], [], [W("pgn")])])
-    dmas([("y", u8(W("Cw")), T.wc[:, :], [], [W("Cw")]), ("y", T.Sw[:, :], T.ws[:, :], [], [W("Sw")]),
-          ("y", T.vt[:, :], T.v[:, :], [], [W("vt")])], 5000.0)
+    dmas([("y", T.ut[:, :], T.u[:, :], [], [W("ut")])], 3000.0, [zero])
+    dmas([("y", T.x0[:, :], T.x[:, :], [], [W("x0")])], 3500.0, [zero])
+    dmas([("y", T.pgn[:, :], T.pg[:, :], [], [W("pgn")])], 3500.0, [zero])
 
     P = lambda j: L("pi", j, 1)
     Q = lambda j: L("pf", j, 1)
     iota(P(0), [[0, 1]], 0, 1)
     for j, (sh, bits) in enumerate(((0, 15), (4, 1), (3, 1), (5, 3), (1, 3), (0, 1), (2, 1), (0, 3), (5, 1))):
         ts(P(1 + j), P(0), sh, A.arith_shift_right, bits, A.bitwise_and)
-        copy(Q(1 + j), P(1 + j)) if j < 2 else None
-    copy(L("pf", 3, 7), L("pi", 3, 7))
+    cast(L("pf", 1, 2), L("pi", 1, 2))
+    cast(L("pf", 3, 7), L("pi", 3, 7))
     I, S, HI, M, MI, OD, K4, K1, PAR = [Q(j) for j in range(1, 10)]
-    iota(W("one"), [[0, 520]], 1)
-    iota(W("wli"), [[1, 20]], -1)
-    ts(Q(10), I, 18, A.mult)
-    ts(W("nf")[:2] + (W("nf")[1] + 20, 1, 0, 128), W("wli"), 0, A.max, 17, A.min)
-    ts(W("wl"), L("nf", 0, 20), Q(10), A.add)
+    iota(L("wli", 1, 18), [[1, 18]], 0)
+    iota(L("wli", 0, 2, 19), [[0, 2]], 0)
+    aff(Q(10), I, 18, 0)
+    ts(W("wl"), W("wli"), Q(10), A.add)
     iota(W("ix"), [[1, 320]], -160)
     ts(Q(11), I, 0, A.is_equal)
-    ts(Q(12), I, -4.5, A.add)
+    aff(Q(12), I, 1, -4.5)
     act(Q(12), Q(12), AF.Abs)
     ts(Q(12), Q(12), 4, A.is_lt, -144, A.mult)
+    ts(Q(19), I, 14, A.is_ge, OUT, A.mult)
+    aff(Q(12), Q(12), 1, Q(19))
     aff(W("idm"), W("ix"), Q(11), Q(12))
     iota(L("ab", 0, 10), [[16, 10]], 0)
     aff(L("ab", 10, 10), L("ab", 0, 10), 1, I)
@@ -234,7 +230,7 @@ def rank_program(g, core, T, topo):
     tt(L("ab", 20, 10), L("ab", 20, 10), L("ni", 10, 10), A.add)
     ts(L("ab", 10, 10), L("ni", 20, 10), 304, A.mult)
     tt(L("ab", 0, 10), L("ab", 10, 10), L("ab", 20, 10), A.add)
-    copy(W("pll"), L("ab", 0, 10))
+    cast(W("pll"), L("ab", 0, 10))
     iota(W("oi"), [[0, 2], [64, 5]], 9)
     aff(Q(15), K4, 16, K1)
     aff(Q(16), HI, 32, Q(15))
@@ -244,9 +240,7 @@ def rank_program(g, core, T, topo):
     ts(L("ol_", 0, 5), L("oi", 0, 5), Q(16), A.add)
     ts(L("ol_", 5, 5), L("oi", 5, 5), Q(18), A.add, Q(17), A.add)
     iota(W("bi"), [[1, 16]], 0)
-    ts(Q(19), I, 14, A.is_ge, OUT, A.mult)
     ts(W("bias"), L("bi", 1, 10), I, A.is_equal, LOW, A.mult)
-    aff(W("bias"), W("bias"), 1, Q(19))
     iota(L("fh", 0, 64), [[1, 8], [0, 8]], 1)
     iota(L("fh", 64, 16), [[12, 2], [1, 8]], 1)
     iota(L("fh", 80, 64), [[0, 8], [1, 8]], 1)
@@ -254,8 +248,6 @@ def rank_program(g, core, T, topo):
     aff(Q(20), I, 1, -1)
     ts(W("e1"), W("fh"), I, A.is_equal, -UP, A.mult)
     ts(W("e2"), W("fh"), Q(20), A.is_equal, UP, A.mult)
-    ts(Q(21), I, 1, A.is_equal, UP, A.mult)
-    aff(L("e1", 64, 8), L("e1", 64, 8), (UP + 288.0) / UP, Q(21))
     tt(L("e1", 0, 80), L("e1", 0, 80), L("e1", 80, 80), A.add)
     tt(L("e2", 0, 80), L("e2", 0, 80), L("e2", 80, 80), A.add)
     ts(Q(22), I, 14, A.is_equal, -UP, A.mult)
@@ -268,221 +260,209 @@ def rank_program(g, core, T, topo):
     aff(Q(24), S, 32, I)
     ts(W("j0"), L("ji", 0, 10), Q(23), A.add, 143, A.min)
     ts(W("j1"), L("ji", 10, 10), Q(24), A.add, 143, A.min)
-    iota(W("keep8"), [[0, 40], [1, 8]], 0)
+    iota(W("keep8"), [[0, 20], [1, 8]], 0)
     act(W("keep8"), W("keep8"), AF.Sign)
     iota(W("k3"), [[0, 10], [1, 3]], 0)
     act(W("k3"), W("k3"), AF.Sign)
-    sfill(W("ak"), 0)
-    sfill(L("o", 160, 8), 0)
-    sfill(L("rt", 160, 16), 0)
-    iota(W("xb"), [[0, 512]], 0)
-    iota(L("tab", 2592, 576), [[0, 2], [1, 288]], -144)
+    fill(L("cw", 0, 160), 0)
+    fill(L("cw", 960, 160), 0)
+    for c in range(4):
+        fill(L("pr", 80 * c + 72, 8), 0)
+    fill(L("o", 160, 8), 0)
+    fill(L("rt", 160, 16), 0)
+    fill(W("xb"), 0)
     iota(L("two", 0, 2), [[256, 2]], 1)
-    iota(L("two", 2, 18), [[-1, 18]], 1)
+    iota(L("two", 2, 18), [[0, 18]], 0)
     aff(Q(33), M, 2, 0)
     aff(Q(34), M, 2, 1)
     aff(Q(32), PAR, -1, 1)
     aff(Q(39), PAR, 80, Q(33))
-    aff(Q(40), PAR, 1, Q(34))
-    aff(Q(41), PAR, -1, Q(34))
+    aff(Q(40), M, 160, 0)
     aff(L("ki", 0, 2), L("bi", 0, 2), 1, Q(39))
-    iota(L("nf", 20, 8), [[-160, 2], [-1, 2], [1, 2]], 81)
-    aff(L("ki", 2, 8), L("nf", 20, 8), 1, Q(33))
-    aff(L("ki", 6, 2, 3), L("ki", 6, 2, 3), PAR, 160)
-    aff(L("ki", 7, 2), L("ki", 7, 2), Q(32), 160)
-    for c in range(2):
-        aff(L("ki", 10 + 2 * c, 2), L("two", 2, 2), Q(40 + c), 0)
+    iota(L("nf", 20, 4), [[-1, 2], [1, 2]], 81)
+    aff(L("ki", 2, 4), L("nf", 20, 4), 1, Q(33))
+    iota(L("nf", 24, 6), [[146, 3], [14, 2]], 14)
+    aff(L("nf", 24, 6), L("nf", 24, 6), 1, Q(40))
+    aff(L("ki", 6, 2), L("nf", 26, 2))
+    for c, src, k in ((8, 27, PAR), (9, 29, Q(32)), (10, 24, Q(32)), (11, 26, PAR)):
+        aff(L("ki", c, 1), L("nf", src, 1), k, 0)
+    aff(L("ki", 12, 1), PAR, 146, L("nf", 27, 1))
+    aff(L("ki", 14, 1), PAR, -146, L("nf", 26, 1))
+    fill(L("ki", 13, 2, 2), 160)
     ts(Q(25), I, 9, A.min, 8, A.mult)
-    ts(W("kl"), W("ki"), Q(25), A.add)
+    aff(Q(41), Q(25), 2, 0)
+    ts(L("kl", 0, 6), L("ki", 0, 6), Q(25), A.add)
+    ts(L("kl", 6, 10), L("ki", 6, 10), Q(41), A.add)
     aff(Q(26), S, 1, Q(33))
     aff(Q(26), I, 16, Q(26))
     ts(W("fl"), L("two", 0, 2), Q(26), A.add, 287, A.min)
     ts(Q(27), MI, M, A.is_equal)
     ts(Q(28), OD, 0, A.is_equal, Q(27), A.mult)
     ts(Q(29), HI, S, A.is_equal, Q(27), A.mult)
-    aff(Q(30), HI, 16, -160)
+    aff(Q(30), HI, 16, -16)
     ts(Q(31), S, OD, A.not_equal, 16, A.mult)
-    aff(Q(31), Q(31), 1, -160)
+    aff(Q(31), Q(31), 1, -16)
     for c in range(2):
-        ts(L("nf", 5 * c, 5), L("ji", 0, 5), 144, A.add, Q(30 + c), A.add)
+        aff(L("nf", 5 * c, 5), L("ji", 0, 5), 1, Q(30 + c))
         aff(L("nf", 5 * c, 5), L("nf", 5 * c, 5), Q(28 + c), 160)
-    copy(L("ar", 10, 10), L("nf", 0, 10))
+    cast(L("ar", 10, 10), L("nf", 0, 10))
     for c in range(2):
         aff(L("nf", 10 + 5 * c, 5), L("nf", 5 * c, 5), PAR, 0)
-        ts(L("oi", 5 * c, 5), L("nf", 5 - 5 * c, 5), Q(32), A.mult)
+        aff(L("oi", 5 * c, 5), L("nf", 5 - 5 * c, 5), Q(32), 0)
     tt(L("nf", 10, 10), L("nf", 10, 10), W("oi"), A.add)
-    copy(L("ar", 0, 10), L("nf", 10, 10))
+    cast(L("ar", 0, 10), L("nf", 10, 10))
     aff(Q(35), I, 1, 1)
     ts(L("dq", 16, 16), W("bi"), I, A.is_equal, OUT, A.mult)
     ts(L("dq", 32, 16), W("bi"), Q(35), A.is_equal, UP, A.mult)
     tt(L("dq", 0, 16), L("dq", 16, 16), L("dq", 32, 16), A.add)
-    ts(W("il"), L("two", 2, 18), 0, A.mult, I, A.add)
-    act(W("dg"), L("dq", 0, 16), idx=W("il"))
+    ts(W("il"), L("two", 2, 18), I, A.add)
+    aff(W("dg"), L("dq", 0, 16), idx=W("il"))
     ts(Q(36), I, 15, A.is_lt, -UP, A.mult)
-    copy(W("pgu"), W("pgn"))
-    act(W("pall"), L("tab", 2592, 288), idx=W("pgu"))
+    cast(W("pgu"), W("pgn"))
+    aff(W("pall"), L("ix", 16, 288), idx=W("pgu"))
+    fill(W("one"), 1)
     do("g", lambda: g.affine_select(ap(W("et")), ap(W("one")), [[-1, 520]], A.is_equal, 0.0, 3, 4), [W("one")], [W("et")], 200 + 2.1 * 520)
     for b in range(4):
         quant("e", 128 * b, 128, "et", 3 - b)
     iota(W("io"), [[-1, 128]], 128, 1)
-    iota(W("lt"), [[0, 512]], 0)
+    fill(W("lt"), 0)
     ts(W("io"), W("io"), 31, A.bitwise_and)
     ts(L("lt", 0, 128, 4), W("io"), 0, A.is_equal)
     ts(L("lt", 2, 128, 4), W("io"), 16, A.is_equal)
     quant("l", 0, 128, "lt")
     ts(Q(38), I, OD, A.subtract, 8, A.mult)
-    ts(W("ul"), L("two", 2, 10), 0, A.mult, Q(38), A.add)
+    ts(W("ul"), L("two", 2, 10), Q(38), A.add)
     quant("u", 0, 128, "ut")
     ul = L("ul", 0, 9)
     do("v", lambda: g.vector.tensor_copy(ap(W("Cr")).bitcast(dt.uint32), ap(W("Cu")).bitcast(dt.uint32).indirect(ap(ul))),
        [W("Cu"), ul], [W("Cr")], 280.0)
-    act(W("Sr"), W("Su"), idx=ul)
+    act(W("Sr"), W("Su"), AF.Copy, idx=ul)
 
     def products(t):
         x = "x%d" % t
-        for h, (c0, n) in enumerate(HALF):
+        for c0, n in HALF if t else ((0, 288),):
             quant(x, c0, n, x)
-            if t == 3:
-                continue
-            for i in range(8):
-                bank = (8 * h + i) % 7
-                mm(bank, n, "r", 2 * i, x, c0)
-                (copy if h == 1 and i % 2 == 0 else act)(L("sw", 288 * i + c0, n), PS(bank, 0, n))
+            for i in range(8 if t < 3 else 0):
+                mm(i, n, "r", 2 * i, x, c0)
+                aff(L("sw", 288 * i + c0, n), PS(i, 0, n), spread=True)
         if t == 3:
             return
         dst = T.cores[rank ^ STEP[t]]
-        send(dst, W("Cp%d" % t), W("C" + x), "ca%d" % t, "cb%d" % t, True, 5000.0)
-        send(dst, W("Sp%d" % t), W("S" + x), "sa%d" % t, "sb%d" % t, False, 5000.0)
-        for b in range(3):
-            mm(1 + b, 288, "e", 128 * b, x)
-            act(W("f%d" % b), PS(1 + b, 0, 288))
-        mm(7, 288, "e", 384, x)
+        send(dst, W("Cp%d" % t), W("C" + x), "ca%d" % t, "cb%d" % t, True, 5000.0 if t else 8000.0)
+        send(dst, W("Sp%d" % t), W("S" + x), "sa%d" % t, "sb%d" % t, False, 5000.0 if t else 8000.0)
+        for b in range(4):
+            mm(7 if t == 2 and b == 3 else 1 + b, 288, "e", 128 * b, x)
+            if t < 2 or b < 3:
+                aff(W("f%d" % b), PS(1 + b, 0, 288))
 
     O = lambda name, lay, k: L(name, 80 * lay + k, 10, 8)
     run = lambda name, lo, slot, n=10: L(name, lo + slot, n, 16)
+    R = lambda n, slot=None: L("cw", 160 + 160 * n, 160) if slot is None else run("cw", 160 + 160 * n, slot)
 
     def prepare(t):
         par = t % 2
         first, second = L("o", par, 80, 2), L("o", par + 1, 80, 2)
         tt(W("dd"), second, first, A.subtract)
         if par:
-            sfill(L("dd", 3, 20, 4), 0)
+            fill(L("dd", 3, 20, 4), 0)
         aff(W("cp"), first, 8, 0)
         tt(W("cp"), W("cp"), second, A.add)
         if par:
             aff(L("cp", 3, 10, 4), O("o", 0, 7), 1, 64)
-        for c, src in ((0, 40), (10, 42), (40, 1), (50, 3)):
-            if t < 2 or c < 50:
-                copy(L("uc", c, 10), L("cp", src, 10, 4))
-        sfill(W("ct"), 72)
-        for k in (4 + par, 5 + par):
-            aff(O("ct", 0, k), O("o", 1, k), 1, 64)
-        for k in range(6 + par, 8):
-            act(O("ct", 0, k), L("cp", 42, 10, 4))
-        for e in range(2):
-            ts(L("cq", 80 * e, 80), L("o", 80, 80), Q(33 + e), A.is_equal)
-            tt(L("cq", 80 * e, 80), L("cq", 80 * e, 80), W("ct"), A.mult)
-        sums(W("cs"), L("keep8", 0, 160), W("cq"))
-        copy(L("uc", 20, 20), L("cs", 7, 20, 8))
-        for r, d, lo, n, u0 in (("ra", "da", 0, 160, 0), ("rb", "db", 0, 160, 40), ("ra", "da", 160, 160, 10), ("rb", "db", 160, 160, 50),
-                                ("ra", "da", 320, 160, 20), ("ra", "da", 480, 160, 30)):
-            if (t == 2 and u0 == 50) or (t == 2 and u0 == 10):
-                continue
-            act(L(r, lo, n), W("dtab"), idx=L("uc", u0, n // 16))
-            turn(L(d, lo, n), L(r, lo, n))
-        s0 = O("ak", 1, 0) if par else W("j1")
+        for r, lo, u0, src, d, to in (("ra", 0, 0, 40, "da", (0,)), ("rb", 0, 20, 1, "db", (0,)),
+                                      ("ra", 160, 10, 42, "da", (160, 320, 480)[t // 2:]), ("rb", 160, 30, 3, "db", (160,)))[:4 - t // 2]:
+            cast(L("uc", u0, 10), L("cp", src, 10, 4))
+            aff(L(r, lo, 160), W("dtab"), idx=L("uc", u0, 10))
+            for c in to:
+                turn(L(d, c, 160), L(r, lo, 160))
+        fill(W("st"), -UP)
+        fill(O("st", 0, 4 + par), OUT)
+        for k in range(2 + par):
+            aff(O("st", 0, k), R(0, 0) if par else W("j0"))
+        s0 = R(-1, 14) if par else W("j1")
         for w in range(2):
             tt(L("bw", 10 * w, 10), s0, O("o288", 1, par + w), A.add)
-            copy(L("ub", 10 * w, 10), L("bw", 10 * w, 10))
+            cast(L("ub", 10 * w, 10), L("bw", 10 * w, 10))
             pick(L("g0", 160 * w, 160), W("tab"), L("ub", 10 * w, 10), 6 if t + w == 0 else 0)
-            turn(L("t0", 160 * w, 160), L("g0", 160 * w, 160))
-            scan(L("c0", 160 * w, 160), L("da", 0, 160), L("t0", 160 * w, 160))
+            turn(R(4 * w), L("g0", 160 * w, 160))
+            scan(L("c0", 160 * w, 160), L("da", 0, 160), R(4 * w))
         tt(L("s3", 2, 10, 3), run("c0", 0, 15), O("o288", 0, 2 + par), A.add)
         tt(L("co", 0, 10), run("c0", 160, 15), run("c0", 0, 15), A.subtract)
         aff(L("co", 10, 10), L("dd", 1, 10, 4), 288, 0)
         if t < 2:
-            tt(L("co", 20, 10), run("t0", 160, 0), run("t0", 0, 0), A.subtract)
-        sfill(W("st"), -UP)
-        for k in range(2 + par):
-            act(O("st", 0, k), O("ak", 0, 0) if par else W("j0"))
+            tt(L("co", 20, 10), R(4, 0), R(0, 0), A.subtract)
 
     def bases(par, t):
         aff(run("db", 0, 15), O("o", 1, 4 + par), 288, 144 - SHIFT)
         if par:
-            sfill(run("da", 160, 15), 288 * 8 + 144 - SHIFT)
+            fill(run("da", 160, 15), 288 * 8 + 144 - SHIFT)
         elif t < 2:
             aff(run("da", 160, 15), O("o", 0, 6), 288, 144 - SHIFT)
 
-    def look(n, nv, d=None):
-        n = str(n)
-        pick(W("g" + n), W("tab"), W("u" + n), nv)
-        turn(W("t" + n), W("g" + n))
+    def look(n, cut, d=None):
+        pick(W("g%d" % n), W("tab"), W("u%d" % n), cut)
+        turn(R(n), W("g%d" % n))
         if d:
-            scan(W("c" + n), d, W("t" + n))
+            scan(W("c%d" % n), d, R(n))
 
-    def rest(par, nv, last):
-        scan(W("c2"), L("da", 160, 160), W("t2"))
+    def rest(par, cut, last):
+        scan(W("c2"), L("da", 160, 160), R(2))
         ts(W("u3"), run("c2", 0, 15), SHIFT, A.add)
-        look(3, nv, L("db", 160, 160) if last else None)
-        act(O("ak", 1, 2 + par), run("t1", 0, 0))
-        copy(O("ak", 1, 3 + par), run("c1", 0, 14))
-        act(O("ak", 0, 4 + par), run("t2", 0, 0))
-        copy(O("ak", 0, 5 + par), run("c2", 0, 14))
-        if not par:
-            act(O("ak", 1, 6), run("t3", 0, 0))
-        if last:
-            copy(O("ak", 1, 7), run("c3", 0, 14))
+        look(3, cut, L("db", 160, 160) if last else None)
+        for n in (1, 2, 3) if last else (1, 2):
+            cast(R(n, 0 if par and n == 3 else 14), run("c%d" % n, 0, 14))
 
     def score_lists(t):
         if t:
-            ts(W("ut_"), W("ak"), 144 + 288 * 9, A.add, idx=L("kl", 8 + 2 * t, 2))
-            for c in range(3 - t):
-                act(L("gl", 160 * c, 160), W("tab"), idx=L("ut_", 16 * c, 10))
-                turn(L("tl", 160 * c, 160), L("gl", 160 * c, 160))
-                act(O("ak", 2 - c, 0), run("tl", 160 * c, 0))
-        act(W("sg"), L("o288", 0, 168), idx=L("kl", 2 * t, 2))
-        tt(W("sa"), W("ak"), W("sg"), A.add, idx=L("kl", 4 + 2 * t if t else 0, 2))
-        copy(W("so"), W("sa"))
+            ts(W("ut_"), W("cw"), 144 + 288 * 9, A.add, idx=L("kl", 10 + 2 * t, 2))
+            aff(L("gl", 0, 160), W("tab"), idx=L("ut_", 0, 10))
+            if t == 1:
+                aff(L("gl", 160, 160), W("tab"), idx=L("ut_", 16, 10))
+                turn(R(5), L("gl", 160, 160))
+            turn(R(-1), L("gl", 0, 160))
+            aff(R(-1, 14), R(5, 0))
+        aff(W("sg"), L("o288", 0, 168), idx=L("kl", 2 * t, 2))
+        tt(W("sa"), W("cw"), W("sg"), A.add, idx=L("kl", 6 + 2 * t, 2))
+        cast(W("so"), W("sa"))
 
     products(0)
-    tt(W("wx"), W("raw"), W("idm"), A.add, idx=W("wl"))
-    turn(L("tw", 0, 288), L("wx", 16, 288))
-    turn(L("tw", 288, 320), W("wx"))
+    rows = tt(L("tab", 2288, 320), W("raw"), W("idm"), A.add, idx=W("wl"))
+    dmas([("y", u8(W("Cw")), T.wc[:, :], [], [W("Cw")]), ("y", T.Sw[:, :], T.ws[:, :], [], [W("Sw")]),
+          ("y", T.vt[:, :], T.v[:, :], [], [W("vt")])], 5000.0, [rows])
+    turn(L("tw", 0, 288), L("tab", 2304, 288))
+    turn(L("tw", 288, 320), L("tab", 2288, 320))
+    iota(L("tab", 2592, 288), [[1, 288]], -144)
     ts(W("pl"), W("tw"), 144, A.add, idx=L("pll", 0, 9))
-    act(L("o", 0, 160), W("tw"), idx=W("ol_"))
+    aff(L("o", 0, 160), W("tw"), idx=W("ol_"))
     for r in range(8):
-        o, w, b, i = L("tab", 288 * r, 288), L("wx", 16, 288), L("bias", r, 1), L("pl", 18 * r, 18)
-        aff(o, w, 1, b, idx=i)
-    aff(L("tab", 2304, 288), L("wx", 16, 288), 1, Q(19))
+        aff(L("tab", 288 * r, 288), L("tab", 2304, 288), 1, L("bias", r, 1), idx=L("pl", 18 * r, 18))
     aff(W("o288"), W("o"), 288, 144)
     prepare(0)
     bases(0, 0)
-    copy(W("u1"), L("s3", 2, 10, 3))
+    cast(W("u1"), L("s3", 2, 10, 3))
     look(1, 6, L("db", 0, 160))
     ts(W("u2"), run("c1", 0, 15), SHIFT, A.add)
     look(2, 6)
-    act(O("ak", 0, 0), run("t0", 0, 0))
-    copy(O("ak", 0, 1), run("c0", 0, 15))
+    cast(R(0, 14), run("c0", 0, 15))
     rest(0, 6, True)
     score_lists(0)
     quant("v", 0, 128, "vt")
 
     for t in range(3):
         dst, par = T.cores[rank ^ STEP[t]], t % 2
-        act(L("eb", 0, 96), W("sw"), idx=L("so", 16, 6))
-        copy(L("eb", 96, 64), W("sw"), idx=L("so", 22, 4))
+        pick(W("eb"), W("sw"), L("so", 16, 10), 6)
         tt(L("rr", 96, 64), W("sw"), L("eb", 96, 64), A.is_gt, idx=L("so", 6, 4))
         tt(L("rr", 0, 96), W("sw"), L("eb", 0, 96), A.is_gt, idx=L("so", 0, 6))
         turn(L("rt", 0, 160), W("rr"))
         ar = 10 if t else 0
-        copy(L("xb", 0, 96, 2), W("rt"), idx=L("ar", ar, 6))
-        act(L("xb", 192, 64, 2), W("rt"), idx=L("ar", ar + 6, 4))
+        aff(L("xb", 0, 96, 2), W("rt"), idx=L("ar", ar, 6))
+        aff(L("xb", 192, 64, 2), W("rt"), idx=L("ar", ar + 6, 4))
         quant("b", 0, 128, "xb")
         mm(0, 128, "l", 0, "b")
         for m in range(2):
             tt(L("s3", m, 10, 3), PS(0, m, 10, 4), L("co", 10 * m, 10), A.mult)
         sums(W("s3o"), W("k3"), W("s3"))
-        copy(W("u1"), L("s3o", 2, 10, 3))
+        cast(W("u1"), L("s3o", 2, 10, 3))
         tt(W("mm"), PS(0, 0, 80), W("dd"), A.mult)
         if t < 2:
             tt(L("bw", 0, 10), PS(0, 0, 10, 4), L("co", 20, 10), A.mult)
@@ -493,43 +473,41 @@ def rank_program(g, core, T, topo):
                 tt(second, second, d, A.subtract)
         bases(par, t)
         tt(O("st", 0, 2 + par), L("s3", 0, 10, 3), run("c0", 0, 15), A.add)
-        act(O("st", 0, 3 + par), O("st", 0, 2 + par))
-        sfill(L("bt", par, 40, 2), 288 * 8 + 144 - SHIFT)
+        aff(O("st", 0, 3 + par), O("st", 0, 2 + par))
+        fill(L("bt", par, 40, 2), 288 * 8 + 144 - SHIFT)
         aff(L("bt", par + 1, 40, 2), L("o", par, 40, 2), 288, 144 - SHIFT)
-        for k in (4 + par, 5 + par):
-            sfill(O("bt", 0, k), 288 * 10 + 144 - SHIFT)
-        if par:
-            sfill(O("bt", 0, 0), 288 * 9 + 144 - SHIFT)
+        for k in (4 + par, 5 + par) + (0,) * par:
+            fill(O("bt", 0, k), 288 * 9 + 144 - SHIFT)
         for e in range(2):
             ts(L("oh", 80 * e, 80), L("o", 0, 80), Q(33 + e), A.is_equal)
             tt(L("pr", 80 * e, 72), L("oh", 80 * e, 72), L("st", 0, 72), A.mult)
             tt(L("pr", 160 + 80 * e, 72), L("oh", 80 * e, 72), L("bt", 0, 72), A.mult)
-        if t == 0:
-            sfill(L("pr", 72, 8), 0), sfill(L("pr", 152, 8), 0), sfill(L("pr", 232, 8), 0), sfill(L("pr", 312, 8), 0)
         for c in range(2):
-            sums(L("ss", 160 * c, 160), L("keep8", 0, 160), L("pr", 160 * c, 160))
-            act(run("da", 320, 14 + c, 20), L("ss", 160 * c + 7, 20, 8))
+            sums(L("ss", 160 * c, 160), W("keep8"), L("pr", 160 * c, 160))
+            aff(run("da", 320, 14 + c, 20), L("ss", 160 * c + 7, 20, 8))
+        ts(run("da", 320, 13, 20), L("ss", 7, 20, 8), -200, A.is_gt, OUT, A.mult)
+        ts(W("aa"), L("ss", 7, 20, 8), -2000, A.is_lt, -OUT, A.mult)
+        tt(run("da", 320, 1, 20), run("da", 320, 1, 20), W("aa"), A.add)
         look(1, 6, L("db", 0, 160))
         ts(W("u2"), run("c1", 0, 15), SHIFT, A.add)
         look(2, 6)
         for e in range(2):
-            scan(L("cf", 160 * e, 144), L("da", 320 + 160 * e, 144), L("t2", 0, 144))
+            scan(L("cf", 160 * e, 144), L("da", 320 + 160 * e, 144), L("cw", 480, 144))
             ts(L("uf", e, 9, 2), run("cf", 160 * e, 15, 9), SHIFT, A.add)
         pick(W("gf"), W("tab"), W("uf"), 10)
         turn(W("tf"), W("gf"))
-        al, bl, ll = "al%d" % t, "bl%d" % t, W("ll%d" % t)
+        al, bl, ll = "al%d" % t, "bl%d" % t, "ll%d" % t
         ts(W(al), W("tf"), 144, A.add, idx=W("fl"))
-        send(dst, ll, L(al, 0, 18), "la%d" % t, "lb%d" % t)
-        act(W("gb"), W("pall"), idx=L(al, 0, 18))
+        send(dst, W(ll), L(al, 0, 18), "la%d" % t, "lb%d" % t)
+        aff(W("gb"), W("pall"), idx=L(al, 0, 18))
         scan(W("cb"), W("dg"), W("gb"))
         ts(W(bl), run("cb", 0, 15, 18), Q(36), A.add, 144, A.add)
         for b in range(4):
-            bank = 5 + b % 2
-            mm(bank, 288, "e", 128 * b, "p%d" % t)
-            act(W("d%d" % b), PS(bank, 0, 288))
+            mm(5 + b % 2, 288, "e", 128 * b, "p%d" % t)
+            aff(W("d%d" % b), PS(5 + b % 2, 0, 288))
         if t < 2:
-            tt(O("ak", 0, par), L("bw", 0, 10), run("t0", 0, 0), A.add)
-            act(O("ak", 0, par + 1), O("st", 0, 2 + par))
+            tt(R(0, 0), L("bw", 0, 10), R(0, 0), A.add)
+            aff(R(0, 14), O("st", 0, 2 + par))
             aff(W("o288"), W("o"), 288, 144)
             rest(par, 0, t == 1)
             score_lists(t + 1)
@@ -538,27 +516,31 @@ def rank_program(g, core, T, topo):
             turn(W("ot"), L("o", 0, 96))
             dmas([("y", T.ol[:, 32 * c:32 * c + 32], T.ot[8 * (c % 4):8 * (c % 4) + 8, 32 * (c // 4):32 * (c // 4) + 32], [W("ot")], [])
                   for c in range(9)])
-        z = "z%d" % t
-        for b in (0, 2, 1, 3):
-            (copy if b < 2 else act)(L(z, b, 288, 4), W("d%d" % b), idx=ll)
-        quant(z, 0, 288, z)
-        for b in range(4):
-            mm(1 + b, 288, "w", 128 * b, z)
-            aff(W("r%d" % b), PS(1 + b, 0, 288), 0.03125)
+        z, x = "z%d" % t, "x%d" % (t + 1)
+        for h, (c0, n) in enumerate(HALF):
+            for b in range(4):
+                aff(L(z, 4 * c0 + b, n, 4), W("d%d" % b), idx=L(ll, c0 // 16, n // 16))
+            quant(z, c0, n, z)
+            for b in range(4):
+                bank = (1 + b, (5, 6, 0, 1)[b])[h]
+                mm(bank, n, "w", 128 * b, z, c0)
+                aff(L("r%d" % b, c0, n), PS(bank, 0, n), 0.03125)
         for c0, n in HALF:
-            x, i = "x%d" % (t + 1), L(bl, c0 // 16, n // 16)
-            for b in range(3):
-                tt(L(x, 4 * c0 + b, n, 4), W("r%d" % b), L("f%d" % b, c0, n), A.add, idx=i)
-            act(L("r4", c0, n), W("r3"), idx=i)
-            tt(L(x, 4 * c0 + 3, n, 4), PS(7, c0, n), L("r4", c0, n), A.add)
+            i = L(bl, c0 // 16, n // 16)
+            for b in range(4):
+                if t < 2 or b < 3:
+                    tt(L(x, 4 * c0 + b, n, 4), W("r%d" % b), L("f%d" % b, c0, n), A.add, idx=i)
+                else:
+                    aff(L("r4", c0, n), W("r3"), idx=i)
+                    tt(L(x, 4 * c0 + 3, n, 4), PS(7, c0, n), L("r4", c0, n), A.add)
         products(t + 1)
 
     for h, (c0, n) in enumerate(HALF):
         mm(5 + h, n, "v", 0, "x3", c0)
-        (copy if h else act)(L("yt", c0, n), PS(5 + h, 0, n))
-    dmas([("y", T.y[:, :], T.yt[:, :], [W("yt")], [])])
-    dmas([("y", T.oc[:, :], u8(W("Cx3")), [W("Cx3")], [])]
-         + [("s", T.osc[4 * k:4 * k + 4, :], T.Sx3[32 * k:32 * k + 4, 0:288], [W("Sx3")], []) for k in range(4)])
+        aff(L("yt", c0, n), PS(5 + h, 0, n))
+        dmas([("y", T.y[:, c0:c0 + n], T.yt[:, c0:c0 + n], [L("yt", c0, n)], [])])
+        dmas([("s", T.oc[:, 4 * c0:4 * c0 + 4 * n], u8(L("Cx3", c0, n)), [L("Cx3", c0, n)], [])])
+    dmas([("y", T.osc[4 * k:4 * k + 4, :], T.Sx3[32 * k:32 * k + 4, 0:288], [W("Sx3")], []) for k in range(4)], 2000.0)
 
     if not ORDER:
         N = len(ops)
@@ -580,7 +562,7 @@ def rank_program(g, core, T, topo):
                 o = ops[i]
                 at0 = max([0.0] + [end[m] + WAKE for m in before[i]])
                 best = None
-                for q in ([on[i]] if back or o["q"] != "f" else ["v", "s"]):
+                for q in ([on[i]] if back or o["q"] != "f" else sorted(o["dur"])):
                     dur = o["dur"][q] if o["q"] == "f" else o["dur"]
                     lat = o["lat"] if q and o["lat"] else dur
                     at, n = at0 + (lat - dur if back else 0.0), 0
@@ -589,7 +571,7 @@ def rank_program(g, core, T, topo):
                             if a >= at + dur:
                                 break
                             at = b
-                    if best is None or at + dur < best[0] + best[1]:
+                    if best is None or at + dur + (FAVOUR if q == "v" else 0.0) < best[0] + best[1]:
                         best = (at, dur, lat, q, n)
                 at, dur, lat, q, n = best
                 if q:
@@ -606,7 +588,7 @@ def rank_program(g, core, T, topo):
 
         pre = [sorted(o["wait"]) for o in ops]
         key, on, kept = [-p for p in prio], {i: o["q"] for i, o in enumerate(ops)}, None
-        for _ in range(6):
+        for _ in range(8):
             start, end, on = place(key, pre, nxt, on, False)
             if kept is None or max(end) < max(kept[1]):
                 kept = (start, end, on)

@@ -1,22 +1,24 @@
 import math
+import numpy
 from concourse.mybir import dt, AluOpType, ActivationFunctionType
 
 STEP = (4, 1, 2)
 HALF = ((0, 160), (160, 128))
+STAY = (1, 1, 1)
 UP, LOW, OUT = 1024, -768, -4096
 SHIFT = 1600
 
 BF, F32, I32, U16, F16 = "bfloat16", "float32", "int32", "uint16", "float16"
 SCRATCH, PLACE = {}, {}
 for _d, _names in (
-        (BF, "one 520 et 520 lt 512 ut 512 vt 512 tab 2880 tw 608 ix 320 idm 320 dtab 80 pall 288 ra 320 rb 320 da 640 db 320 dg 288 "
-             "g0 320 g1 160 g2 160 g3 160 cw 1120 gf 288 tf 288 gl 320 gb 288 rr 160 rt 176 fh 160 e1 160 "
-             "e2 160 xb 512 oh 160 bt 88 st 80 pr 320 ss 320 keep8 160 dq 48 aa 20 f0 288 f1 288 f2 288 f3 288 d0 288 d1 288 "
+        (BF, "one 520 et 520 lt 512 ut 512 vt 512 tab 2880 tw 608 ix 320 idm 320 dtab 72 pall 288 ra 320 rb 320 da 640 db 320 dg 288 "
+             "g0 320 g1 160 g2 160 g3 160 cw 1120 gf 288 tf 288 gl 320 gb 288 rr 160 rt 176 o 168 dd 160 cp 160 "
+             "two8 320 xb 512 oh 160 bt 88 st 80 pr 320 ss 320 keep8 160 dq 48 aa 40 f0 288 f1 288 f2 288 f3 288 d0 288 d1 288 "
              "d2 288 d3 288 x0 1152 x1 1152 x2 1152 x3 1152 z0 1152 z1 1152 z2 1152"),
-        (F32, "pf 48 bias 10 o 168 o288 168 dd 80 mm 80 cp 80 j0 10 j1 10 bw 20 co 30 s3 30 k3 30 s3o 30 sg 32 sa 32 "
-              "sw 2304 eb 160 ot 96 yt 288 r0 288 r1 288 r2 288 r3 288 r4 288 ab 30 nf 30 ki 16 oi 10 ji 20 bi 16 wli 20 two 20"),
+        (F32, "pf 48 bias 10 o288 168 mm 80 j0 10 j1 10 bw 20 co 30 s3 30 k3 30 s3o 30 sg 32 sa 32 "
+              "sw 2304 eb 160 ot 96 yt 288 r0 288 r1 288 r2 288 r3 288 r4 576 ab 32 nf 30 ki 16 oi 10 ji 20 bi 16 wli 20 two 20"),
         (I32, "pi 10 io 128 raw 288 pgn 18 ni 30"),
-        (U16, "wl 20 pl 144 pll 10 ol_ 10 ul 10 pgu 18 kl 16 ar 20 fl 2 il 18 uc 40 ub 20 u1 10 u2 10 u3 10 uf 18 ut_ 32 so 32 "
+        (U16, "wl 20 pl 256 pll 16 ol_ 10 ul 10 pgu 18 kl 16 ar 20 fl 2 il 18 uc 40 ub 20 u1 10 u2 10 u3 10 uf 18 ut_ 32 so 32 "
               "al0 32 al1 32 al2 32 bl0 18 bl1 18 bl2 18 ll0 18 ll1 18 ll2 18"),
         (F16, "c0 320 c1 160 c2 160 c3 160 cf 320 cb 288")):
     _w = _names.split()
@@ -35,7 +37,11 @@ SEMAPHORES = ["vq_", "sq_", "tq_", "gq_"] + ["dm%d" % i for i in range(20)] + [
     n + str(t) for t in range(3) for n in ("ca", "cb", "sa", "sb", "la", "lb")]
 ORDER = []
 INFO = {}
-WAKE = 100.0
+CASES = ((100.0, 1.0, 15.0, 3400.0), (130.0, 1.1, 0.0, 2300.0))
+POLISH = 9000
+TRIES = 500
+WAKE = 120.0
+CODES, LIST, COLUMN = 6000.0, 2800.0, 0.75
 FAVOUR = 100.0
 
 
@@ -121,7 +127,7 @@ def rank_program(g, core, T, topo):
             ops[i]["mates"] = ids
             ops[i]["wait"].update(after)
 
-    def send(dst, out, in_, arr, loc, code=False, lat=2200.0):
+    def send(dst, out, in_, arr, loc, code=False, lat=LIST):
         rid, pid = topo.addr(dst, core)
         n = len(topo.engines(core, dst))
         f = u8 if code else ap
@@ -153,8 +159,13 @@ def rank_program(g, core, T, topo):
     def turn(out, a):
         do("v", lambda: g.vector.transpose(ap(out), ap(a)), [a], [out], cost("v", out, [a], None))
 
-    def act(out, a, func, idx=None):
-        do("s", lambda: g.scalar.activation(ap(out), ap(a, idx), func), [a] + more(idx), [out], cost("s", out, [a], idx))
+    def act(out, a, func, scale=None, bias=0, idx=None):
+        kw = {} if scale is None else {k: ap(s) if isinstance(s, tuple) else float(s) for k, s in (("scale", scale), ("bias", bias))}
+        do("s", lambda: g.scalar.activation(ap(out), ap(a, idx), func, **kw), [a] + more(idx, scale, bias), [out], cost("s", out, [a], idx))
+
+    def same(out, a, minus, k=1):
+        act(out, a, AF.Abs, 1, minus)
+        act(out, out, AF.Relu, -k, k)
 
     def aff(out, a, scale=1, bias=0, idx=None, spread=False):
         k, c = [ap(s) if isinstance(s, tuple) else float(s) for s in (scale, bias)]
@@ -165,6 +176,9 @@ def rank_program(g, core, T, topo):
         dur = {q: cost(q, out, [a], idx) for q in "vs"}
         if spread:
             calls["g"], dur["g"] = lambda: g.partition_broadcast(ap(out), ap(a[:5] + (1,)), 128), 180 + 4.2 * size(out)
+        elif plain and not idx and size(out) <= 80 and SCRATCH[out[0]][2] == SCRATCH[a[0]][2]:
+            calls["g"] = lambda: g.affine_select(ap(out), ap(a), [[0, size(out)]], A.is_ge, 0.0, 0, 0)
+            dur["g"] = 210 + 2.1 * size(out)
         rec("f", calls, [a] + more(scale, bias, idx), [out], dur, None)
 
     def fill(v, k):
@@ -179,7 +193,7 @@ def rank_program(g, core, T, topo):
     def mm(bank, n, w, w0, x, x0=0):
         a, b, c, d = L("C" + w, w0, 128), L("S" + w, w0, 128), L("C" + x, x0, n), L("S" + x, x0, n)
         o = PS(bank, 0, n)
-        do("t", lambda: g.tensor.matmul_mx(ap(o), ap(a), ap(b), ap(c), ap(d), True, True), [a, b, c, d], [o], 0.7 * (n + 16))
+        do("t", lambda: g.tensor.matmul_mx(ap(o), ap(a), ap(b), ap(c), ap(d), True, True), [a, b, c, d], [o], COLUMN * (n + 16))
 
     def iota(v, pattern, base, cm=0):
         small = SCRATCH[v[0]][2] != I32
@@ -195,7 +209,7 @@ def rank_program(g, core, T, topo):
     dmas([(("y", "s")[h % 2], T.raw[16 * h + 1:16 * h + 9, :], T.pg[:, :], [], [L("raw", 0, 288, 1, 16 * h + 1, 16 * h + 9)]) for h in range(8)]
          + [(("s", "y")[h % 2], T.raw[16 * h + 9:16 * h + 13, :], T.og[64 * (h % 2):64 * (h % 2) + 64, :], [],
              [L("raw", 0, 288, 1, 16 * h + 9, 16 * h + 13)]) for h in range(8)])
-    dmas([("y", T.ut[:, :], T.u[:, :], [], [W("ut")])], 3000.0, [zero])
+    dmas([("y", T.ut[:, :], T.u[:, :], [], [W("ut")])], 2500.0)
     dmas([("y", T.x0[:, :], T.x[:, :], [], [W("x0")])], 3500.0, [zero])
     dmas([("y", T.pgn[:, :], T.pg[:, :], [], [W("pgn")])], 3500.0, [zero])
 
@@ -212,48 +226,41 @@ def rank_program(g, core, T, topo):
     aff(Q(10), I, 18, 0)
     ts(W("wl"), W("wli"), Q(10), A.add)
     iota(W("ix"), [[1, 320]], -160)
-    ts(Q(11), I, 0, A.is_equal)
-    aff(Q(12), I, 1, -4.5)
-    act(Q(12), Q(12), AF.Abs)
-    ts(Q(12), Q(12), 4, A.is_lt, -144, A.mult)
-    ts(Q(19), I, 14, A.is_ge, OUT, A.mult)
-    aff(Q(12), Q(12), 1, Q(19))
+    act(Q(11), I, AF.Relu, -1, 1)
+    ts(Q(12), I, 9, A.is_lt, -144, A.mult)
+    aff(Q(12), Q(11), 144, Q(12))
+    act(Q(19), I, AF.Relu, 1, -13)
+    aff(Q(12), Q(19), OUT, Q(12))
     aff(W("idm"), W("ix"), Q(11), Q(12))
-    iota(L("ab", 0, 10), [[16, 10]], 0)
-    aff(L("ab", 10, 10), L("ab", 0, 10), 1, I)
-    ts(L("ni", 10, 10), L("ab", 10, 10), -8.5, A.add, 1.0 / 18, A.mult)
-    ts(L("ab", 20, 10), L("ni", 10, 10), -18, A.mult, S, A.add)
-    tt(L("ni", 0, 10), L("ab", 10, 10), L("ab", 20, 10), A.add)
-    ts(L("ni", 20, 10), L("ni", 0, 10), 1, A.bitwise_and)
-    aff(Q(14), S, -32, 1)
-    ts(L("ab", 20, 10), L("ni", 0, 10), 16, A.mult, Q(14), A.add)
-    tt(L("ab", 20, 10), L("ab", 20, 10), L("ni", 10, 10), A.add)
-    ts(L("ab", 10, 10), L("ni", 20, 10), 304, A.mult)
-    tt(L("ab", 0, 10), L("ab", 10, 10), L("ab", 20, 10), A.add)
-    cast(W("pll"), L("ab", 0, 10))
+    iota(W("bi"), [[1, 16]], 0)
+    aff(Q(42), S, -304, 0)
+    act(Q(14), OD, AF.Abs, 304, Q(42))
+    aff(Q(14), S, -16, Q(14))
+    aff(Q(13), I, 16, Q(14))
+    aff(Q(14), OD, 16, Q(14))
+    ts(L("pll", 0, 8, 2), L("bi", 1, 8), Q(13), A.add)
+    ts(L("pll", 1, 8, 2), L("bi", 1, 8), Q(14), A.add, 256, A.add)
     iota(W("oi"), [[0, 2], [64, 5]], 9)
     aff(Q(15), K4, 16, K1)
     aff(Q(16), HI, 32, Q(15))
-    ts(Q(17), S, HI, A.not_equal, 304, A.mult)
+    act(Q(17), HI, AF.Abs, 304, Q(42))
     aff(Q(18), S, 16, Q(15))
     aff(Q(18), HI, 16, Q(18))
     ts(L("ol_", 0, 5), L("oi", 0, 5), Q(16), A.add)
     ts(L("ol_", 5, 5), L("oi", 5, 5), Q(18), A.add, Q(17), A.add)
-    iota(W("bi"), [[1, 16]], 0)
-    ts(W("bias"), L("bi", 1, 10), I, A.is_equal, LOW, A.mult)
-    iota(L("fh", 0, 64), [[1, 8], [0, 8]], 1)
-    iota(L("fh", 64, 16), [[12, 2], [1, 8]], 1)
-    iota(L("fh", 80, 64), [[0, 8], [1, 8]], 1)
-    iota(L("fh", 144, 16), [[0, 16]], 30)
-    aff(Q(20), I, 1, -1)
-    ts(W("e1"), W("fh"), I, A.is_equal, -UP, A.mult)
-    ts(W("e2"), W("fh"), Q(20), A.is_equal, UP, A.mult)
-    tt(L("e1", 0, 80), L("e1", 0, 80), L("e1", 80, 80), A.add)
-    tt(L("e2", 0, 80), L("e2", 0, 80), L("e2", 80, 80), A.add)
-    ts(Q(22), I, 14, A.is_equal, -UP, A.mult)
+    aff(Q(20), I, -1, 0)
+    same(L("ab", 0, 16), W("bi"), Q(20))
+    aff(W("bias"), L("ab", 1, 10), LOW, 0)
+    tt(L("ab", 16, 8), L("ab", 2, 8), L("ab", 1, 8), A.subtract)
+    aff(L("ab", 16, 8), L("ab", 16, 8), UP, 0)
+    aff(Q(22), L("ab", 14, 1), -UP, 0)
     aff(Q(22), Q(11), OUT, Q(22))
-    aff(L("e2", 0, 80), L("e2", 0, 80), 1, Q(22))
-    tt(W("dtab"), L("e1", 0, 80), L("e2", 0, 80), A.add)
+    aff(L("ab", 24, 8), L("ab", 16, 8), 1, Q(22))
+    for f in range(8):
+        aff(L("dtab", 8 * f, 8), L("ab", 24, 8), 1, L("ab", 16 + f, 1))
+    aff(L("dtab", 64, 8), L("ab", 24, 8))
+    iota(L("two8", 0, 160), [[0, 80], [8, 2]], 0)
+    iota(L("two8", 160, 160), [[0, 80], [-1, 2]], 0)
     iota(L("ji", 0, 10), [[32, 10]], -144)
     iota(L("ji", 10, 10), [[64, 5], [16, 2]], -144)
     aff(Q(23), S, 16, I)
@@ -275,6 +282,8 @@ def rank_program(g, core, T, topo):
     iota(L("two", 2, 18), [[0, 18]], 0)
     aff(Q(33), M, 2, 0)
     aff(Q(34), M, 2, 1)
+    aff(Q(44), M, -2, 0)
+    aff(Q(45), M, -2, -1)
     aff(Q(32), PAR, -1, 1)
     aff(Q(39), PAR, 80, Q(33))
     aff(Q(40), M, 160, 0)
@@ -289,19 +298,23 @@ def rank_program(g, core, T, topo):
     aff(L("ki", 12, 1), PAR, 146, L("nf", 27, 1))
     aff(L("ki", 14, 1), PAR, -146, L("nf", 26, 1))
     fill(L("ki", 13, 2, 2), 160)
-    ts(Q(25), I, 9, A.min, 8, A.mult)
-    aff(Q(41), Q(25), 2, 0)
+    act(Q(43), I, AF.Relu, -1, 9)
+    aff(Q(25), Q(43), -8, 72)
+    aff(Q(41), Q(43), -16, 144)
     ts(L("kl", 0, 6), L("ki", 0, 6), Q(25), A.add)
     ts(L("kl", 6, 10), L("ki", 6, 10), Q(41), A.add)
     aff(Q(26), S, 1, Q(33))
     aff(Q(26), I, 16, Q(26))
     ts(W("fl"), L("two", 0, 2), Q(26), A.add, 287, A.min)
-    ts(Q(27), MI, M, A.is_equal)
-    ts(Q(28), OD, 0, A.is_equal, Q(27), A.mult)
-    ts(Q(29), HI, S, A.is_equal, Q(27), A.mult)
+    aff(Q(27), M, -1, 0)
+    same(Q(27), MI, Q(27))
+    aff(Q(28), OD, -1, 1)
+    aff(Q(28), Q(28), Q(27), 0)
+    act(Q(29), Q(17), AF.Relu, -1, 1)
+    aff(Q(29), Q(29), Q(27), 0)
     aff(Q(30), HI, 16, -16)
-    ts(Q(31), S, OD, A.not_equal, 16, A.mult)
-    aff(Q(31), Q(31), 1, -16)
+    act(Q(31), OD, AF.Abs, 304, Q(42))
+    aff(Q(31), Q(31), 16.0 / 304, -16)
     for c in range(2):
         aff(L("nf", 5 * c, 5), L("ji", 0, 5), 1, Q(30 + c))
         aff(L("nf", 5 * c, 5), L("nf", 5 * c, 5), Q(28 + c), 160)
@@ -311,13 +324,13 @@ def rank_program(g, core, T, topo):
         aff(L("oi", 5 * c, 5), L("nf", 5 - 5 * c, 5), Q(32), 0)
     tt(L("nf", 10, 10), L("nf", 10, 10), W("oi"), A.add)
     cast(L("ar", 0, 10), L("nf", 10, 10))
-    aff(Q(35), I, 1, 1)
-    ts(L("dq", 16, 16), W("bi"), I, A.is_equal, OUT, A.mult)
-    ts(L("dq", 32, 16), W("bi"), Q(35), A.is_equal, UP, A.mult)
+    aff(L("dq", 16, 16), L("ab", 0, 16), OUT, 0)
+    fill(L("dq", 32, 1), 0)
+    aff(L("dq", 33, 15), L("ab", 0, 15), UP, 0)
     tt(L("dq", 0, 16), L("dq", 16, 16), L("dq", 32, 16), A.add)
     ts(W("il"), L("two", 2, 18), I, A.add)
     aff(W("dg"), L("dq", 0, 16), idx=W("il"))
-    ts(Q(36), I, 15, A.is_lt, -UP, A.mult)
+    aff(Q(36), L("ab", 15, 1), UP, -UP)
     cast(W("pgu"), W("pgn"))
     aff(W("pall"), L("ix", 16, 288), idx=W("pgu"))
     fill(W("one"), 1)
@@ -330,7 +343,8 @@ def rank_program(g, core, T, topo):
     ts(L("lt", 0, 128, 4), W("io"), 0, A.is_equal)
     ts(L("lt", 2, 128, 4), W("io"), 16, A.is_equal)
     quant("l", 0, 128, "lt")
-    ts(Q(38), I, OD, A.subtract, 8, A.mult)
+    aff(Q(38), OD, -8, 0)
+    aff(Q(38), I, 8, Q(38))
     ts(W("ul"), L("two", 2, 10), Q(38), A.add)
     quant("u", 0, 128, "ut")
     ul = L("ul", 0, 9)
@@ -343,17 +357,20 @@ def rank_program(g, core, T, topo):
         for c0, n in HALF if t else ((0, 288),):
             quant(x, c0, n, x)
             for i in range(8 if t < 3 else 0):
-                mm(i, n, "r", 2 * i, x, c0)
-                aff(L("sw", 288 * i + c0, n), PS(i, 0, n), spread=True)
+                bank = (i + (8 if c0 else 0)) % (8 - STAY[t - 1] if t else 8)
+                mm(bank, n, "r", 2 * i, x, c0)
+                aff(L("sw", 288 * i + c0, n), PS(bank, 0, n), spread=True)
         if t == 3:
             return
         dst = T.cores[rank ^ STEP[t]]
-        send(dst, W("Cp%d" % t), W("C" + x), "ca%d" % t, "cb%d" % t, True, 5000.0 if t else 8000.0)
-        send(dst, W("Sp%d" % t), W("S" + x), "sa%d" % t, "sb%d" % t, False, 5000.0 if t else 8000.0)
+        send(dst, W("Cp%d" % t), W("C" + x), "ca%d" % t, "cb%d" % t, True, CODES + (0 if t else 1500))
+        send(dst, W("Sp%d" % t), W("S" + x), "sa%d" % t, "sb%d" % t, False, CODES + (0 if t else 1500))
         for b in range(4):
-            mm(7 if t == 2 and b == 3 else 1 + b, 288, "e", 128 * b, x)
-            if t < 2 or b < 3:
+            if b < 4 - STAY[t]:
+                mm(1 + b, 288, "e", 128 * b, x)
                 aff(W("f%d" % b), PS(1 + b, 0, 288))
+            else:
+                mm(4 + b, 288, "e", 128 * b, x)
 
     O = lambda name, lay, k: L(name, 80 * lay + k, 10, 8)
     run = lambda name, lo, slot, n=10: L(name, lo + slot, n, 16)
@@ -361,17 +378,14 @@ def rank_program(g, core, T, topo):
 
     def prepare(t):
         par = t % 2
-        first, second = L("o", par, 80, 2), L("o", par + 1, 80, 2)
-        tt(W("dd"), second, first, A.subtract)
+        sums(W("dd"), L("two8", 160, 160), L("o", par, 160))
+        sums(W("cp"), L("two8", 0, 160), L("o", par, 160))
         if par:
-            fill(L("dd", 3, 20, 4), 0)
-        aff(W("cp"), first, 8, 0)
-        tt(W("cp"), W("cp"), second, A.add)
-        if par:
-            aff(L("cp", 3, 10, 4), O("o", 0, 7), 1, 64)
-        for r, lo, u0, src, d, to in (("ra", 0, 0, 40, "da", (0,)), ("rb", 0, 20, 1, "db", (0,)),
-                                      ("ra", 160, 10, 42, "da", (160, 320, 480)[t // 2:]), ("rb", 160, 30, 3, "db", (160,)))[:4 - t // 2]:
-            cast(L("uc", u0, 10), L("cp", src, 10, 4))
+            fill(L("dd", 7, 20, 8), 0)
+            aff(L("cp", 7, 10, 8), O("o", 0, 7), 1, 64)
+        for r, lo, u0, src, d, to in (("ra", 0, 0, 81, "da", (0,)), ("rb", 0, 20, 3, "db", (0,)),
+                                      ("ra", 160, 10, 85, "da", (160, 320, 480)[t // 2:]), ("rb", 160, 30, 7, "db", (160,)))[:4 - t // 2]:
+            cast(L("uc", u0, 10), L("cp", src, 10, 8))
             aff(L(r, lo, 160), W("dtab"), idx=L("uc", u0, 10))
             for c in to:
                 turn(L(d, c, 160), L(r, lo, 160))
@@ -388,7 +402,7 @@ def rank_program(g, core, T, topo):
             scan(L("c0", 160 * w, 160), L("da", 0, 160), R(4 * w))
         tt(L("s3", 2, 10, 3), run("c0", 0, 15), O("o288", 0, 2 + par), A.add)
         tt(L("co", 0, 10), run("c0", 160, 15), run("c0", 0, 15), A.subtract)
-        aff(L("co", 10, 10), L("dd", 1, 10, 4), 288, 0)
+        aff(L("co", 10, 10), L("dd", 3, 10, 8), 288, 0)
         if t < 2:
             tt(L("co", 20, 10), R(4, 0), R(0, 0), A.subtract)
 
@@ -432,17 +446,18 @@ def rank_program(g, core, T, topo):
     turn(L("tw", 0, 288), L("tab", 2304, 288))
     turn(L("tw", 288, 320), L("tab", 2288, 320))
     iota(L("tab", 2592, 288), [[1, 288]], -144)
-    ts(W("pl"), W("tw"), 144, A.add, idx=L("pll", 0, 9))
+    for h in range(2):
+        ts(L("pl", 128 * h, 128), W("tw"), 144, A.add, idx=L("pll", 8 * h, 8))
     aff(L("o", 0, 160), W("tw"), idx=W("ol_"))
     for r in range(8):
-        aff(L("tab", 288 * r, 288), L("tab", 2304, 288), 1, L("bias", r, 1), idx=L("pl", 18 * r, 18))
+        aff(L("tab", 288 * r, 288), L("tab", 2304, 288), 1, L("bias", r, 1), idx=L("pl", 32 * r, 18))
     aff(W("o288"), W("o"), 288, 144)
     prepare(0)
     bases(0, 0)
     cast(W("u1"), L("s3", 2, 10, 3))
-    look(1, 6, L("db", 0, 160))
+    look(1, 0, L("db", 0, 160))
     ts(W("u2"), run("c1", 0, 15), SHIFT, A.add)
-    look(2, 6)
+    look(2, 0)
     cast(R(0, 14), run("c0", 0, 15))
     rest(0, 6, True)
     score_lists(0)
@@ -463,7 +478,7 @@ def rank_program(g, core, T, topo):
             tt(L("s3", m, 10, 3), PS(0, m, 10, 4), L("co", 10 * m, 10), A.mult)
         sums(W("s3o"), W("k3"), W("s3"))
         cast(W("u1"), L("s3o", 2, 10, 3))
-        tt(W("mm"), PS(0, 0, 80), W("dd"), A.mult)
+        tt(W("mm"), PS(0, 0, 80), L("dd", 1, 80, 2), A.mult)
         if t < 2:
             tt(L("bw", 0, 10), PS(0, 0, 10, 4), L("co", 20, 10), A.mult)
         for lay in range(2):
@@ -479,18 +494,19 @@ def rank_program(g, core, T, topo):
         for k in (4 + par, 5 + par) + (0,) * par:
             fill(O("bt", 0, k), 288 * 9 + 144 - SHIFT)
         for e in range(2):
-            ts(L("oh", 80 * e, 80), L("o", 0, 80), Q(33 + e), A.is_equal)
+            same(L("oh", 80 * e, 80), L("o", 0, 80), Q(44 + e))
             tt(L("pr", 80 * e, 72), L("oh", 80 * e, 72), L("st", 0, 72), A.mult)
             tt(L("pr", 160 + 80 * e, 72), L("oh", 80 * e, 72), L("bt", 0, 72), A.mult)
         for c in range(2):
             sums(L("ss", 160 * c, 160), W("keep8"), L("pr", 160 * c, 160))
             aff(run("da", 320, 14 + c, 20), L("ss", 160 * c + 7, 20, 8))
-        ts(run("da", 320, 13, 20), L("ss", 7, 20, 8), -200, A.is_gt, OUT, A.mult)
-        ts(W("aa"), L("ss", 7, 20, 8), -2000, A.is_lt, -OUT, A.mult)
-        tt(run("da", 320, 1, 20), run("da", 320, 1, 20), W("aa"), A.add)
-        look(1, 6, L("db", 0, 160))
+        act(L("aa", 20, 20), L("ss", 7, 20, 8), AF.Sign, 1, 200)
+        aff(run("da", 320, 13, 20), L("aa", 20, 20), OUT // 2, OUT // 2)
+        aff(L("aa", 0, 20), L("oh", 4 + par, 20, 8), -OUT, 0)
+        tt(run("da", 320, 1, 20), run("da", 320, 1, 20), L("aa", 0, 20), A.add)
+        look(1, 0, L("db", 0, 160))
         ts(W("u2"), run("c1", 0, 15), SHIFT, A.add)
-        look(2, 6)
+        look(2, 0)
         for e in range(2):
             scan(L("cf", 160 * e, 144), L("da", 320 + 160 * e, 144), L("cw", 480, 144))
             ts(L("uf", e, 9, 2), run("cf", 160 * e, 15, 9), SHIFT, A.add)
@@ -503,8 +519,8 @@ def rank_program(g, core, T, topo):
         scan(W("cb"), W("dg"), W("gb"))
         ts(W(bl), run("cb", 0, 15, 18), Q(36), A.add, 144, A.add)
         for b in range(4):
-            mm(5 + b % 2, 288, "e", 128 * b, "p%d" % t)
-            aff(W("d%d" % b), PS(5 + b % 2, 0, 288))
+            mm(2 + b, 288, "e", 128 * b, "p%d" % t)
+            aff(W("d%d" % b), PS(2 + b, 0, 288))
         if t < 2:
             tt(R(0, 0), L("bw", 0, 10), R(0, 0), A.add)
             aff(R(0, 14), O("st", 0, 2 + par))
@@ -513,7 +529,8 @@ def rank_program(g, core, T, topo):
             score_lists(t + 1)
             prepare(t + 1)
         else:
-            turn(W("ot"), L("o", 0, 96))
+            aff(L("o288", 0, 96), L("o", 0, 96))
+            turn(W("ot"), L("o288", 0, 96))
             dmas([("y", T.ol[:, 32 * c:32 * c + 32], T.ot[8 * (c % 4):8 * (c % 4) + 8, 32 * (c // 4):32 * (c // 4) + 32], [W("ot")], [])
                   for c in range(9)])
         z, x = "z%d" % t, "x%d" % (t + 1)
@@ -522,17 +539,17 @@ def rank_program(g, core, T, topo):
                 aff(L(z, 4 * c0 + b, n, 4), W("d%d" % b), idx=L(ll, c0 // 16, n // 16))
             quant(z, c0, n, z)
             for b in range(4):
-                bank = (1 + b, (5, 6, 0, 1)[b])[h]
+                bank = (1 + b, (5, 0, 1, 2)[b])[h]
                 mm(bank, n, "w", 128 * b, z, c0)
                 aff(L("r%d" % b, c0, n), PS(bank, 0, n), 0.03125)
         for c0, n in HALF:
             i = L(bl, c0 // 16, n // 16)
             for b in range(4):
-                if t < 2 or b < 3:
+                if b < 4 - STAY[t]:
                     tt(L(x, 4 * c0 + b, n, 4), W("r%d" % b), L("f%d" % b, c0, n), A.add, idx=i)
                 else:
-                    aff(L("r4", c0, n), W("r3"), idx=i)
-                    tt(L(x, 4 * c0 + 3, n, 4), PS(7, c0, n), L("r4", c0, n), A.add)
+                    aff(L("r4", 288 * (3 - b) + c0, n), W("r%d" % b), idx=i)
+                    tt(L(x, 4 * c0 + b, n, 4), PS(4 + b, c0, n), L("r4", 288 * (3 - b) + c0, n), A.add)
         products(t + 1)
 
     for h, (c0, n) in enumerate(HALF):
@@ -544,7 +561,7 @@ def rank_program(g, core, T, topo):
 
     if not ORDER:
         N = len(ops)
-        nxt, prio = [[] for _ in ops], [0.0] * N
+        nxt, prio, favour = [[] for _ in ops], [0.0] * N, [FAVOUR] * N
         for i, o in enumerate(ops):
             for m in o["wait"]:
                 nxt[m].append(i)
@@ -571,7 +588,7 @@ def rank_program(g, core, T, topo):
                             if a >= at + dur:
                                 break
                             at = b
-                    if best is None or at + dur + (FAVOUR if q == "v" else 0.0) < best[0] + best[1]:
+                    if best is None or at + dur + (favour[i] if q == "v" else 0.0) < best[0] + best[1] - (2 * favour[i] if best[3] == "g" else 0.0):
                         best = (at, dur, lat, q, n)
                 at, dur, lat, q, n = best
                 if q:
@@ -588,12 +605,68 @@ def rank_program(g, core, T, topo):
 
         pre = [sorted(o["wait"]) for o in ops]
         key, on, kept = [-p for p in prio], {i: o["q"] for i, o in enumerate(ops)}, None
-        for _ in range(8):
+        dice = numpy.random.RandomState(1)
+
+        def lasts(order, on):
+            both, tight = 0.0, []
+            for wake, slow, each, way in CASES:
+                free, done, why, last = {}, [0.0] * N, [None] * N, {}
+                for i in order:
+                    o, q = ops[i], on[i]
+                    at, why[i] = max([(0.0, -1)] + [(done[m] + wake, m) for m in pre[i]])
+                    if q is None:
+                        done[i] = at - wake
+                        continue
+                    if free.get(q, 0.0) > at:
+                        why[i] = -2 - last[q]
+                    last[q] = i
+                    at, dur = max(at, free.get(q, 0.0)), o["dur"][q] if o["q"] == "f" else o["dur"]
+                    if o["lat"]:
+                        free[q], done[i] = at + dur, at + (way if o["lat"] == LIST else o["lat"])
+                    else:
+                        free[q] = done[i] = at + dur * slow + each
+                both += max(done)
+                i = done.index(max(done))
+                while i != -1:
+                    if why[i] < -1:
+                        tight.append((i, -2 - why[i]))
+                    i = why[i] if why[i] >= -1 else -2 - why[i]
+            return both, tight
+
+        for n in range(TRIES):
             start, end, on = place(key, pre, nxt, on, False)
-            if kept is None or max(end) < max(kept[1]):
-                kept = (start, end, on)
-            key = [-e for e in place([-e for e in end], nxt, pre, on, True)[1]]
-        ORDER.extend((i, kept[2][i]) for i in sorted(range(N), key=lambda i: (kept[0][i], i)))
+            took = lasts(sorted(range(N), key=lambda i: (start[i], i)), on)[0]
+            if kept is None or took <= kept[4]:
+                kept = (start, end, on, list(favour), took)
+                base = key = [-e for e in place([-e for e in end], nxt, pre, on, True)[1]]
+                if n % 2:
+                    continue
+            lo = float(dice.rand()) * max(kept[1])
+            shake, other = dice.normal(0.0, float(dice.choice((60.0, 200.0, 500.0))), N), dice.choice((-100.0, 0.0, 100.0, 300.0), N)
+            near = [lo <= s < lo + 2500.0 for s in kept[0]]
+            key = [k + float(shake[i]) if near[i] else k for i, k in enumerate(base)]
+            favour[:] = [float(other[i]) if near[i] and abs(shake[i]) < 50.0 else f for i, f in enumerate(kept[3])]
+        order, on = sorted(range(N), key=lambda i: (kept[0][i], i)), kept[2]
+        took, tight = lasts(order, on)
+        for n in range(POLISH):
+            i, k = tight[dice.randint(len(tight))]
+            new, to = list(order), dict(on)
+            how, a, b = dice.randint(3), order.index(k), order.index(i)
+            if how == 0 and ops[k]["q"] == "f":
+                to[k] = sorted(ops[k]["dur"])[dice.randint(len(ops[k]["dur"]))]
+            elif how == 1:
+                if any(order.index(m) > a for m in pre[i]):
+                    continue
+                new.insert(a, new.pop(b))
+            else:
+                b += dice.randint(4)
+                if any(order.index(m) <= b for m in nxt[k]):
+                    continue
+                new.insert(b, new.pop(a))
+            t2, w2 = lasts(new, to)
+            if t2 <= took:
+                order, on, took, tight = new, to, t2, w2
+        ORDER.extend((i, on[i]) for i in order)
         INFO.update(ops=ops, start=kept[0], done=kept[1], on=kept[2])
 
     known, total, waited, snap, token = {q: {} for q in queue}, {}, {}, {}, {}

@@ -6,21 +6,19 @@ STEP = (4, 1, 2)
 HALF = ((0, 160), (160, 128))
 STAY = (1, 1, 1)
 UP, LOW, OUT = 1024, -768, -4096
-SHIFT = 1600
 
-BF, F32, I32, U16, F16 = "bfloat16", "float32", "int32", "uint16", "float16"
+BF, F32, I32, U16 = "bfloat16", "float32", "int32", "uint16"
 SCRATCH, PLACE = {}, {}
 for _d, _names in (
-        (BF, "one 520 et 520 lt 512 ut 512 vt 512 tab 2880 tw 608 ix 320 idm 320 dtab 72 pall 288 ra 320 rb 320 da 640 db 320 dg 288 "
-             "g0 320 g1 160 g2 160 g3 160 cw 1120 gf 288 tf 288 gl 320 gb 288 rr 160 rt 176 o 168 dd 160 cp 160 "
-             "two8 320 xb 512 oh 160 bt 88 st 80 pr 320 ss 320 keep8 160 dq 48 aa 40 f0 288 f1 288 f2 288 f3 288 d0 288 d1 288 "
-             "d2 288 d3 288 x0 1152 x1 1152 x2 1152 x3 1152 z0 1152 z1 1152 z2 1152"),
-        (F32, "pf 48 bias 10 o288 168 mm 80 j0 10 j1 10 bw 20 co 30 s3 30 k3 30 s3o 30 sg 32 sa 32 "
-              "sw 2304 eb 160 ot 96 yt 288 r0 288 r1 288 r2 288 r3 288 r4 576 ab 32 nf 30 ki 16 oi 10 ji 20 bi 16 wli 20 two 20"),
-        (I32, "pi 10 io 128 raw 288 pgn 18 ni 30"),
-        (U16, "wl 20 pl 256 pll 16 ol_ 10 ul 10 pgu 18 kl 16 ar 20 fl 2 il 18 uc 40 ub 20 u1 10 u2 10 u3 10 uf 18 ut_ 32 so 32 "
-              "al0 32 al1 32 al2 32 bl0 18 bl1 18 bl2 18 ll0 18 ll1 18 ll2 18"),
-        (F16, "c0 320 c1 160 c2 160 c3 160 cf 320 cb 288")):
+        (BF, "one 520 et 520 ut 512 vt 512 tab 2608 tw 608 ix 320 idm 320 dtab 72 pall 288 ra 384 da 384 dg 288 "
+             "g0 192 g1 96 g2 96 g3 96 g4 384 cw 1056 gb 288 rr 224 rt 432 o 80 cp 64 two8 64 keep8 256 dq 48 mk 256 fin 256 "
+             "f0 288 f1 288 f2 288 f3 288 d0 288 d1 288 d2 288 d3 288 x0 1152 x1 1152 x2 1152 x3 1152 z0 1152 z1 1152 z2 1152"),
+        (F32, "pf 64 bias 10 o288 80 mm 48 j0 6 bw 16 co 104 cf 48 s3 48 k4 48 s3o 48 sg 32 sa 32 cs 864 gc 4 ou 32 "
+              "sw 2304 eb 192 ot 32 yt 288 r0 288 r1 288 r2 288 r3 288 r4 576 ab 40 nf 16 bi 16 wli 20 col 32"),
+        (I32, "pi 14 raw 288 pgn 18 ni 2"),
+        (U16, "wl 20 pl 256 pll 16 ol_ 4 ul 10 pgu 18 il 18 uc 32 ub 16 ue 32 u1 16 u2 16 u3 16 so 32 lb 8 lm 4 lc 4 lo 4 la 6 lk 6 lf 2 "
+              "lu 2 ld 2 ls 4 lz 2 al0 32 al1 32 al2 32 bl0 18 bl1 18 bl2 18 ll0 18 ll1 18 ll2 18"),
+        ("float16", "cb 288")):
     _w = _names.split()
     for _n, _c in zip(_w[0::2], _w[1::2]):
         if _d != BF and _n[:2] not in ("ra", "pg", "ll", "al", "sw", "eb", "ot", "yt", "r0", "r1", "r2", "r3", "r4"):
@@ -29,7 +27,7 @@ for _d, _names in (
             PLACE[_n] = ("all" + _d, _at, int(_c))
         else:
             SCRATCH[_n] = ("sbuf", [128, int(_c)], _d)
-for _n, _c in (("e", 512), ("l", 128), ("u", 128), ("r", 144), ("v", 128), ("w", 512), ("b", 128)) + tuple(
+for _n, _c in (("e", 512), ("u", 128), ("r", 144), ("v", 128), ("w", 512)) + tuple(
         (_m, 288) for _m in ("x0", "x1", "x2", "x3", "p0", "p1", "p2", "z0", "z1", "z2")):
     SCRATCH["C" + _n], SCRATCH["S" + _n] = ("sbuf", [128, _c], "float8_e4m3fn_x4"), ("sbuf", [128, _c], "uint8")
 SCRATCH["ps"] = ("psum", [128, 4096], F32)
@@ -37,10 +35,10 @@ SEMAPHORES = ["vq_", "sq_", "tq_", "gq_"] + ["dm%d" % i for i in range(20)] + [
     n + str(t) for t in range(3) for n in ("ca", "cb", "sa", "sb", "la", "lb")]
 ORDER = []
 INFO = {}
-CASES = ((100.0, 1.0, 15.0, 3400.0), (130.0, 1.1, 0.0, 2300.0))
-POLISH = 9000
-TRIES = 500
-WAKE = 120.0
+CASES = ((150.0, 0.9, 0.0, 2700.0), (110.0, 1.05, 10.0, 3000.0))
+POLISH = 6000
+TRIES = 300
+WAKE = 140.0
 CODES, LIST, COLUMN = 6000.0, 2800.0, 0.75
 FAVOUR = 100.0
 
@@ -109,7 +107,7 @@ def rank_program(g, core, T, topo):
         n = size(out)
         if idx:
             return (50 if q == "v" else 65) + 1.6 * size(idx) * 16
-        two_byte = all(SCRATCH[v[0]][2] in (BF, F16, U16) for v in [out] + ins)
+        two_byte = all(SCRATCH[v[0]][2] in (BF, "float16", U16) for v in [out] + ins)
         psum = any(v[0] == "ps" for v in ins)
         return 1.04 * max(64, n * (2 if two and not psum else 0.5 if two_byte and q == "v" and not two else 1))
 
@@ -147,8 +145,8 @@ def rank_program(g, core, T, topo):
         o2 = (op0,) if op1 is None else (op0, op1)
         do("v", lambda: g.vector.tensor_scalar(ap(out), ap(a, idx), c[0], c[1], *o2), [a] + more(s1, s2, idx), [out], cost("v", out, [a], idx))
 
-    def cast(out, a):
-        do("v", lambda: g.vector.tensor_copy(ap(out), ap(a)), [a], [out], cost("v", out, [a], None))
+    def cast(out, a, idx=None):
+        do("v", lambda: g.vector.tensor_copy(ap(out), ap(a, idx)), [a] + more(idx), [out], cost("v", out, [a], idx))
 
     def scan(out, d0, d1, op0=A.add, op1=A.max):
         do("v", lambda: g.vector.tensor_tensor_scan(ap(out), ap(d0), ap(d1), 0.0, op0, op1), [d0, d1], [out], cost("v", out, [d0, d1], None))
@@ -176,7 +174,7 @@ def rank_program(g, core, T, topo):
         dur = {q: cost(q, out, [a], idx) for q in "vs"}
         if spread:
             calls["g"], dur["g"] = lambda: g.partition_broadcast(ap(out), ap(a[:5] + (1,)), 128), 180 + 4.2 * size(out)
-        elif plain and not idx and size(out) <= 80 and SCRATCH[out[0]][2] == SCRATCH[a[0]][2]:
+        elif plain and not idx and size(out) <= 80 and SCRATCH[out[0]][2] == SCRATCH[a[0]][2] and out[4:] == (0, 128):
             calls["g"] = lambda: g.affine_select(ap(out), ap(a), [[0, size(out)]], A.is_ge, 0.0, 0, 0)
             dur["g"] = 210 + 2.1 * size(out)
         rec("f", calls, [a] + more(scale, bias, idx), [out], dur, None)
@@ -214,138 +212,133 @@ def rank_program(g, core, T, topo):
     dmas([("y", T.pgn[:, :], T.pg[:, :], [], [W("pgn")])], 3500.0, [zero])
 
     P = lambda j: L("pi", j, 1)
-    Q = lambda j: L("pf", j, 1)
-    iota(P(0), [[0, 1]], 0, 1)
-    for j, (sh, bits) in enumerate(((0, 15), (4, 1), (3, 1), (5, 3), (1, 3), (0, 1), (2, 1), (0, 3), (5, 1))):
-        ts(P(1 + j), P(0), sh, A.arith_shift_right, bits, A.bitwise_and)
-    cast(L("pf", 1, 2), L("pi", 1, 2))
-    cast(L("pf", 3, 7), L("pi", 3, 7))
-    I, S, HI, M, MI, OD, K4, K1, PAR = [Q(j) for j in range(1, 10)]
+    nq = [13]
+
+    def Q():
+        nq[0] += 1
+        return L("pf", nq[0] - 1, 1)
+
+    def mix(first, *terms):
+        out = Q()
+        for a, k in terms:
+            aff(out, a, k, first)
+            first = out
+        return out
+
+    def listed(name, lo, n, steps, add, most=None, st=1):
+        if most is None:
+            ts(L(name, lo, n, st), steps, add, A.add)
+        else:
+            ts(L(name, lo, n, st), steps, add, A.add, most, A.min)
+
+    iota(L("pi", 0, 2), [[64, 2]], 0, 1)
+    for j, (sh, bits) in enumerate(((0, 15), (4, 1), (3, 1), (0, 1), (2, 1), (0, 3), (5, 3), (1, 1), (1, 3), (2, 3), (0, 7))):
+        ts(P(2 + j), P(0), sh, A.arith_shift_right, bits, A.bitwise_and)
+    ts(P(13), P(1), 5, A.arith_shift_right, 3, A.bitwise_and)
+    cast(L("pf", 1, 2), L("pi", 2, 2))
+    cast(L("pf", 3, 5), L("pi", 4, 5))
+    cast(L("pf", 8, 5), L("pi", 9, 5))
+    I, S, HI, B0, K4, K1, M, B1, MI, I4, I7, M2 = [L("pf", j, 1) for j in range(1, 13)]
     iota(L("wli", 1, 18), [[1, 18]], 0)
     iota(L("wli", 0, 2, 19), [[0, 2]], 0)
-    aff(Q(10), I, 18, 0)
-    ts(W("wl"), W("wli"), Q(10), A.add)
+    listed("wl", 0, 20, W("wli"), mix(0, (I, 18)))
     iota(W("ix"), [[1, 320]], -160)
-    act(Q(11), I, AF.Relu, -1, 1)
-    ts(Q(12), I, 9, A.is_lt, -144, A.mult)
-    aff(Q(12), Q(11), 144, Q(12))
-    act(Q(19), I, AF.Relu, 1, -13)
-    aff(Q(12), Q(19), OUT, Q(12))
-    aff(W("idm"), W("ix"), Q(11), Q(12))
+    top, lose, far = Q(), Q(), Q()
+    act(top, I, AF.Relu, -1, 1)
+    ts(lose, I, 9, A.is_lt, -144, A.mult)
+    act(far, I, AF.Relu, 1, -13)
+    aff(W("idm"), W("ix"), top, mix(lose, (top, 144), (far, OUT)))
     iota(W("bi"), [[1, 16]], 0)
-    aff(Q(42), S, -304, 0)
-    act(Q(14), OD, AF.Abs, 304, Q(42))
-    aff(Q(14), S, -16, Q(14))
-    aff(Q(13), I, 16, Q(14))
-    aff(Q(14), OD, 16, Q(14))
-    ts(L("pll", 0, 8, 2), L("bi", 1, 8), Q(13), A.add)
-    ts(L("pll", 1, 8, 2), L("bi", 1, 8), Q(14), A.add, 256, A.add)
-    iota(W("oi"), [[0, 2], [64, 5]], 9)
-    aff(Q(15), K4, 16, K1)
-    aff(Q(16), HI, 32, Q(15))
-    act(Q(17), HI, AF.Abs, 304, Q(42))
-    aff(Q(18), S, 16, Q(15))
-    aff(Q(18), HI, 16, Q(18))
-    ts(L("ol_", 0, 5), L("oi", 0, 5), Q(16), A.add)
-    ts(L("ol_", 5, 5), L("oi", 5, 5), Q(18), A.add, Q(17), A.add)
-    aff(Q(20), I, -1, 0)
-    same(L("ab", 0, 16), W("bi"), Q(20))
+    less, X0, X2, X3 = mix(0, (S, -1)), Q(), Q(), Q()
+    for x, b in ((X0, B0), (X3, HI), (X2, K4)):
+        act(x, b, AF.Abs, 1, less)
+    S16 = mix(0, (S, -16))
+    q = mix(S16, (X0, 304))
+    listed("pll", 0, 8, L("bi", 1, 8), mix(q, (I, 16)), st=2)
+    ts(L("pll", 1, 8, 2), L("bi", 1, 8), mix(q, (B0, 16)), A.add, 256, A.add)
+    SET, SET2 = Q(), Q()
+    ts(SET, M, 2, A.min)
+    ts(SET2, M2, 2, A.min)
+    iota(L("col", 0, 8), [[16, 8]], 0)
+    iota(L("col", 8, 8), [[128, 2], [2, 4]], 0)
+    iota(L("col", 16, 4), [[1, 2], [1, 2]], 0)
+    iota(L("col", 20, 4), [[96, 2], [82, 2]], 14)
+    ts(L("ol_", 0, 3), L("col", 0, 3, 2), mix(K1, (SET, 96), (HI, 16), (K4, 16), (X3, 304), (S, -16)), A.add, 9, A.add)
+    ts(W("j0"), L("col", 0, 6), mix(I, (SET, 96)), A.add, -144, A.add)
+    same(L("ab", 0, 16), W("bi"), mix(0, (I, -1)))
     aff(W("bias"), L("ab", 1, 10), LOW, 0)
     tt(L("ab", 16, 8), L("ab", 2, 8), L("ab", 1, 8), A.subtract)
     aff(L("ab", 16, 8), L("ab", 16, 8), UP, 0)
-    aff(Q(22), L("ab", 14, 1), -UP, 0)
-    aff(Q(22), Q(11), OUT, Q(22))
-    aff(L("ab", 24, 8), L("ab", 16, 8), 1, Q(22))
+    aff(L("ab", 24, 8), L("ab", 16, 8), 1, mix(0, (L("ab", 14, 1), -UP), (top, OUT)))
     for f in range(8):
         aff(L("dtab", 8 * f, 8), L("ab", 24, 8), 1, L("ab", 16 + f, 1))
     aff(L("dtab", 64, 8), L("ab", 24, 8))
-    iota(L("two8", 0, 160), [[0, 80], [8, 2]], 0)
-    iota(L("two8", 160, 160), [[0, 80], [-1, 2]], 0)
-    iota(L("ji", 0, 10), [[32, 10]], -144)
-    iota(L("ji", 10, 10), [[64, 5], [16, 2]], -144)
-    aff(Q(23), S, 16, I)
-    aff(Q(24), S, 32, I)
-    ts(W("j0"), L("ji", 0, 10), Q(23), A.add, 143, A.min)
-    ts(W("j1"), L("ji", 10, 10), Q(24), A.add, 143, A.min)
-    iota(W("keep8"), [[0, 20], [1, 8]], 0)
+    iota(W("two8"), [[0, 32], [8, 2]], 0)
+    iota(W("keep8"), [[0, 32], [1, 8]], 0)
     act(W("keep8"), W("keep8"), AF.Sign)
-    iota(W("k3"), [[0, 10], [1, 3]], 0)
-    act(W("k3"), W("k3"), AF.Sign)
-    fill(L("cw", 0, 160), 0)
-    fill(L("cw", 960, 160), 0)
-    for c in range(4):
-        fill(L("pr", 80 * c + 72, 8), 0)
-    fill(L("o", 160, 8), 0)
-    fill(L("rt", 160, 16), 0)
-    fill(W("xb"), 0)
-    iota(L("two", 0, 2), [[256, 2]], 1)
-    iota(L("two", 2, 18), [[0, 18]], 0)
-    aff(Q(33), M, 2, 0)
-    aff(Q(34), M, 2, 1)
-    aff(Q(44), M, -2, 0)
-    aff(Q(45), M, -2, -1)
-    aff(Q(32), PAR, -1, 1)
-    aff(Q(39), PAR, 80, Q(33))
-    aff(Q(40), M, 160, 0)
-    aff(L("ki", 0, 2), L("bi", 0, 2), 1, Q(39))
-    iota(L("nf", 20, 4), [[-1, 2], [1, 2]], 81)
-    aff(L("ki", 2, 4), L("nf", 20, 4), 1, Q(33))
-    iota(L("nf", 24, 6), [[146, 3], [14, 2]], 14)
-    aff(L("nf", 24, 6), L("nf", 24, 6), 1, Q(40))
-    aff(L("ki", 6, 2), L("nf", 26, 2))
-    for c, src, k in ((8, 27, PAR), (9, 29, Q(32)), (10, 24, Q(32)), (11, 26, PAR)):
-        aff(L("ki", c, 1), L("nf", src, 1), k, 0)
-    aff(L("ki", 12, 1), PAR, 146, L("nf", 27, 1))
-    aff(L("ki", 14, 1), PAR, -146, L("nf", 26, 1))
-    fill(L("ki", 13, 2, 2), 160)
-    act(Q(43), I, AF.Relu, -1, 9)
-    aff(Q(25), Q(43), -8, 72)
-    aff(Q(41), Q(43), -16, 144)
-    ts(L("kl", 0, 6), L("ki", 0, 6), Q(25), A.add)
-    ts(L("kl", 6, 10), L("ki", 6, 10), Q(41), A.add)
-    aff(Q(26), S, 1, Q(33))
-    aff(Q(26), I, 16, Q(26))
-    ts(W("fl"), L("two", 0, 2), Q(26), A.add, 287, A.min)
-    aff(Q(27), M, -1, 0)
-    same(Q(27), MI, Q(27))
-    aff(Q(28), OD, -1, 1)
-    aff(Q(28), Q(28), Q(27), 0)
-    act(Q(29), Q(17), AF.Relu, -1, 1)
-    aff(Q(29), Q(29), Q(27), 0)
-    aff(Q(30), HI, 16, -16)
-    act(Q(31), OD, AF.Abs, 304, Q(42))
-    aff(Q(31), Q(31), 16.0 / 304, -16)
-    for c in range(2):
-        aff(L("nf", 5 * c, 5), L("ji", 0, 5), 1, Q(30 + c))
-        aff(L("nf", 5 * c, 5), L("nf", 5 * c, 5), Q(28 + c), 160)
-    cast(L("ar", 10, 10), L("nf", 0, 10))
-    for c in range(2):
-        aff(L("nf", 10 + 5 * c, 5), L("nf", 5 * c, 5), PAR, 0)
-        aff(L("oi", 5 * c, 5), L("nf", 5 - 5 * c, 5), Q(32), 0)
-    tt(L("nf", 10, 10), L("nf", 10, 10), W("oi"), A.add)
-    cast(L("ar", 0, 10), L("nf", 10, 10))
+    fill(L("cw", 0, 288), 0)
+    fill(L("o", 48, 32), 0)
+    fill(L("rr", 0, 16), 0)
+    fill(L("rr", 208, 16), 0)
+    iota(L("rt", 192, 16), [[-1, 2], [0, 8]], 1)
+    fill(L("co", 32, 72), 0)
+    fill(L("bw", 12, 4), 0)
+    twice = mix(I, (B0, -1), (S, 1))
+    cast(L("ld", 0, 1), twice)
+    q = mix(15, (twice, 16))
+    ts(L("ls", 0, 1), q, 95, A.min)
+    ts(L("ls", 2, 1), q, -8, A.add, 183, A.min)
+    aff(L("nf", 0, 2), L("col", 0, 2), 1, I)
+    ts(L("nf", 2, 2), L("nf", 0, 2), -2.5, A.add, 1.0 / 6, A.mult)
+    cast(W("ni"), L("nf", 2, 2))
+    aff(L("nf", 2, 2), W("ni"), -6, 0)
+    tt(L("nf", 2, 2), L("nf", 2, 2), L("nf", 0, 2), A.add)
+    aff(L("nf", 4, 2), W("ni"), 2, mix(1, (S, 8), (B0, -8)))
+    aff(L("nf", 6, 2), L("nf", 2, 2), 8, 0)
+    tt(L("nf", 4, 2), L("nf", 4, 2), L("nf", 6, 2), A.add)
+    ts(W("lu"), L("nf", 4, 2), 63, A.min)
+    ts(L("nf", 8, 2), W("ni"), SET, A.is_equal, 2, A.mult)
+    ts(L("nf", 10, 2), W("ni"), SET2, A.is_equal, mix(5, (M, 64)), A.add)
+    tt(L("nf", 8, 2), L("nf", 8, 2), L("nf", 10, 2), A.add)
+    tt(L("nf", 8, 2), L("nf", 8, 2), L("nf", 6, 2), A.add)
+    cast(W("lf"), L("nf", 8, 2))
+    hot = L("ab", 32, 8)
+    ts(hot, L("bi", 0, 8), I7, A.is_equal)
+    H = lambda k: L("ab", 32 + k, 1)
+    aff(L("col", 24, 3), L("col", 0, 3), 4, 0)
+    listed("lb", 0, 3, L("col", 24, 3), mix(0, (B0, 32), (H(6), 16), (H(2), 1000), (H(7), 1000)), 192)
+    listed("lb", 4, 3, L("col", 24, 3), mix(1000, (H(4), -1000)), mix(192, (H(0), 8), (H(3), 8)))
+    listed("lm", 0, 2, L("col", 8, 2, 4), mix(S16, (HI, 64), (B0, 32), (K4, 16), (B1, 16), (X2, 224)), 431)
+    ts(L("lm", 2, 1), mix(S16, (MI, 64), (B0, 16), (X0, 224)), 431, A.min)
+    H2S = mix(S, (HI, 2))
+    listed("lc", 0, 3, L("col", 8, 3), mix(S, (I7, 8)))
+    q = mix(0, (I4, 16), (B0, 8))
+    listed("lo", 0, 4, L("col", 16, 4), mix(q, (S, 4), (B1, 2)))
+    q = mix(0, (q, 2), (S, 192), (B1, 96))
+    listed("la", 0, 4, L("col", 20, 4), q)
+    listed("la", 4, 2, L("col", 21, 2), q)
+    q = Q()
+    ts(q, I7, 5, A.min, 16, A.mult)
+    listed("lk", 0, 2, L("col", 16, 2), q, q)
+    ts(L("lk", 2, 2), L("lk", 0, 2), 14, A.add)
+    ts(L("lk", 4, 2), L("col", 8, 2, 2), mix(H2S, (q, 1)), A.add, 1, A.add)
+    aff(W("gc"), L("col", 8, 4), 1, S)
+    listed("lz", 0, 2, L("col", 0, 2, 2), mix(I, (HI, 8), (S, 8)))
     aff(L("dq", 16, 16), L("ab", 0, 16), OUT, 0)
     fill(L("dq", 32, 1), 0)
     aff(L("dq", 33, 15), L("ab", 0, 15), UP, 0)
     tt(L("dq", 0, 16), L("dq", 16, 16), L("dq", 32, 16), A.add)
-    ts(W("il"), L("two", 2, 18), I, A.add)
+    listed("il", 0, 18, L("wli", 1, 18), I, I)
     aff(W("dg"), L("dq", 0, 16), idx=W("il"))
-    aff(Q(36), L("ab", 15, 1), UP, -UP)
+    back = mix(144 - UP, (L("ab", 15, 1), UP))
     cast(W("pgu"), W("pgn"))
     aff(W("pall"), L("ix", 16, 288), idx=W("pgu"))
     fill(W("one"), 1)
     do("g", lambda: g.affine_select(ap(W("et")), ap(W("one")), [[-1, 520]], A.is_equal, 0.0, 3, 4), [W("one")], [W("et")], 200 + 2.1 * 520)
     for b in range(4):
         quant("e", 128 * b, 128, "et", 3 - b)
-    iota(W("io"), [[-1, 128]], 128, 1)
-    fill(W("lt"), 0)
-    ts(W("io"), W("io"), 31, A.bitwise_and)
-    ts(L("lt", 0, 128, 4), W("io"), 0, A.is_equal)
-    ts(L("lt", 2, 128, 4), W("io"), 16, A.is_equal)
-    quant("l", 0, 128, "lt")
-    aff(Q(38), OD, -8, 0)
-    aff(Q(38), I, 8, Q(38))
-    ts(W("ul"), L("two", 2, 10), Q(38), A.add)
+    q = mix(0, (B0, -8), (I, 8))
+    listed("ul", 0, 10, L("bi", 0, 10), q, q)
     quant("u", 0, 128, "ut")
     ul = L("ul", 0, 9)
     do("v", lambda: g.vector.tensor_copy(ap(W("Cr")).bitcast(dt.uint32), ap(W("Cu")).bitcast(dt.uint32).indirect(ap(ul))),
@@ -372,71 +365,75 @@ def rank_program(g, core, T, topo):
             else:
                 mm(4 + b, 288, "e", 128 * b, x)
 
-    O = lambda name, lay, k: L(name, 80 * lay + k, 10, 8)
-    run = lambda name, lo, slot, n=10: L(name, lo + slot, n, 16)
-    R = lambda n, slot=None: L("cw", 160 + 160 * n, 160) if slot is None else run("cw", 160 + 160 * n, slot)
+    O = lambda name, k: L(name, k, 6, 8)
+    run = lambda name, lo, n=6: L(name, lo, n, 16)
+    R = lambda n, slot=None: L("cw", 96 + 96 * n, 96) if slot is None else run("cw", 96 + 96 * n + slot)
+    SC = lambda n: L("cs", 480 + 96 * n, 96)
 
     def prepare(t):
-        par = t % 2
-        sums(W("dd"), L("two8", 160, 160), L("o", par, 160))
-        sums(W("cp"), L("two8", 0, 160), L("o", par, 160))
+        par, n = t % 2, 4 - t // 2
+        tt(L("co", 0, 32), L("o", par + 1, 32, 2), L("o", par, 32, 2), A.subtract)
+        sums(W("cp"), W("two8"), L("o", par, 64))
         if par:
-            fill(L("dd", 7, 20, 8), 0)
-            aff(L("cp", 7, 10, 8), O("o", 0, 7), 1, 64)
-        for r, lo, u0, src, d, to in (("ra", 0, 0, 81, "da", (0,)), ("rb", 0, 20, 3, "db", (0,)),
-                                      ("ra", 160, 10, 85, "da", (160, 320, 480)[t // 2:]), ("rb", 160, 30, 7, "db", (160,)))[:4 - t // 2]:
-            cast(L("uc", u0, 10), L("cp", src, 10, 8))
-            aff(L(r, lo, 160), W("dtab"), idx=L("uc", u0, 10))
-            for c in to:
-                turn(L(d, c, 160), L(r, lo, 160))
-        fill(W("st"), -UP)
-        fill(O("st", 0, 4 + par), OUT)
-        for k in range(2 + par):
-            aff(O("st", 0, k), R(0, 0) if par else W("j0"))
-        s0 = R(-1, 14) if par else W("j1")
+            fill(L("co", 3, 8, 4), 0)
+            aff(O("cp", 7), O("o", 7), 1, 64)
+            aff(R(-1, 14), R(0, 0))
+        cast(W("uc"), W("cp"), W("lu"))
+        for a, b in ((0, 1), (1, n)):
+            aff(L("ra", 96 * a, 96 * (b - a)), W("dtab"), idx=L("uc", 6 * a, 6 * (b - a)))
+            turn(L("da", 96 * a, 96 * (b - a)), L("ra", 96 * a, 96 * (b - a)))
         for w in range(2):
-            tt(L("bw", 10 * w, 10), s0, O("o288", 1, par + w), A.add)
-            cast(L("ub", 10 * w, 10), L("bw", 10 * w, 10))
-            pick(L("g0", 160 * w, 160), W("tab"), L("ub", 10 * w, 10), 6 if t + w == 0 else 0)
-            turn(R(4 * w), L("g0", 160 * w, 160))
-            scan(L("c0", 160 * w, 160), L("da", 0, 160), R(4 * w))
-        tt(L("s3", 2, 10, 3), run("c0", 0, 15), O("o288", 0, 2 + par), A.add)
-        tt(L("co", 0, 10), run("c0", 160, 15), run("c0", 0, 15), A.subtract)
-        aff(L("co", 10, 10), L("dd", 3, 10, 8), 288, 0)
-        if t < 2:
-            tt(L("co", 20, 10), R(4, 0), R(0, 0), A.subtract)
+            tt(L("bw", 6 * w, 6), R(-1, 14) if par else W("j0"), O("o288", par + w), A.add)
+        cast(W("ub"), W("bw"), L("ld", 0, 1))
+        for n in range(2):
+            aff(run("da", 15 + 96 * n), O("o288", 2 + 2 * n + par))
+        for w in range(2):
+            aff(L("g0", 96 * w, 96), W("tab"), idx=L("ub", 6 * w, 6))
+            turn(R(4 + w), L("g0", 96 * w, 96))
+            scan(L("cs", 96 * w, 96), L("da", 0, 96), R(4 + w))
+        K = lambda k: L("co", 32 + 8 * k, 6)
+        aff(K(2), L("co", 1, 6, 4), 288, 0)
+        aff(K(7), L("co", 2, 6, 4), 288, 0)
+        for w in range(2):
+            tt(run("cs", 96 * w + 7), run("cs", 96 * w + 15), K(2), A.add)
+        for v in range(2):
+            cast(L("ue", 16 * v, 16), L("cs", 8 - 8 * v, 184), L("ls", 2, 1))
+            for a, b in ((0, 2),) if t else ((0, 1), (1, 2)):
+                c, n = 192 * v + 96 * a, 96 * (b - a)
+                aff(L("g4", c, n), W("tab"), idx=L("ue", 16 * v + 6 * a, n // 16))
+                turn(L("cw", 672 + c, n), L("g4", c, n))
+            for w in range(2):
+                scan(L("cs", 192 + 192 * v + 96 * w, 96), L("da", 96, 96), R(6 + 2 * v + w))
+        X = lambda w, v: run("cs", 207 + 192 * v + 96 * w)
+        tt(K(0), R(5, 0), R(4, 0), A.subtract)
+        tt(K(1), run("cs", 111), run("cs", 15), A.subtract)
+        aff(K(3), run("cs", 15))
+        tt(K(5), X(1, 0), X(0, 0), A.subtract)
+        tt(K(6), X(0, 1), X(0, 0), A.subtract)
+        tt(K(4), X(1, 1), X(0, 1), A.subtract)
+        tt(K(4), K(4), K(5), A.subtract)
+        aff(K(8), X(0, 0))
+        aff(W("cf"), L("co", 40, 64), idx=L("lc", 0, 3))
 
-    def bases(par, t):
-        aff(run("db", 0, 15), O("o", 1, 4 + par), 288, 144 - SHIFT)
+    def base(par):
         if par:
-            fill(run("da", 160, 15), 288 * 8 + 144 - SHIFT)
-        elif t < 2:
-            aff(run("da", 160, 15), O("o", 0, 6), 288, 144 - SHIFT)
+            fill(run("da", 207), 288 * 8 + 144)
+        else:
+            aff(run("da", 207), O("o", 6), 288, 144)
 
-    def look(n, cut, d=None):
-        pick(W("g%d" % n), W("tab"), W("u%d" % n), cut)
+    def look(n, more_=True):
+        aff(W("g%d" % n), W("tab"), idx=L("u%d" % n, 0, 6))
         turn(R(n), W("g%d" % n))
-        if d:
-            scan(W("c%d" % n), d, R(n))
+        if more_:
+            scan(SC(n), L("da", 96 * n, 96), R(n))
+        if n == 2:
+            cast(W("u3"), SC(n), L("ls", 0, 1))
 
-    def rest(par, cut, last):
-        scan(W("c2"), L("da", 160, 160), R(2))
-        ts(W("u3"), run("c2", 0, 15), SHIFT, A.add)
-        look(3, cut, L("db", 160, 160) if last else None)
-        for n in (1, 2, 3) if last else (1, 2):
-            cast(R(n, 0 if par and n == 3 else 14), run("c%d" % n, 0, 14))
-
-    def score_lists(t):
-        if t:
-            ts(W("ut_"), W("cw"), 144 + 288 * 9, A.add, idx=L("kl", 10 + 2 * t, 2))
-            aff(L("gl", 0, 160), W("tab"), idx=L("ut_", 0, 10))
-            if t == 1:
-                aff(L("gl", 160, 160), W("tab"), idx=L("ut_", 16, 10))
-                turn(R(5), L("gl", 160, 160))
-            turn(R(-1), L("gl", 0, 160))
-            aff(R(-1, 14), R(5, 0))
-        aff(W("sg"), L("o288", 0, 168), idx=L("kl", 2 * t, 2))
-        tt(W("sa"), W("cw"), W("sg"), A.add, idx=L("kl", 6 + 2 * t, 2))
+    def score_lists(t, which):
+        for n in which:
+            aff(R(n, 0 if t == 2 and n == 3 else 14), run("cs", 494 + 96 * n))
+        aff(W("sg"), W("o288"), idx=L("lo", 2 * (t % 2), 2))
+        tt(W("sa"), W("cw"), W("sg"), A.add, idx=L("la", (4, 2, 0)[t], 2))
         cast(W("so"), W("sa"))
 
     products(0)
@@ -445,93 +442,70 @@ def rank_program(g, core, T, topo):
           ("y", T.vt[:, :], T.v[:, :], [], [W("vt")])], 5000.0, [rows])
     turn(L("tw", 0, 288), L("tab", 2304, 288))
     turn(L("tw", 288, 320), L("tab", 2288, 320))
-    iota(L("tab", 2592, 288), [[1, 288]], -144)
     for h in range(2):
         ts(L("pl", 128 * h, 128), W("tw"), 144, A.add, idx=L("pll", 8 * h, 8))
-    aff(L("o", 0, 160), W("tw"), idx=W("ol_"))
+    aff(L("o", 0, 48), W("tw"), idx=L("ol_", 0, 3))
     for r in range(8):
         aff(L("tab", 288 * r, 288), L("tab", 2304, 288), 1, L("bias", r, 1), idx=L("pl", 32 * r, 18))
     aff(W("o288"), W("o"), 288, 144)
     prepare(0)
-    bases(0, 0)
-    cast(W("u1"), L("s3", 2, 10, 3))
-    look(1, 0, L("db", 0, 160))
-    ts(W("u2"), run("c1", 0, 15), SHIFT, A.add)
-    look(2, 0)
-    cast(R(0, 14), run("c0", 0, 15))
-    rest(0, 6, True)
-    score_lists(0)
+    base(0)
+    cast(W("u2"), L("cs", 192, 96), L("ls", 0, 1))
+    for n, c in ((0, 0), (1, 192)):
+        aff(R(n, 0), R(4 + 2 * n, 0))
+        aff(R(n, 14), run("cs", c + 14))
+    for n in (2, 3):
+        look(n)
+    score_lists(0, (2, 3))
     quant("v", 0, 128, "vt")
 
     for t in range(3):
         dst, par = T.cores[rank ^ STEP[t]], t % 2
-        pick(W("eb"), W("sw"), L("so", 16, 10), 6)
-        tt(L("rr", 96, 64), W("sw"), L("eb", 96, 64), A.is_gt, idx=L("so", 6, 4))
-        tt(L("rr", 0, 96), W("sw"), L("eb", 0, 96), A.is_gt, idx=L("so", 0, 6))
-        turn(L("rt", 0, 160), W("rr"))
-        ar = 10 if t else 0
-        aff(L("xb", 0, 96, 2), W("rt"), idx=L("ar", ar, 6))
-        aff(L("xb", 192, 64, 2), W("rt"), idx=L("ar", ar + 6, 4))
-        quant("b", 0, 128, "xb")
-        mm(0, 128, "l", 0, "b")
-        for m in range(2):
-            tt(L("s3", m, 10, 3), PS(0, m, 10, 4), L("co", 10 * m, 10), A.mult)
-        sums(W("s3o"), W("k3"), W("s3"))
-        cast(W("u1"), L("s3o", 2, 10, 3))
-        tt(W("mm"), PS(0, 0, 80), L("dd", 1, 80, 2), A.mult)
-        if t < 2:
-            tt(L("bw", 0, 10), PS(0, 0, 10, 4), L("co", 20, 10), A.mult)
-        for lay in range(2):
-            first, second, d = L("o", 80 * lay + par, 40, 2), L("o", 80 * lay + par + 1, 40, 2), L("mm", 40 * lay, 40)
-            tt(first, first, d, A.add)
-            if t < 2 or not lay:
-                tt(second, second, d, A.subtract)
-        bases(par, t)
-        tt(O("st", 0, 2 + par), L("s3", 0, 10, 3), run("c0", 0, 15), A.add)
-        aff(O("st", 0, 3 + par), O("st", 0, 2 + par))
-        fill(L("bt", par, 40, 2), 288 * 8 + 144 - SHIFT)
-        aff(L("bt", par + 1, 40, 2), L("o", par, 40, 2), 288, 144 - SHIFT)
-        for k in (4 + par, 5 + par) + (0,) * par:
-            fill(O("bt", 0, k), 288 * 9 + 144 - SHIFT)
-        for e in range(2):
-            same(L("oh", 80 * e, 80), L("o", 0, 80), Q(44 + e))
-            tt(L("pr", 80 * e, 72), L("oh", 80 * e, 72), L("st", 0, 72), A.mult)
-            tt(L("pr", 160 + 80 * e, 72), L("oh", 80 * e, 72), L("bt", 0, 72), A.mult)
-        for c in range(2):
-            sums(L("ss", 160 * c, 160), W("keep8"), L("pr", 160 * c, 160))
-            aff(run("da", 320, 14 + c, 20), L("ss", 160 * c + 7, 20, 8))
-        act(L("aa", 20, 20), L("ss", 7, 20, 8), AF.Sign, 1, 200)
-        aff(run("da", 320, 13, 20), L("aa", 20, 20), OUT // 2, OUT // 2)
-        aff(L("aa", 0, 20), L("oh", 4 + par, 20, 8), -OUT, 0)
-        tt(run("da", 320, 1, 20), run("da", 320, 1, 20), L("aa", 0, 20), A.add)
-        look(1, 0, L("db", 0, 160))
-        ts(W("u2"), run("c1", 0, 15), SHIFT, A.add)
-        look(2, 0)
-        for e in range(2):
-            scan(L("cf", 160 * e, 144), L("da", 320 + 160 * e, 144), L("cw", 480, 144))
-            ts(L("uf", e, 9, 2), run("cf", 160 * e, 15, 9), SHIFT, A.add)
-        pick(W("gf"), W("tab"), W("uf"), 10)
-        turn(W("tf"), W("gf"))
+        pick(W("eb"), W("sw"), L("so", 16, 12), 6)
+        for h in range(2):
+            tt(L("rr", 16 + 96 * h, 96), W("sw"), L("eb", 96 * h, 96), A.is_gt, idx=L("so", 6 * h, 6))
+        turn(L("rt", 0, 192), L("rr", 16, 192))
+        tt(W("s3"), L("rt", 0, 208), W("cf"), A.mult, idx=L("lb", 0, 3))
+        aff(W("k4"), L("rt", 0, 208), idx=L("lb", 4, 3))
+        sums(W("s3o"), W("k4"), W("s3"))
+        cast(L("u2", 0, 6), L("s3o", 7, 6, 8))
+        cast(L("u1", 0, 6), L("s3o", 2, 6, 8))
+        turn(L("rt", 208, 224), W("rr"))
+        tt(W("mm"), W("rt"), L("co", 0, 48), A.mult, idx=L("lm", 0, 3))
+        first, second = L("o", par, 32, 2), L("o", par + 1, 32, 2)
+        tt(first, first, L("mm", 0, 32), A.add)
+        base(par)
+        tt(second, second, L("mm", 0, 32), A.subtract)
+        tt(R(0, 0), L("mm", 32, 6), R(4, 0), A.add)
+        tt(R(0, 14), L("mm", 40, 6), run("cs", 14), A.add)
+        for c in range(4):
+            ts(L("mk", 64 * c, 64), L("o", 0, 64), L("gc", c, 1), A.is_equal)
+        for k in range(8):
+            n, e = (k + 2 - par) // 2 - 1, (k + par) % 2
+            if n > 0 and not e:
+                look(n, n < 3 or par)
+            which = 2 if k == 7 or (n > 0 and e) else e
+            tt(L("mk", k, 32, 8), R(n), L("mk", k, 32, 8), A.mult, idx=L("lk", 2 * which, 2))
+        sums(W("fin"), W("keep8"), W("mk"))
+        for to, of, n, slot in ((64, 0, 64, 6), (0, 64, 64, 6), (0, 32, 32, 5), (32, 0, 32, 5), (64, 32, 32, 5), (96, 0, 32, 5)):
+            aff(L("fin", slot, 32, 8, to, to + n), L("fin", 7, 32, 8, of, of + n))
         al, bl, ll = "al%d" % t, "bl%d" % t, "ll%d" % t
-        ts(W(al), W("tf"), 144, A.add, idx=W("fl"))
+        ts(W(al), W("fin"), 144, A.add, idx=W("lf"))
         send(dst, W(ll), L(al, 0, 18), "la%d" % t, "lb%d" % t)
         aff(W("gb"), W("pall"), idx=L(al, 0, 18))
         scan(W("cb"), W("dg"), W("gb"))
-        ts(W(bl), run("cb", 0, 15, 18), Q(36), A.add, 144, A.add)
+        ts(W(bl), run("cb", 15, 18), back, A.add)
         for b in range(4):
             mm(2 + b, 288, "e", 128 * b, "p%d" % t)
             aff(W("d%d" % b), PS(2 + b, 0, 288))
         if t < 2:
-            tt(R(0, 0), L("bw", 0, 10), R(0, 0), A.add)
-            aff(R(0, 14), O("st", 0, 2 + par))
             aff(W("o288"), W("o"), 288, 144)
-            rest(par, 0, t == 1)
-            score_lists(t + 1)
+            score_lists(t + 1, (1, 2, 3) if t else (1, 2))
             prepare(t + 1)
         else:
-            aff(L("o288", 0, 96), L("o", 0, 96))
-            turn(W("ot"), L("o288", 0, 96))
-            dmas([("y", T.ol[:, 32 * c:32 * c + 32], T.ot[8 * (c % 4):8 * (c % 4) + 8, 32 * (c // 4):32 * (c // 4) + 32], [W("ot")], [])
+            aff(W("ou"), L("o", 0, 64), idx=W("lz"))
+            turn(W("ot"), W("ou"))
+            dmas([("y", T.ol[:, 32 * c:32 * c + 32], T.ot[32 * (c // 3) + 8 * (c % 3):32 * (c // 3) + 8 * (c % 3) + 8, :], [W("ot")], [])
                   for c in range(9)])
         z, x = "z%d" % t, "x%d" % (t + 1)
         for h, (c0, n) in enumerate(HALF):
@@ -648,26 +622,29 @@ def rank_program(g, core, T, topo):
             favour[:] = [float(other[i]) if near[i] and abs(shake[i]) < 50.0 else f for i, f in enumerate(kept[3])]
         order, on = sorted(range(N), key=lambda i: (kept[0][i], i)), kept[2]
         took, tight = lasts(order, on)
+        where = {m: n for n, m in enumerate(order)}
         for n in range(POLISH):
             i, k = tight[dice.randint(len(tight))]
-            new, to = list(order), dict(on)
-            how, a, b = dice.randint(3), order.index(k), order.index(i)
+            new, to = list(order), on
+            how, a, b = dice.randint(3), where[k], where[i]
             if how == 0 and ops[k]["q"] == "f":
+                to = dict(on)
                 to[k] = sorted(ops[k]["dur"])[dice.randint(len(ops[k]["dur"]))]
             elif how == 1:
-                if any(order.index(m) > a for m in pre[i]):
+                if any(where[m] > a for m in pre[i]):
                     continue
                 new.insert(a, new.pop(b))
             else:
                 b += dice.randint(4)
-                if any(order.index(m) <= b for m in nxt[k]):
+                if any(where[m] <= b for m in nxt[k]):
                     continue
                 new.insert(b, new.pop(a))
             t2, w2 = lasts(new, to)
             if t2 <= took:
                 order, on, took, tight = new, to, t2, w2
+                where = {m: n for n, m in enumerate(order)}
         ORDER.extend((i, on[i]) for i in order)
-        INFO.update(ops=ops, start=kept[0], done=kept[1], on=kept[2])
+        INFO.update(ops=ops, start=kept[0], done=kept[1], on=kept[2], took=took)
 
     known, total, waited, snap, token = {q: {} for q in queue}, {}, {}, {}, {}
     for i, q in ORDER:

@@ -4,21 +4,23 @@ from concourse.mybir import dt, AluOpType, ActivationFunctionType
 
 STEP = (4, 1, 2)
 HALF = ((0, 160), (160, 128))
-STAY = (1, 1, 1)
+RUNS = HALF
+LAST, YW, OW, REDO, RAW, FREE, CUT, TWO = 4, 1, 1, 1, 4, 0, 4, 1
+CUT0, ENDS = 0, 0
+STAY = (1, 1, 2)
 UP, LOW, OUT = 1024, -768, -4096
 
 BF, F32, I32, U16 = "bfloat16", "float32", "int32", "uint16"
 SCRATCH, PLACE = {}, {}
 for _d, _names in (
-        (BF, "one 520 et 520 ut 512 vt 512 tab 2608 tw 608 ix 320 idm 320 dtab 72 pall 288 ra 384 da 384 dg 288 "
-             "g0 192 g1 96 g2 96 g3 96 g4 384 cw 1056 gb 288 rr 224 rt 432 o 80 cp 64 two8 64 keep8 256 dq 48 mk 256 fin 256 "
+        (BF, "one 520 et 520 ut 512 vt 512 tab 2608 tw 608 idm 320 dtab 72 ra 384 da0 384 da1 384 tb 816 "
+             "g0 192 g1 96 g2 96 g3 96 g4 384 cw 1216 gb 320 rr 224 rt 464 o 96 cp 64 two8 64 anew 256 mk 256 fin 256 "
              "f0 288 f1 288 f2 288 f3 288 d0 288 d1 288 d2 288 d3 288 x0 1152 x1 1152 x2 1152 x3 1152 z0 1152 z1 1152 z2 1152"),
-        (F32, "pf 64 bias 10 o288 80 mm 48 j0 6 bw 16 co 104 cf 48 s3 48 k4 48 s3o 48 sg 32 sa 32 cs 864 gc 4 ou 32 "
-              "sw 2304 eb 192 ot 32 yt 288 r0 288 r1 288 r2 288 r3 288 r4 576 ab 40 nf 16 bi 16 wli 20 col 32"),
-        (I32, "pi 14 raw 288 pgn 18 ni 2"),
-        (U16, "wl 20 pl 256 pll 16 ol_ 4 ul 10 pgu 18 il 18 uc 32 ub 16 ue 32 u1 16 u2 16 u3 16 so 32 lb 8 lm 4 lc 4 lo 4 la 6 lk 6 lf 2 "
-              "lu 2 ld 2 ls 4 lz 2 al0 32 al1 32 al2 32 bl0 18 bl1 18 bl2 18 ll0 18 ll1 18 ll2 18"),
-        ("float16", "cb 288")):
+        (F32, "pf 64 bias 4 o288 96 ob 48 oa 96 sa 32 mm 64 j0 6 bw 16 co 128 cf 48 s3 48 k4 48 s3o 48 sg 32 cs 928 gc 4 ou 32 st 52 "
+              "sw 2304 eb 256 ot 32 yt 288 r0 288 r1 288 r2 288 r3 288 r4 576 ab 40 nf 16 bi 16 wli 20 col 32 ix 320"),
+        (I32, "pi 28 raw 288 pgn 36 ni 2"),
+        (U16, "wl 20 pl 72 ol_ 4 ul 10 uc 32 ub 16 ue 32 u1 16 u2 16 u3 16 so 32 s0 32 li 52 l6 2 "
+              "ls 4 al0 32 al1 32 al2 32 bl0 32 bl1 32 bl2 32 ll0 18 ll1 18 ll2 18")):
     _w = _names.split()
     for _n, _c in zip(_w[0::2], _w[1::2]):
         if _d != BF and _n[:2] not in ("ra", "pg", "ll", "al", "sw", "eb", "ot", "yt", "r0", "r1", "r2", "r3", "r4"):
@@ -27,19 +29,24 @@ for _d, _names in (
             PLACE[_n] = ("all" + _d, _at, int(_c))
         else:
             SCRATCH[_n] = ("sbuf", [128, int(_c)], _d)
+LISTS = dict(ld=0, lu=2, lo=4, la=8, ly=14, lm=16, lb=20, lc=28, lk=32, lz=38, il=40, lf=42, l0=44, lw=46)
+for _n, _c in LISTS.items():
+    PLACE[_n] = (PLACE["li"][0], PLACE["li"][1] + _c, 2)
 for _n, _c in (("e", 512), ("u", 128), ("r", 144), ("v", 128), ("w", 512)) + tuple(
         (_m, 288) for _m in ("x0", "x1", "x2", "x3", "p0", "p1", "p2", "z0", "z1", "z2")):
     SCRATCH["C" + _n], SCRATCH["S" + _n] = ("sbuf", [128, _c], "float8_e4m3fn_x4"), ("sbuf", [128, _c], "uint8")
 SCRATCH["ps"] = ("psum", [128, 4096], F32)
 SEMAPHORES = ["vq_", "sq_", "tq_", "gq_"] + ["dm%d" % i for i in range(20)] + [
-    n + str(t) for t in range(3) for n in ("ca", "cb", "sa", "sb", "la", "lb")]
+    n + str(t) for t in range(3) for n in ("ca", "cb", "la", "lb")]
 ORDER = []
 INFO = {}
-CASES = ((150.0, 0.9, 0.0, 2700.0), (110.0, 1.05, 10.0, 3000.0))
-POLISH = 6000
-TRIES = 300
+CASES = ((150.0, 0.9, 0.0, 2700.0), (120.0, 1.0, 0.0, 2300.0), (190.0, 0.8, 0.0, 2900.0))
+LOOSE, EARLY, HEAT = 0.2, 0.03, 15.0
+SWEEPS = ((330, 60, 300), (200, 80, 800), (140, 50, 1000), (180, 80, 600), (120, 60, 1000), (250, 50, 600), (100, 40, 1000))
+TRIES, SEED = 20, 26
 WAKE = 140.0
-CODES, LIST, COLUMN = 6000.0, 2800.0, 0.75
+CODES, LIST, COLUMN = 6200.0, 2800.0, 0.75
+FIRST, ISSUE = 1000.0, 200.0
 FAVOUR = 100.0
 
 
@@ -125,12 +132,12 @@ def rank_program(g, core, T, topo):
             ops[i]["mates"] = ids
             ops[i]["wait"].update(after)
 
-    def send(dst, out, in_, arr, loc, code=False, lat=LIST):
+    def send(dst, jobs, arr, loc, lat=LIST, more_=0.0):
         rid, pid = topo.addr(dst, core)
-        n = len(topo.engines(core, dst))
-        f = u8 if code else ap
-        s = rec("g", lambda: g.remote_dma(f(out), f(in_), T.sem[arr], T.sem[loc], pid, rid, topo.mask(core, dst)), [in_], [], 100.0, loc, n, lat)
-        r = rec(None, None, [], [out], 0.0, arr, n, lat)
+        n = len(topo.engines(core, dst)) * len(jobs)
+        s = rec("g", lambda: [g.remote_dma(f(out), f(in_), T.sem[arr], T.sem[loc], pid, rid, topo.mask(core, dst)) for out, in_, f in jobs],
+                [j[1] for j in jobs], [], ISSUE * len(jobs) + more_, loc, n, lat)
+        r = rec(None, None, [], [j[0] for j in jobs], 0.0, arr, n, lat)
         ops[r]["wait"].add(s)
 
     def more(*vs):
@@ -204,15 +211,18 @@ def rank_program(g, core, T, topo):
                 aff(L(out[0], out[1] + 16 * a, 16 * (b - a)), win, idx=L(idx[0], idx[1] + a, b - a))
 
     zero = do("v", lambda: g.vector.memset(ap(W("raw")), 0), [], [W("raw")], 300.0)
-    dmas([(("y", "s")[h % 2], T.raw[16 * h + 1:16 * h + 9, :], T.pg[:, :], [], [L("raw", 0, 288, 1, 16 * h + 1, 16 * h + 9)]) for h in range(8)]
+    dmas([("y", T.pgn[:, 0:18], T.pg[:, :], [], [L("pgn", 0, 18)]),
+          ("y", T.pgn[0:112, 18:36], T.pg[16:128, :], [], [L("pgn", 18, 18, 1, 0, 112)]),
+          ("y", T.pgn[112:128, 18:36], T.pg[0:16, :], [], [L("pgn", 18, 18, 1, 112, 128)])], 2300.0)
+    dmas([(("y", "s")[h % 2], T.raw[16 * h + 1:16 * h + 9, :], T.pg[:, :], [], [L("raw", 0, 288, 1, 16 * h + 1, 16 * h + 9)]) for h in range(RAW)]
          + [(("s", "y")[h % 2], T.raw[16 * h + 9:16 * h + 13, :], T.og[64 * (h % 2):64 * (h % 2) + 64, :], [],
-             [L("raw", 0, 288, 1, 16 * h + 9, 16 * h + 13)]) for h in range(8)])
-    dmas([("y", T.ut[:, :], T.u[:, :], [], [W("ut")])], 2500.0)
-    dmas([("y", T.x0[:, :], T.x[:, :], [], [W("x0")])], 3500.0, [zero])
-    dmas([("y", T.pgn[:, :], T.pg[:, :], [], [W("pgn")])], 3500.0, [zero])
+             [L("raw", 0, 288, 1, 16 * h + 9, 16 * h + 13)]) for h in range(RAW)], 2300.0)
+    dmas([("y", T.ut[:, :], T.u[:, :], [], [W("ut")])], 3000.0, [zero])
+    dmas([("y", T.x0[:, :], T.x[:, :], [], [W("x0")])], 4500.0, [zero])
+    loads = len(ops)
 
     P = lambda j: L("pi", j, 1)
-    nq = [13]
+    nq = [14]
 
     def Q():
         nq[0] += 1
@@ -231,42 +241,43 @@ def rank_program(g, core, T, topo):
         else:
             ts(L(name, lo, n, st), steps, add, A.add, most, A.min)
 
-    iota(L("pi", 0, 2), [[64, 2]], 0, 1)
-    for j, (sh, bits) in enumerate(((0, 15), (4, 1), (3, 1), (0, 1), (2, 1), (0, 3), (5, 3), (1, 1), (1, 3), (2, 3), (0, 7))):
-        ts(P(2 + j), P(0), sh, A.arith_shift_right, bits, A.bitwise_and)
-    ts(P(13), P(1), 5, A.arith_shift_right, 3, A.bitwise_and)
-    cast(L("pf", 1, 2), L("pi", 2, 2))
-    cast(L("pf", 3, 5), L("pi", 4, 5))
-    cast(L("pf", 8, 5), L("pi", 9, 5))
-    I, S, HI, B0, K4, K1, M, B1, MI, I4, I7, M2 = [L("pf", j, 1) for j in range(1, 13)]
+    iota(L("pi", 0, 2), [[-64, 2]], 64, 1)
+    ts(P(7), P(1), 15, A.bitwise_and)
+    cast(L("pf", 1, 1), P(7))
+    for j in range(1, 6):
+        ts(P(1 + j), P(1), 2 ** j, A.mult) if j % 2 else iota(P(1 + j), [[0, 1]], 0, 2 ** j)
+    ts(L("pi", 8, 5), L("pi", 1, 5), 4, A.arith_shift_right, 1, A.bitwise_and)
+    ts(L("pi", 13, 7), L("pi", 0, 7), 5, A.arith_shift_right, 3, A.bitwise_and)
+    cast(L("pf", 2, 5), L("pi", 8, 5))
+    cast(L("pf", 7, 7), L("pi", 13, 7))
+    I, S, HI, K4, B1, B0, M2, M = [L("pf", j, 1) for j in range(1, 9)]
+    I4, MI, K1 = [L("pf", j, 1) for j in range(11, 14)]
+    I7 = mix(I, (HI, -8))
     iota(L("wli", 1, 18), [[1, 18]], 0)
     iota(L("wli", 0, 2, 19), [[0, 2]], 0)
     listed("wl", 0, 20, W("wli"), mix(0, (I, 18)))
-    iota(W("ix"), [[1, 320]], -160)
-    top, lose, far = Q(), Q(), Q()
-    act(top, I, AF.Relu, -1, 1)
-    ts(lose, I, 9, A.is_lt, -144, A.mult)
-    act(far, I, AF.Relu, 1, -13)
-    aff(W("idm"), W("ix"), top, mix(lose, (top, 144), (far, OUT)))
+    iota(W("ix"), [[1, 320]], -16)
     iota(W("bi"), [[1, 16]], 0)
-    less, X0, X2, X3 = mix(0, (S, -1)), Q(), Q(), Q()
-    for x, b in ((X0, B0), (X3, HI), (X2, K4)):
-        act(x, b, AF.Abs, 1, less)
-    S16 = mix(0, (S, -16))
-    q = mix(S16, (X0, 304))
-    listed("pll", 0, 8, L("bi", 1, 8), mix(q, (I, 16)), st=2)
-    ts(L("pll", 1, 8, 2), L("bi", 1, 8), mix(q, (B0, 16)), A.add, 256, A.add)
-    SET, SET2 = Q(), Q()
-    ts(SET, M, 2, A.min)
-    ts(SET2, M2, 2, A.min)
+    ts(L("ab", 0, 16), W("bi"), I, A.is_equal)
+    top, far = L("ab", 0, 1), Q()
+    act(far, I, AF.Relu, 1, -13)
+    aff(W("idm"), W("ix"), top, mix(-144, (far, OUT)))
+    X3, X2, X1, X0 = Q(), Q(), Q(), Q()
+    ts(L("pf", nq[0] - 4, 4), L("pf", 3, 4), S, A.not_equal)
+    SET2, SET = Q(), Q()
+    ts(L("pf", nq[0] - 2, 2), L("pf", 7, 2), 2, A.min)
     iota(L("col", 0, 8), [[16, 8]], 0)
     iota(L("col", 8, 8), [[128, 2], [2, 4]], 0)
     iota(L("col", 16, 4), [[1, 2], [1, 2]], 0)
     iota(L("col", 20, 4), [[96, 2], [82, 2]], 14)
-    ts(L("ol_", 0, 3), L("col", 0, 3, 2), mix(K1, (SET, 96), (HI, 16), (K4, 16), (X3, 304), (S, -16)), A.add, 9, A.add)
-    ts(W("j0"), L("col", 0, 6), mix(I, (SET, 96)), A.add, -144, A.add)
-    same(L("ab", 0, 16), W("bi"), mix(0, (I, -1)))
-    aff(W("bias"), L("ab", 1, 10), LOW, 0)
+    own = q = mix(I, (SET, 96))
+    ts(L("ol_", 0, 3), L("col", 0, 3, 2), mix(q, (HI, 8), (K4, 12), (X3, 304), (S, -16)), A.add, 9, A.add)
+    ts(W("j0"), L("col", 0, 6), q, A.add, -144, A.add)
+    iota(L("pi", 20, 4), [[16, 4]], 0, 1)
+    ts(L("pi", 24, 4), L("pi", 20, 4), 4, A.arith_shift_right, 7, A.bitwise_and)
+    ts(W("bias"), L("pi", 24, 4), mix(-1, (I, 1)), A.is_equal, LOW, A.mult)
+    GR = mix(S, (M, 2))
+    less = mix(144, (GR, -288))
     tt(L("ab", 16, 8), L("ab", 2, 8), L("ab", 1, 8), A.subtract)
     aff(L("ab", 16, 8), L("ab", 16, 8), UP, 0)
     aff(L("ab", 24, 8), L("ab", 16, 8), 1, mix(0, (L("ab", 14, 1), -UP), (top, OUT)))
@@ -274,17 +285,23 @@ def rank_program(g, core, T, topo):
         aff(L("dtab", 8 * f, 8), L("ab", 24, 8), 1, L("ab", 16 + f, 1))
     aff(L("dtab", 64, 8), L("ab", 24, 8))
     iota(W("two8"), [[0, 32], [8, 2]], 0)
-    iota(W("keep8"), [[0, 32], [1, 8]], 0)
-    act(W("keep8"), W("keep8"), AF.Sign)
+    fill(W("anew"), 0)
+    fill(L("anew", 0, 32, 8), -4 * OUT)
     fill(L("cw", 0, 288), 0)
-    fill(L("o", 48, 32), 0)
+    fill(L("cw", 480, 160), 0)
+    fill(L("o", 48, 48), 0)
     fill(L("rr", 0, 16), 0)
     fill(L("rr", 208, 16), 0)
-    iota(L("rt", 192, 16), [[-1, 2], [0, 8]], 1)
-    fill(L("co", 32, 72), 0)
+    iota(L("rt", 0, 16), [[-1, 2], [0, 8]], 1)
+    fill(L("rt", 432, 32), 0)
+    fill(L("cs", 896, 32), 0)
+    fill(L("co", 0, 16), 0)
+    fill(L("co", 48, 80), 0)
     fill(L("bw", 12, 4), 0)
-    twice = mix(I, (B0, -1), (S, 1))
-    cast(L("ld", 0, 1), twice)
+    ST = lambda name, lo, n: L("st", LISTS[name] + lo, n)
+    fill(W("st"), 0)
+    twice = ST("ld", 0, 1)
+    aff(twice, S, 1, mix(I, (B0, -1)))
     q = mix(15, (twice, 16))
     ts(L("ls", 0, 1), q, 95, A.min)
     ts(L("ls", 2, 1), q, -8, A.add, 183, A.min)
@@ -295,44 +312,54 @@ def rank_program(g, core, T, topo):
     tt(L("nf", 2, 2), L("nf", 2, 2), L("nf", 0, 2), A.add)
     aff(L("nf", 4, 2), W("ni"), 2, mix(1, (S, 8), (B0, -8)))
     aff(L("nf", 6, 2), L("nf", 2, 2), 8, 0)
-    tt(L("nf", 4, 2), L("nf", 4, 2), L("nf", 6, 2), A.add)
-    ts(W("lu"), L("nf", 4, 2), 63, A.min)
+    tt(ST("lu", 0, 2), L("nf", 4, 2), L("nf", 6, 2), A.add)
     ts(L("nf", 8, 2), W("ni"), SET, A.is_equal, 2, A.mult)
     ts(L("nf", 10, 2), W("ni"), SET2, A.is_equal, mix(5, (M, 64)), A.add)
     tt(L("nf", 8, 2), L("nf", 8, 2), L("nf", 10, 2), A.add)
-    tt(L("nf", 8, 2), L("nf", 8, 2), L("nf", 6, 2), A.add)
-    cast(W("lf"), L("nf", 8, 2))
+    tt(ST("lf", 0, 2), L("nf", 8, 2), L("nf", 6, 2), A.add)
     hot = L("ab", 32, 8)
     ts(hot, L("bi", 0, 8), I7, A.is_equal)
     H = lambda k: L("ab", 32 + k, 1)
-    aff(L("col", 24, 3), L("col", 0, 3), 4, 0)
-    listed("lb", 0, 3, L("col", 24, 3), mix(0, (B0, 32), (H(6), 16), (H(2), 1000), (H(7), 1000)), 192)
-    listed("lb", 4, 3, L("col", 24, 3), mix(1000, (H(4), -1000)), mix(192, (H(0), 8), (H(3), 8)))
-    listed("lm", 0, 2, L("col", 8, 2, 4), mix(S16, (HI, 64), (B0, 32), (K4, 16), (B1, 16), (X2, 224)), 431)
-    ts(L("lm", 2, 1), mix(S16, (MI, 64), (B0, 16), (X0, 224)), 431, A.min)
-    H2S = mix(S, (HI, 2))
-    listed("lc", 0, 3, L("col", 8, 3), mix(S, (I7, 8)))
-    q = mix(0, (I4, 16), (B0, 8))
-    listed("lo", 0, 4, L("col", 16, 4), mix(q, (S, 4), (B1, 2)))
-    q = mix(0, (q, 2), (S, 192), (B1, 96))
-    listed("la", 0, 4, L("col", 20, 4), q)
-    listed("la", 4, 2, L("col", 21, 2), q)
+    aff(ST("lb", 0, 3), L("col", 1, 3, 2), 1, mix(0, (B0, 16), (H(5), 80), (H(2), -1000), (H(6), -1000)))
+    aff(ST("lb", 4, 3), L("col", 1, 3, 2), H(4), mix(0, (H(0), 8), (H(3), 8)))
+    q = mix(16, (S, -16), (B0, 16))
+    aff(ST("lm", 0, 1), MI, 32, 128)
+    aff(ST("lm", 1, 2), L("col", 0, 2, 4), 1, mix(q, (HI, 32), (B1, 96), (K4, 16), (X2, 208)))
+    aff(ST("lm", 3, 1), X0, 208, mix(q, (MI, 32)))
+    aff(ST("lc", 0, 3), L("col", 8, 3), 1, mix(S, (I7, 8)))
+    later = Q()
+    ts(later, I, 6, A.is_ge)
+    aff(ST("lo", 0, 4), L("col", 16, 4), 1, mix(0, (I, 8), (later, -44), (S, 2)))
+    aff(ST("ly", 0, 2), L("col", 6, 2), 1, I)
+    aff(ST("ly", 1, 1), mix(0, (S, later)), mix(-193, (I, 15)), ST("ly", 1, 1))
+    q = mix(0, (I, 16), (later, 96), (S, 96))
+    aff(ST("la", 0, 4), L("col", 20, 4), 1, q)
+    aff(ST("la", 4, 2), L("col", 21, 2), 1, q)
+    if REDO:
+        listed("l6", 0, 2, L("col", 21, 2), q, 383)
     q = Q()
     ts(q, I7, 5, A.min, 16, A.mult)
-    listed("lk", 0, 2, L("col", 16, 2), q, q)
-    ts(L("lk", 2, 2), L("lk", 0, 2), 14, A.add)
-    ts(L("lk", 4, 2), L("col", 8, 2, 2), mix(H2S, (q, 1)), A.add, 1, A.add)
-    aff(W("gc"), L("col", 8, 4), 1, S)
-    listed("lz", 0, 2, L("col", 0, 2, 2), mix(I, (HI, 8), (S, 8)))
-    aff(L("dq", 16, 16), L("ab", 0, 16), OUT, 0)
-    fill(L("dq", 32, 1), 0)
-    aff(L("dq", 33, 15), L("ab", 0, 15), UP, 0)
-    tt(L("dq", 0, 16), L("dq", 16, 16), L("dq", 32, 16), A.add)
-    listed("il", 0, 18, L("wli", 1, 18), I, I)
-    aff(W("dg"), L("dq", 0, 16), idx=W("il"))
-    back = mix(144 - UP, (L("ab", 15, 1), UP))
-    cast(W("pgu"), W("pgn"))
-    aff(W("pall"), L("ix", 16, 288), idx=W("pgu"))
+    aff(ST("lk", 0, 2), L("col", 16, 2), 0, q)
+    aff(ST("lk", 2, 2), ST("lk", 0, 2), 1, 14)
+    aff(ST("lk", 4, 2), L("bi", 1, 2, 4), 1, mix(q, (S, 1), (HI, 2)))
+    aff(W("gc"), L("col", 8, 4), -2048, mix(0, (S, -2048)))
+    aff(ST("lz", 0, 2), L("col", 0, 2, 2), 1, mix(I, (HI, 8), (S, 8)))
+    aff(ST("il", 0, 2), L("nf", 0, 2), 16, mix(1, (GR, 1), (X0, 304)))
+    if FREE:
+        aff(ST("l0", 0, 1), later, -47, mix(0, (twice, 8)))
+        q = mix(own, (S, -16))
+        aff(L("st", LISTS["lw"], 3, 2), L("col", 0, 3, 2), 1, mix(q, (S, 304)))
+        aff(L("st", LISTS["lw"] + 1, 3, 2), L("col", 1, 3, 2), 1, mix(304, (q, 1), (S, -304)))
+    for c, n in ((0, 4), (4, 12), (16, 16), (32, 12), (44, 8))[:4 + FREE]:
+        cast(L("li", c, n), L("st", c, n))
+    fill(L("gb", 0, 16), 0)
+    fill(L("gb", 304, 16), 0)
+    fill(L("tb", 608, 208), 0)
+    cast(L("pl", 0, 36), W("pgn"))
+    for m in range(4):
+        cast(L("pl", 36, 36, 1, 32 * m, 32 * m + 32), L("pgn", 0, 36, 1, 32 * ((m + 1) % 4), 32 * ((m + 1) % 4) + 32))
+    for c in range(4):
+        iota(L("sw", 576 * c, 576), [[0, 576]], 0)
     fill(W("one"), 1)
     do("g", lambda: g.affine_select(ap(W("et")), ap(W("one")), [[-1, 520]], A.is_equal, 0.0, 3, 4), [W("one")], [W("et")], 200 + 2.1 * 520)
     for b in range(4):
@@ -341,23 +368,26 @@ def rank_program(g, core, T, topo):
     listed("ul", 0, 10, L("bi", 0, 10), q, q)
     quant("u", 0, 128, "ut")
     ul = L("ul", 0, 9)
-    do("v", lambda: g.vector.tensor_copy(ap(W("Cr")).bitcast(dt.uint32), ap(W("Cu")).bitcast(dt.uint32).indirect(ap(ul))),
-       [W("Cu"), ul], [W("Cr")], 280.0)
+    views = do("v", lambda: g.vector.tensor_copy(ap(W("Cr")).bitcast(dt.uint32), ap(W("Cu")).bitcast(dt.uint32).indirect(ap(ul))),
+               [W("Cu"), ul], [W("Cr")], 280.0)
     act(W("Sr"), W("Su"), AF.Copy, idx=ul)
 
     def products(t):
         x = "x%d" % t
-        for c0, n in HALF if t else ((0, 288),):
+        for c0, n in RUNS if t else ((0, 288),):
             quant(x, c0, n, x)
-            for i in range(8 if t < 3 else 0):
-                bank = (i + (8 if c0 else 0)) % (8 - STAY[t - 1] if t else 8)
+            for i in range(8 if t else 0):
+                bank = (i + (8 if c0 else 0)) % (8 - STAY[t - 1])
                 mm(bank, n, "r", 2 * i, x, c0)
                 aff(L("sw", 288 * i + c0, n), PS(bank, 0, n), spread=True)
-        if t == 3:
-            return
+        if not t:
+            mm(0, 288, "u", 0, x)
+            aff(W("yt"), PS(0, 0, 288))
+            dmas([("y", T.sw[16 * h:16 * h + 1, :], T.yt[0:128:16, :], [W("yt")], [L("sw", 0, 2304, 1, 16 * h, 16 * h + 1)])
+                  for h in range(8)], 2400.0)
         dst = T.cores[rank ^ STEP[t]]
-        send(dst, W("Cp%d" % t), W("C" + x), "ca%d" % t, "cb%d" % t, True, CODES + (0 if t else 1500))
-        send(dst, W("Sp%d" % t), W("S" + x), "sa%d" % t, "sb%d" % t, False, CODES + (0 if t else 1500))
+        send(dst, [(W("Cp%d" % t), W("C" + x), u8), (W("Sp%d" % t), W("S" + x), ap)], "ca%d" % t, "cb%d" % t,
+             CODES + (0 if t else FIRST), 0 if t else FIRST)
         for b in range(4):
             if b < 4 - STAY[t]:
                 mm(1 + b, 288, "e", 128 * b, x)
@@ -367,140 +397,177 @@ def rank_program(g, core, T, topo):
 
     O = lambda name, k: L(name, k, 6, 8)
     run = lambda name, lo, n=6: L(name, lo, n, 16)
-    R = lambda n, slot=None: L("cw", 96 + 96 * n, 96) if slot is None else run("cw", 96 + 96 * n + slot)
+    at = lambda n: 96 * n + (96 if n < 4 else 256)
+    R = lambda n, slot=None: L("cw", at(n), 96) if slot is None else run("cw", at(n) + slot)
     SC = lambda n: L("cs", 480 + 96 * n, 96)
 
+    def blocks(out, o, a, b):
+        ts(a, o, GR, A.is_lt, 2304, A.mult)
+        aff(b, o, 288, less)
+        tt(out, a, b, A.add)
+
     def prepare(t):
-        par, n = t % 2, 4 - t // 2
-        tt(L("co", 0, 32), L("o", par + 1, 32, 2), L("o", par, 32, 2), A.subtract)
+        par, n, da = t % 2, 4 - t // 2, "da%d" % (t % 2)
+        blocks(L("ob", 0, 48), L("o", 0, 48), L("oa", 0, 48), L("oa", 48, 48))
+        tt(L("co", 16, 32), L("o", par + 1, 32, 2), L("o", par, 32, 2), A.subtract)
         sums(W("cp"), W("two8"), L("o", par, 64))
         if par:
-            fill(L("co", 3, 8, 4), 0)
+            fill(L("co", 19, 8, 4), 0)
             aff(O("cp", 7), O("o", 7), 1, 64)
             aff(R(-1, 14), R(0, 0))
         cast(W("uc"), W("cp"), W("lu"))
-        for a, b in ((0, 1), (1, n)):
+        for a, b in ((0, 1), (1, n)) if t or not FREE else ((1, 2), (2, n)):
             aff(L("ra", 96 * a, 96 * (b - a)), W("dtab"), idx=L("uc", 6 * a, 6 * (b - a)))
-            turn(L("da", 96 * a, 96 * (b - a)), L("ra", 96 * a, 96 * (b - a)))
+            turn(L(da, 96 * a, 96 * (b - a)), L("ra", 96 * a, 96 * (b - a)))
+        if t or not FREE:
+            for w in range(2):
+                tt(L("bw", 6 * w, 6), R(-1, 14) if par else W("j0"), O("ob", par + w), A.add)
+            cast(W("ub"), W("bw"), L("ld", 0, 1))
+            aff(run(da, 15), O("ob", 2 + par))
+        else:
+            ts(W("u3"), W("o"), 64, A.add, idx=L("l0", 0, 1))
+            aff(L("g4", 0, 192), W("dtab"), idx=L("u3", 0, 12))
+            turn(L("da1", 0, 192), L("g4", 0, 192))
+            aff(W("g1"), W("tw"), idx=L("lw", 0, 6))
+            for w in range(2):
+                scan(L("cs", 96 * w, 96), L("da1", 96 * w, 96), W("g1"))
+            ts(W("ub"), L("cs", 8, 184), 144, A.add, idx=L("ls", 2, 1))
+            for w in range(2):
+                aff(run("da1", 15 + 96 * w), O("ob", 2))
+        aff(run(da, 111), O("ob", 4 + par))
+        if t < 2:
+            aff(run(da, 303), O("o288", 7))
         for w in range(2):
-            tt(L("bw", 6 * w, 6), R(-1, 14) if par else W("j0"), O("o288", par + w), A.add)
-        cast(W("ub"), W("bw"), L("ld", 0, 1))
-        for n in range(2):
-            aff(run("da", 15 + 96 * n), O("o288", 2 + 2 * n + par))
-        for w in range(2):
-            aff(L("g0", 96 * w, 96), W("tab"), idx=L("ub", 6 * w, 6))
+            aff(L("g0", 96 * w, 96), W("tab") if t or not FREE else L("tab", 2304, 288), idx=L("ub", 6 * w, 6))
             turn(R(4 + w), L("g0", 96 * w, 96))
-            scan(L("cs", 96 * w, 96), L("da", 0, 96), R(4 + w))
-        K = lambda k: L("co", 32 + 8 * k, 6)
-        aff(K(2), L("co", 1, 6, 4), 288, 0)
-        aff(K(7), L("co", 2, 6, 4), 288, 0)
+            scan(L("cs", 96 * w, 96), L(da, 0, 96) if t or not FREE else L("da1", 96 - 96 * w, 96), R(4 + w))
+        if not t:
+            cast(W("u1"), L("cs", 0, 96), L("ls", 0, 1))
+        K = lambda k: L("co", 48 + 8 * k, 6)
+        tt(K(2), O("ob", 3 + par), O("ob", 2 + par), A.subtract)
+        tt(K(6), O("ob", 5 + par), O("ob", 4 + par), A.subtract)
         for w in range(2):
             tt(run("cs", 96 * w + 7), run("cs", 96 * w + 15), K(2), A.add)
         for v in range(2):
             cast(L("ue", 16 * v, 16), L("cs", 8 - 8 * v, 184), L("ls", 2, 1))
-            for a, b in ((0, 2),) if t else ((0, 1), (1, 2)):
+            for a, b in ((0, 2),) if t or v else ((0, 1), (1, 2)):
                 c, n = 192 * v + 96 * a, 96 * (b - a)
-                aff(L("g4", c, n), W("tab"), idx=L("ue", 16 * v + 6 * a, n // 16))
-                turn(L("cw", 672 + c, n), L("g4", c, n))
+                pick(L("g4", c, n), W("tab"), L("ue", 16 * v + 6 * a, n // 16) if t + v + a else L("u1", 0, 6), 0 if t + v + a else CUT0)
+                turn(L("cw", at(6) + c, n), L("g4", c, n))
             for w in range(2):
-                scan(L("cs", 192 + 192 * v + 96 * w, 96), L("da", 96, 96), R(6 + 2 * v + w))
+                scan(L("cs", 192 + 192 * v + 96 * w, 96), L(da, 96, 96), R(6 + 2 * v + w))
         X = lambda w, v: run("cs", 207 + 192 * v + 96 * w)
         tt(K(0), R(5, 0), R(4, 0), A.subtract)
         tt(K(1), run("cs", 111), run("cs", 15), A.subtract)
         aff(K(3), run("cs", 15))
         tt(K(5), X(1, 0), X(0, 0), A.subtract)
-        tt(K(6), X(0, 1), X(0, 0), A.subtract)
-        tt(K(4), X(1, 1), X(0, 1), A.subtract)
-        tt(K(4), K(4), K(5), A.subtract)
-        aff(K(8), X(0, 0))
-        aff(W("cf"), L("co", 40, 64), idx=L("lc", 0, 3))
-
-    def base(par):
+        tt(L("co", 112, 12), run("cs", 399, 12), run("cs", 207, 12), A.subtract)
+        tt(K(4), L("co", 118, 6), K(8), A.subtract)
+        aff(K(7), X(0, 0))
+        aff(W("cf"), L("co", 56, 64), idx=L("lc", 0, 3))
         if par:
-            fill(run("da", 207), 288 * 8 + 144)
+            fill(run(da, 207), 288 * 8 + 144)
         else:
-            aff(run("da", 207), O("o", 6), 288, 144)
+            tt(L("co", 0, 6), O("ob", 7), O("ob", 6), A.subtract)
 
-    def look(n, more_=True):
-        aff(W("g%d" % n), W("tab"), idx=L("u%d" % n, 0, 6))
+    def look(n, par, more_=True):
+        pick(W("g%d" % n), W("tab"), L("u%d" % n, 0, 6), CUT if n > 1 else 0)
         turn(R(n), W("g%d" % n))
         if more_:
-            scan(SC(n), L("da", 96 * n, 96), R(n))
+            scan(SC(n), L("da%d" % par, 96 * n, 96), R(n))
         if n == 2:
             cast(W("u3"), SC(n), L("ls", 0, 1))
 
     def score_lists(t, which):
         for n in which:
-            aff(R(n, 0 if t == 2 and n == 3 else 14), run("cs", 494 + 96 * n))
+            aff(R(n, 14), run("cs", 494 + 96 * n))
         aff(W("sg"), W("o288"), idx=L("lo", 2 * (t % 2), 2))
-        tt(W("sa"), W("cw"), W("sg"), A.add, idx=L("la", (4, 2, 0)[t], 2))
-        cast(W("so"), W("sa"))
+        if not t and REDO:
+            tt(W("sa"), L("cw", 0, 384), W("sg"), A.add, idx=W("l6"))
+            cast(W("s0"), W("sa"))
+        tt(L("cs", 864, 32), L("cw", 0, 640), W("sg"), A.add, idx=L("la", (4, 2, 0)[t], 2))
+        if t == 1:
+            cast(W("so"), L("cs", 864, 32))
+        else:
+            cast(W("so"), L("cs", 768, 160), W("ly"))
 
+    early = len(ops)
     products(0)
     rows = tt(L("tab", 2288, 320), W("raw"), W("idm"), A.add, idx=W("wl"))
+    if RAW < 8:
+        cast(L("tab", 2288, 320, 1, 64, 128), L("tab", 2288, 320, 1, 0, 64))
     dmas([("y", u8(W("Cw")), T.wc[:, :], [], [W("Cw")]), ("y", T.Sw[:, :], T.ws[:, :], [], [W("Sw")]),
-          ("y", T.vt[:, :], T.v[:, :], [], [W("vt")])], 5000.0, [rows])
+          ("y", T.vt[:, :], T.v[:, :], [], [W("vt")])], 5000.0, range(early + 3, early + 11))
     turn(L("tw", 0, 288), L("tab", 2304, 288))
     turn(L("tw", 288, 320), L("tab", 2288, 320))
-    for h in range(2):
-        ts(L("pl", 128 * h, 128), W("tw"), 144, A.add, idx=L("pll", 8 * h, 8))
-    aff(L("o", 0, 48), W("tw"), idx=L("ol_", 0, 3))
-    for r in range(8):
-        aff(L("tab", 288 * r, 288), L("tab", 2304, 288), 1, L("bias", r, 1), idx=L("pl", 32 * r, 18))
+    aff(L("o", 0, 48), W("tw"), 1, 144, idx=L("ol_", 0, 3))
+    for r in range(4):
+        aff(L("tab", 288 * r, 288), L("tab", 2304, 288), 1, L("bias", r, 1), idx=L("pl", 18 * r, 18))
+        for h in (0, 64):
+            aff(L("tab", 288 * (4 + r), 288, 1, h, h + 64), L("tab", 288 * r, 288, 1, 64 - h, 128 - h))
     aff(W("o288"), W("o"), 288, 144)
     prepare(0)
-    base(0)
+    aff(run("da0", 207), O("ob", 6))
     cast(W("u2"), L("cs", 192, 96), L("ls", 0, 1))
     for n, c in ((0, 0), (1, 192)):
         aff(R(n, 0), R(4 + 2 * n, 0))
         aff(R(n, 14), run("cs", c + 14))
     for n in (2, 3):
-        look(n)
-    score_lists(0, (2, 3))
+        look(n, 0)
+    score_lists(0, (2,))
     quant("v", 0, 128, "vt")
 
     for t in range(3):
         dst, par = T.cores[rank ^ STEP[t]], t % 2
-        pick(W("eb"), W("sw"), L("so", 16, 12), 6)
-        for h in range(2):
-            tt(L("rr", 16 + 96 * h, 96), W("sw"), L("eb", 96 * h, 96), A.is_gt, idx=L("so", 6 * h, 6))
-        turn(L("rt", 0, 192), L("rr", 16, 192))
+        def compare(c, so):
+            aff(L("eb", 16 * c, 96), W("sw"), idx=L(so, 16 + c, 6))
+            tt(L("rr", 16 + 16 * c, 96), W("sw"), L("eb", 16 * c, 96), A.is_gt, idx=L(so, c, 6))
+
+        for c in (0, 6):
+            compare(c, "so" if t or not REDO else "s0")
+        for c, n in ((16, 96), (112, 96)) if TWO else ((16, 192),):
+            turn(L("rt", c, n), L("rr", c, n))
         tt(W("s3"), L("rt", 0, 208), W("cf"), A.mult, idx=L("lb", 0, 3))
         aff(W("k4"), L("rt", 0, 208), idx=L("lb", 4, 3))
+        if not t and REDO:
+            compare(6, "so")
+            turn(L("rt", 112, 96), L("rr", 112, 96))
+        turn(L("rt", 208, 224), W("rr"))
         sums(W("s3o"), W("k4"), W("s3"))
         cast(L("u2", 0, 6), L("s3o", 7, 6, 8))
         cast(L("u1", 0, 6), L("s3o", 2, 6, 8))
-        turn(L("rt", 208, 224), W("rr"))
-        tt(W("mm"), W("rt"), L("co", 0, 48), A.mult, idx=L("lm", 0, 3))
+        tt(W("mm"), W("rt"), L("co", 0, 64), A.mult, idx=L("lm", 0, 4))
+        if not par:
+            tt(run("da0", 207), L("mm", 0, 6), O("ob", 6), A.add)
         first, second = L("o", par, 32, 2), L("o", par + 1, 32, 2)
-        tt(first, first, L("mm", 0, 32), A.add)
-        base(par)
-        tt(second, second, L("mm", 0, 32), A.subtract)
-        tt(R(0, 0), L("mm", 32, 6), R(4, 0), A.add)
-        tt(R(0, 14), L("mm", 40, 6), run("cs", 14), A.add)
+        tt(first, first, L("mm", 16, 32), A.add)
+        tt(second, second, L("mm", 16, 32), A.subtract)
+        tt(R(0, 0), L("mm", 48, 6), R(4, 0), A.add)
+        tt(R(0, 14), L("mm", 56, 6), run("cs", 14), A.add)
         for c in range(4):
-            ts(L("mk", 64 * c, 64), L("o", 0, 64), L("gc", c, 1), A.is_equal)
+            act(L("mk", 64 * c, 64), L("o", 0, 64), AF.Abs, 2048, L("gc", c, 1))
         for k in range(8):
             n, e = (k + 2 - par) // 2 - 1, (k + par) % 2
             if n > 0 and not e:
-                look(n, n < 3 or par)
+                look(n, par, n == 2 or t == 1 or t + n == 1)
             which = 2 if k == 7 or (n > 0 and e) else e
-            tt(L("mk", k, 32, 8), R(n), L("mk", k, 32, 8), A.mult, idx=L("lk", 2 * which, 2))
-        sums(W("fin"), W("keep8"), W("mk"))
+            tt(L("mk", k, 32, 8), R(n), L("mk", k, 32, 8), A.add, idx=L("lk", 2 * which, 2))
+        scan(W("fin"), W("anew"), W("mk"), A.add, A.min)
         for to, of, n, slot in ((64, 0, 64, 6), (0, 64, 64, 6), (0, 32, 32, 5), (32, 0, 32, 5), (64, 32, 32, 5), (96, 0, 32, 5)):
             aff(L("fin", slot, 32, 8, to, to + n), L("fin", 7, 32, 8, of, of + n))
         al, bl, ll = "al%d" % t, "bl%d" % t, "ll%d" % t
         ts(W(al), W("fin"), 144, A.add, idx=W("lf"))
-        send(dst, W(ll), L(al, 0, 18), "la%d" % t, "lb%d" % t)
-        aff(W("gb"), W("pall"), idx=L(al, 0, 18))
-        scan(W("cb"), W("dg"), W("gb"))
-        ts(W(bl), run("cb", 15, 18), back, A.add)
+        send(dst, [(W(ll), L(al, 0, 18), ap)], "la%d" % t, "lb%d" % t)
+        aff(L("gb", 16, 288), L("tab", 2304, 288), idx=L(al, 0, 18))
+        turn(L("tb", 0, 288), L("gb", 16, 288))
+        turn(L("tb", 288, 320), W("gb"))
+        ts(W(bl), W("tb"), 144, A.add, idx=W("il"))
         for b in range(4):
             mm(2 + b, 288, "e", 128 * b, "p%d" % t)
             aff(W("d%d" % b), PS(2 + b, 0, 288))
         if t < 2:
             aff(W("o288"), W("o"), 288, 144)
-            score_lists(t + 1, (1, 2, 3) if t else (1, 2))
+            score_lists(t + 1, (1, 2))
             prepare(t + 1)
         else:
             aff(W("ou"), L("o", 0, 64), idx=W("lz"))
@@ -513,10 +580,10 @@ def rank_program(g, core, T, topo):
                 aff(L(z, 4 * c0 + b, n, 4), W("d%d" % b), idx=L(ll, c0 // 16, n // 16))
             quant(z, c0, n, z)
             for b in range(4):
-                bank = (1 + b, (5, 0, 1, 2)[b])[h]
+                bank = (1 + b, ((5, 6, 0, 1) if STAY[t] == 1 else (5, 0, 1, 2))[b])[h]
                 mm(bank, n, "w", 128 * b, z, c0)
                 aff(L("r%d" % b, c0, n), PS(bank, 0, n), 0.03125)
-        for c0, n in HALF:
+        for c0, n in RUNS:
             i = L(bl, c0 // 16, n // 16)
             for b in range(4):
                 if b < 4 - STAY[t]:
@@ -524,14 +591,24 @@ def rank_program(g, core, T, topo):
                 else:
                     aff(L("r4", 288 * (3 - b) + c0, n), W("r%d" % b), idx=i)
                     tt(L(x, 4 * c0 + b, n, 4), PS(4 + b, c0, n), L("r4", 288 * (3 - b) + c0, n), A.add)
-        products(t + 1)
+                if t == 2 and c0 and b >= LAST:
+                    ops[-1]["wait"].add(stored)
+            if t == 2:
+                stored = len(ops)
+                quant(x, c0, n, x)
+        if t < 2:
+            products(t + 1)
 
-    for h, (c0, n) in enumerate(HALF):
-        mm(5 + h, n, "v", 0, "x3", c0)
-        aff(L("yt", c0, n), PS(5 + h, 0, n))
-        dmas([("y", T.y[:, c0:c0 + n], T.yt[:, c0:c0 + n], [L("yt", c0, n)], [])])
-        dmas([("s", T.oc[:, 4 * c0:4 * c0 + 4 * n], u8(L("Cx3", c0, n)), [L("Cx3", c0, n)], [])])
-    dmas([("y", T.osc[4 * k:4 * k + 4, :], T.Sx3[32 * k:32 * k + 4, 0:288], [W("Sx3")], []) for k in range(4)], 2000.0)
+    for h, (c0, n) in enumerate(RUNS):
+        mm(4 + h, n, "v", 0, "x3", c0)
+        aff(L("yt", c0, n), PS(4 + h, 0, n))
+        if h and ENDS:
+            ops[-1]["dur"] = {"v": ops[-1]["dur"]["v"]}
+    for c0, n in RUNS if YW else ((0, 288),):
+        dmas([("y", T.y[:, c0:c0 + n], T.yt[:, c0:c0 + n], [L("yt", c0, n)], [])], 2150.0 if c0 else 2900.0)
+    for c0, n in RUNS if OW else ((0, 288),):
+        dmas([("s", T.oc[:, 4 * c0:4 * c0 + 4 * n], u8(L("Cx3", c0, n)), [L("Cx3", c0, n)], [])], 2500.0 if c0 else 3300.0)
+    dmas([("ys"[k % 2 * ENDS], T.osc[4 * k:4 * k + 4, :], T.Sx3[32 * k:32 * k + 4, 0:288], [W("Sx3")], []) for k in range(4)], 2000.0)
 
     if not ORDER:
         N = len(ops)
@@ -579,7 +656,7 @@ def rank_program(g, core, T, topo):
 
         pre = [sorted(o["wait"]) for o in ops]
         key, on, kept = [-p for p in prio], {i: o["q"] for i, o in enumerate(ops)}, None
-        dice = numpy.random.RandomState(1)
+        dice = numpy.random.RandomState(SEED)
 
         def lasts(order, on):
             both, tight = 0.0, []
@@ -608,7 +685,7 @@ def rank_program(g, core, T, topo):
             return both, tight
 
         for n in range(TRIES):
-            start, end, on = place(key, pre, nxt, on, False)
+            start, end, on = place([i - 1e9 if i < loads else k for i, k in enumerate(key)], pre, nxt, on, False)
             took = lasts(sorted(range(N), key=lambda i: (start[i], i)), on)[0]
             if kept is None or took <= kept[4]:
                 kept = (start, end, on, list(favour), took)
@@ -621,28 +698,151 @@ def rank_program(g, core, T, topo):
             key = [k + float(shake[i]) if near[i] else k for i, k in enumerate(base)]
             favour[:] = [float(other[i]) if near[i] and abs(shake[i]) < 50.0 else f for i, f in enumerate(kept[3])]
         order, on = sorted(range(N), key=lambda i: (kept[0][i], i)), kept[2]
-        took, tight = lasts(order, on)
-        where = {m: n for n, m in enumerate(order)}
-        for n in range(POLISH):
-            i, k = tight[dice.randint(len(tight))]
-            new, to = list(order), on
-            how, a, b = dice.randint(3), where[k], where[i]
-            if how == 0 and ops[k]["q"] == "f":
-                to = dict(on)
-                to[k] = sorted(ops[k]["dur"])[dice.randint(len(ops[k]["dur"]))]
-            elif how == 1:
-                if any(where[m] > a for m in pre[i]):
-                    continue
-                new.insert(a, new.pop(b))
-            else:
-                b += dice.randint(4)
-                if any(where[m] <= b for m in nxt[k]):
-                    continue
-                new.insert(b, new.pop(a))
-            t2, w2 = lasts(new, to)
-            if t2 <= took:
-                order, on, took, tight = new, to, t2, w2
-                where = {m: n for n, m in enumerate(order)}
+        hold = [{q: [((o["dur"][q] if o["q"] == "f" else o["dur"]) if o["lat"] or not q else
+                      (o["dur"][q] if o["q"] == "f" else o["dur"]) * slow + each) if o["q"] == q or (o["q"] == "f" and q in o["dur"]) else 0.0
+                     for o in ops] for q in list(queue) + [None]} for wake, slow, each, way in CASES]
+        late = [[(way if o["lat"] == LIST else o["lat"]) if o["q"] else 0.0 for o in ops] for wake, slow, each, way in CASES]
+
+        can = [sorted(o["dur"]) if o["q"] == "f" else [o["q"]] for o in ops]
+
+        def inside(part, on, c, done, free, out, outq):
+            wake, why, last, free, end, at_end, all_ = CASES[c][0], {}, {}, dict(free), 0.0, -1, 0.0
+            for i in part:
+                q, at, by = on[i], 0.0, -1
+                for m in pre[i]:
+                    if done[m] + wake > at:
+                        at, by = done[m] + wake, m
+                if q is None:
+                    d = at - wake
+                else:
+                    if free[q] > at:
+                        at, by = free[q], -2 - last.get(q, -1)
+                    last[q] = i
+                    free[q] = at + hold[c][q][i]
+                    d = at + late[c][i] if late[c][i] else free[q]
+                done[i], why[i] = d, by
+                all_ += d
+                if d + out[i] > end:
+                    end, at_end = d + out[i], i
+            for q in free:
+                if free[q] + outq[q] > end:
+                    end, at_end = free[q] + outq[q], last.get(q, -1)
+            tight, i = [], at_end
+            while i in why:
+                if why[i] < -1:
+                    tight.append((i, -2 - why[i]))
+                i = why[i] if why[i] >= -1 else -2 - why[i]
+            return end + EARLY * all_ / len(part), tight
+
+        for WIDE, ANEW, POLISH in SWEEPS:
+            for c0 in range(0, N - WIDE // 2, WIDE // 2):
+                part, rest, state = order[c0:c0 + WIDE], order[c0 + WIDE:], []
+                for c in range(len(CASES)):
+                    wake, done, free, tail, outq = CASES[c][0], [0.0] * N, {q: 0.0 for q in queue}, {}, {q: 0.0 for q in queue}
+                    for i in order[:c0]:
+                        q, at = on[i], max([0.0] + [done[m] + wake for m in pre[i]])
+                        if q is None:
+                            done[i] = at - wake
+                        else:
+                            at = max(at, free[q])
+                            free[q] = at + hold[c][q][i]
+                            done[i] = at + late[c][i] if late[c][i] else free[q]
+                    for i in reversed(rest):
+                        q, after = on[i], max([0.0] + [wake + tail[k] for k in nxt[i]])
+                        tail[i] = after - wake if q is None else max((late[c][i] or hold[c][q][i]) + after, hold[c][q][i] + outq[q])
+                        if q:
+                            outq[q] = tail[i]
+                    state.append((done, free, {i: max([0.0] + [wake + tail[k] for k in nxt[i] if k in tail]) for i in part}, outq))
+
+                def both(part, on):
+                    got = [inside(part, on, c, *state[c]) for c in range(len(CASES))]
+                    return sum(x[0] for x in got), [p for x in got for p in x[1]]
+
+                took, tight = both(part, on)
+                done, free, out, outq = state[0]
+                wake, here, way = CASES[0][0], set(part), {}
+                for i in reversed(part):
+                    way[i] = (late[0][i] or hold[0][on[i]][i]) + max([out[i], outq.get(on[i], 0.0)] + [wake + way[k] for k in nxt[i] if k in here])
+                into = {i: max([0.0] + [done[m] + wake for m in pre[i] if m not in here]) for i in part}
+                inner = [{i: [m for m in x[i] if m in here] for i in part} for x in (pre, nxt)]
+
+                def lay(key, to, lean, back):
+                    before, after, from_, busy = inner[back], inner[1 - back], (into, out)[back], {q: [(0.0, (free, outq)[back][q]), (1e18, 1e18)] for q in queue}
+                    left, start, end = {i: len(before[i]) for i in part}, {}, {}
+                    ready = [(key[i], i) for i in part if not left[i]]
+                    while ready:
+                        ready.sort(reverse=True)
+                        i = ready.pop()[1]
+                        at0, pick_ = from_[i], None
+                        for m in before[i]:
+                            if end[m] + wake > at0:
+                                at0 = end[m] + wake
+                        if to[i] is None:
+                            start[i] = end[i] = at0 - wake
+                        else:
+                            for q in (can[i] if lean is not None else [to[i]]):
+                                dur = hold[0][q][i]
+                                at = at0 + (late[0][i] - dur if back and late[0][i] else 0.0)
+                                for c, (a, b) in enumerate(busy[q]):
+                                    if b > at:
+                                        if a >= at + dur:
+                                            break
+                                        at = b
+                                worth = at + dur + (lean[i] if q == "v" and lean is not None else 0.0)
+                                if pick_ is None or worth < pick_[0]:
+                                    pick_ = (worth, at, dur, q, c)
+                            worth, at, dur, to[i], c = pick_
+                            busy[to[i]].insert(c, (at, at + dur))
+                            start[i], end[i] = at, at + (dur if back else late[0][i] or dur)
+                        for k in after[i]:
+                            left[k] -= 1
+                            if not left[k]:
+                                ready.append((key[k], k))
+                    return start, end
+
+                seed = {i: -way[i] for i in part}
+                for n in range(ANEW):
+                    noise, lean = dice.normal(0.0, (30.0, 80.0, 200.0, 500.0)[n % 4], N), dice.normal(FAVOUR / 2, FAVOUR, N)
+                    to, key = dict(on), {i: i - 1e9 if i < loads else seed[i] + noise[i] for i in part}
+                    for again in range(2):
+                        start, end = lay(key, to, lean if n % 3 or not again else None, 0)
+                        new = sorted(part, key=lambda i: (start[i], i))
+                        t2, w2 = both(new, to)
+                        key = lay({i: -end[i] for i in part}, dict(to), None, 1)[1]
+                        key = {i: i - 1e9 if i < loads else -key[i] for i in part}
+                        if t2 <= took:
+                            part, on, took, tight, seed = new, dict(to), t2, w2, key
+                where, best, M_ = {m: n for n, m in enumerate(part)}, (took, part, on), len(part)
+                for n in range(POLISH):
+                    luck = dice.rand(6)
+                    if luck[0] < LOOSE or not tight:
+                        b = 1 + int(luck[1] * (M_ - 1))
+                        i, k = part[b], part[max(0, b - 1 - int(luck[2] * 40))]
+                    else:
+                        i, k = tight[int(luck[1] * len(tight))]
+                    new, to, how = part, on, int(luck[3] * 3)
+                    if how == 0 and ops[k]["q"] == "f":
+                        to = dict(on)
+                        to[k] = sorted(ops[k]["dur"])[int(luck[4] * len(ops[k]["dur"]))]
+                    else:
+                        up, far = how == 1, (0, 0, 3, 10, 30)[int(luck[4] * 5)]
+                        a, b = (max(0, where[k] - far), where[i]) if up else (where[k], min(M_ - 1, where[i] + far))
+                        move, todo = set(), [i if up else k]
+                        while todo and len(move) < 12:
+                            m = todo.pop()
+                            move.add(m)
+                            todo += [x for x in (pre if up else nxt)[m] if a <= where.get(x, -1) <= b and x not in move]
+                        if todo or (i in move and k in move) or min(move) < loads:
+                            continue
+                        new = part[:a] + [m for m in part[a:b + 1] if (m in move) == up] + [m for m in part[a:b + 1] if (m in move) != up] + part[b + 1:]
+                    t2, w2 = both(new, to)
+                    if t2 <= took - HEAT * (1.0 - n / POLISH) * math.log(1.0 - luck[5]):
+                        part, on, took, tight = new, to, t2, w2
+                        where = {m: c for c, m in enumerate(part)}
+                        if took <= best[0]:
+                            best = (took, part, on)
+                order, on = order[:c0] + best[1] + rest, best[2]
+        took = lasts(order, on)[0]
         ORDER.extend((i, on[i]) for i in order)
         INFO.update(ops=ops, start=kept[0], done=kept[1], on=kept[2], took=took)
 

@@ -5,21 +5,29 @@ from concourse.mybir import dt, AluOpType, ActivationFunctionType
 STEP = (4, 1, 2)
 HALF = ((0, 160), (160, 128))
 RUNS = HALF
-LAST, YW, OW, REDO, RAW, FREE, CUT, TWO = 4, 1, 1, 1, 4, 0, 4, 1
-CUT0, ENDS = 0, 0
-STAY = (1, 1, 2)
+LAST, YW, OW, REDO, RAW, CUT, TWO = 4, 1, 1, 1, 4, 4, 1
+CUTS = ()
+CUT0, ENDS, SWAP, FOUR = 0, 0, 0, 0
+LAYS = "yysyysyy"
+LATE = 3
+SHIFT = (0, 2, 6)
+VIEW = (0, 0, 1, 0, 0, 2, 2, 1)
+FAR = 4096
+PART = ((0, 1, 0), (1, 1, 0), (2, 1, 0))
+STAY = (3, 3, 3)
 UP, LOW, OUT = 1024, -768, -4096
 
 BF, F32, I32, U16 = "bfloat16", "float32", "int32", "uint16"
 SCRATCH, PLACE = {}, {}
 for _d, _names in (
-        (BF, "one 520 et 520 ut 512 vt 512 tab 2608 tw 608 idm 320 dtab 72 ra 384 da0 384 da1 384 tb 816 "
-             "g0 192 g1 96 g2 96 g3 96 g4 384 cw 1216 gb 320 rr 224 rt 464 o 96 cp 64 two8 64 anew 256 mk 256 fin 256 "
+        (BF, "one 520 et 520 ut 512 vt 512 tab 2608 tw 608 dtab 72 ra 384 da0 384 da1 384 tb 608 anew 192 "
+             "g0 192 g1 96 g2 96 g3 96 g4 384 cw 1216 gb 320 rr 224 rt 464 rq 208 mp 192 pm 192 mtab 72 o 96 cp 80 two8 80 "
              "f0 288 f1 288 f2 288 f3 288 d0 288 d1 288 d2 288 d3 288 x0 1152 x1 1152 x2 1152 x3 1152 z0 1152 z1 1152 z2 1152"),
-        (F32, "pf 64 bias 4 o288 96 ob 48 oa 96 sa 32 mm 64 j0 6 bw 16 co 128 cf 48 s3 48 k4 48 s3o 48 sg 32 cs 928 gc 4 ou 32 st 52 "
-              "sw 2304 eb 256 ot 32 yt 288 r0 288 r1 288 r2 288 r3 288 r4 576 ab 40 nf 16 bi 16 wli 20 col 32 ix 320"),
-        (I32, "pi 28 raw 288 pgn 36 ni 2"),
-        (U16, "wl 20 pl 72 ol_ 4 ul 10 uc 32 ub 16 ue 32 u1 16 u2 16 u3 16 so 32 s0 32 li 52 l6 2 "
+        (F32, "pf 96 bias 4 ob 48 oa 96 sa 32 mm 64 j0 6 bw 16 st 52 co 128 cf 48 mk 192 s3 48 k4 48 s3o 48 sg 32 cs 992 gc 4 ou 32 "
+              "sw 2304 eb 256 ot 32 yt 288 r0 288 r1 288 r2 288 r3 288 r4 1152 ab 40 nf 18 bi 20 col 32 "
+              "fin 192 ok 48 vk 48 cap 2 wf 272"),
+        (I32, "pi 28 raw 288 rank0 26 pgn 36 pgm 36 ni 2 wt 72 wi 200"),
+        (U16, "l2 16 um 16 wl 20 pl 72 ol_ 4 ul 10 uc 32 ub 16 ue 32 u1 16 u2 16 u3 16 so 32 s0 32 li 52 l6 2 "
               "ls 4 al0 32 al1 32 al2 32 bl0 32 bl1 32 bl2 32 ll0 18 ll1 18 ll2 18")):
     _w = _names.split()
     for _n, _c in zip(_w[0::2], _w[1::2]):
@@ -29,21 +37,23 @@ for _d, _names in (
             PLACE[_n] = ("all" + _d, _at, int(_c))
         else:
             SCRATCH[_n] = ("sbuf", [128, int(_c)], _d)
-LISTS = dict(ld=0, lu=2, lo=4, la=8, ly=14, lm=16, lb=20, lc=28, lk=32, lz=38, il=40, lf=42, l0=44, lw=46)
+LISTS = dict(ld=0, lu=2, lo=4, l0=6, lm=8, lb=14, lc=22, lk=26, lf=30, lv=32, lw=36, la=40, lq=44, lz=46, il=48)
 for _n, _c in LISTS.items():
     PLACE[_n] = (PLACE["li"][0], PLACE["li"][1] + _c, 2)
 for _n, _c in (("e", 512), ("u", 128), ("r", 144), ("v", 128), ("w", 512)) + tuple(
         (_m, 288) for _m in ("x0", "x1", "x2", "x3", "p0", "p1", "p2", "z0", "z1", "z2")):
     SCRATCH["C" + _n], SCRATCH["S" + _n] = ("sbuf", [128, _c], "float8_e4m3fn_x4"), ("sbuf", [128, _c], "uint8")
 SCRATCH["ps"] = ("psum", [128, 4096], F32)
-SEMAPHORES = ["vq_", "sq_", "tq_", "gq_"] + ["dm%d" % i for i in range(20)] + [
-    n + str(t) for t in range(3) for n in ("ca", "cb", "la", "lb")]
+SEMAPHORES = ["vq_", "sq_", "tq_", "gq_"] + ["dm%d" % i for i in range(24)] + [
+    n + str(t) for t in range(3) for n in ("ca", "cb", "ce", "cf", "la", "lb")]
+AHEAD = 1000.0
 ORDER = []
 INFO = {}
-CASES = ((150.0, 0.9, 0.0, 2700.0), (120.0, 1.0, 0.0, 2300.0), (190.0, 0.8, 0.0, 2900.0))
-LOOSE, EARLY, HEAT = 0.2, 0.03, 15.0
-SWEEPS = ((330, 60, 300), (200, 80, 800), (140, 50, 1000), (180, 80, 600), (120, 60, 1000), (250, 50, 600), (100, 40, 1000))
-TRIES, SEED = 20, 26
+CASES = ((155.0, 1.0, 1.0, 2500.0), (150.0, 1.2, 1.15, 2700.0), (200.0, 0.95, 1.1, 2900.0))
+LOOSE, EARLY, HEAT, ROOM = 0.2, 0.03, 15.0, 60.0
+SWEEPS = ((330, 150, 800), (200, 150, 1500), (140, 100, 1500), (260, 100, 1500), (100, 80, 1500), (180, 100, 1500), (70, 60, 1200),
+          (130, 60, 1500))
+TRIES, SEED = 12, 7
 WAKE = 140.0
 CODES, LIST, COLUMN = 6200.0, 2800.0, 0.75
 FIRST, ISSUE = 1000.0, 200.0
@@ -189,7 +199,14 @@ def rank_program(g, core, T, topo):
     def fill(v, k):
         calls = {"v": lambda: g.vector.memset(ap(v), float(k)),
                  "g": lambda: g.iota(ap(v), [[0, size(v)]], k, 0, allow_small_or_imprecise_dtypes=True)}
-        rec("f", calls, [], [v], {"g": 160 + 2.1 * size(v), "v": cost("v", v, [], None)}, None)
+        dur, none = {"g": 160 + 2.1 * size(v), "v": cost("v", v, [], None)}, L("cs", 0, min(96, size(v)))
+        if size(v) <= 96 and v != none:
+            calls["s"], dur["s"] = lambda: g.scalar.activation(ap(v), ap(none), AF.Identity, bias=float(k), scale=1.0), cost("s", v, [], None)
+        rec("f", calls, [none] if "s" in dur else [], [v], dur, None)
+
+    def plus(out, a, b):
+        for c in range(size(out)):
+            aff(out[:1] + (out[1] + c, out[1] + c + 1) + out[3:], a[:1] + (a[1] + c, a[1] + c + 1) + a[3:], 1, b[:1] + (b[1] + c, b[1] + c + 1) + b[3:])
 
     def quant(name, c0, n, x, x0=None):
         q, s, v = L("C" + name, c0, n), L("S" + name, c0, n), L(x, 4 * c0 if x0 is None else x0, 4 * n)
@@ -210,19 +227,25 @@ def rank_program(g, core, T, topo):
             if b > a:
                 aff(L(out[0], out[1] + 16 * a, 16 * (b - a)), win, idx=L(idx[0], idx[1] + a, b - a))
 
-    zero = do("v", lambda: g.vector.memset(ap(W("raw")), 0), [], [W("raw")], 300.0)
+    iota(L("rank0", 8, 18), [[16, 18]], 0, 1)
+    do("v", lambda: g.vector.memset(ap(L("cs", 0, 96)), 0.0), [], [L("cs", 0, 96)], 100.0)
+    do("v", lambda: g.vector.memset(ap(L("raw", 0, 288, 1, 64, 128)), 0), [], [L("raw", 0, 288, 1, 64, 128)], 300.0)
+    rows = [(h, 1, 9, T.pg[:, :]) for h in range(4)] + [(h, 9, 16, T.og[0:112, :]) for h in (0, 2)] + [
+        (h, a, b, of) for h in (1, 3) for a, b, of in ((9, 13, T.og[64:128, :]), (13, 16, T.og[0:48, :]))]
+    dmas([("ys"[n % 2], T.raw[16 * h + a:16 * h + b, :], of, [], [L("raw", 0, 288, 1, 16 * h + a, 16 * h + b)]) for n, (h, a, b, of) in enumerate(rows)]
+         + [("y", T.raw[0:64:16, :], T.rank0[0:64, 8:26], [L("rank0", 8, 18)], [L("raw", 0, 288, 1, 0, 64)])], 2350.0)
     dmas([("y", T.pgn[:, 0:18], T.pg[:, :], [], [L("pgn", 0, 18)]),
           ("y", T.pgn[0:112, 18:36], T.pg[16:128, :], [], [L("pgn", 18, 18, 1, 0, 112)]),
-          ("y", T.pgn[112:128, 18:36], T.pg[0:16, :], [], [L("pgn", 18, 18, 1, 112, 128)])], 2300.0)
-    dmas([(("y", "s")[h % 2], T.raw[16 * h + 1:16 * h + 9, :], T.pg[:, :], [], [L("raw", 0, 288, 1, 16 * h + 1, 16 * h + 9)]) for h in range(RAW)]
-         + [(("s", "y")[h % 2], T.raw[16 * h + 9:16 * h + 13, :], T.og[64 * (h % 2):64 * (h % 2) + 64, :], [],
-             [L("raw", 0, 288, 1, 16 * h + 9, 16 * h + 13)]) for h in range(RAW)], 2300.0)
-    dmas([("y", T.ut[:, :], T.u[:, :], [], [W("ut")])], 3000.0, [zero])
-    dmas([("y", T.x0[:, :], T.x[:, :], [], [W("x0")])], 4500.0, [zero])
+          ("y", T.pgn[112:128, 18:36], T.pg[0:16, :], [], [L("pgn", 18, 18, 1, 112, 128)])], 2700.0)
+    if FOUR:
+        dmas([("y", T.pgm[a:b, 18 * k:18 * k + 18], T.pg[(a + 32 + 16 * k) % 128:(b + 31 + 16 * k) % 128 + 1, :], [],
+               [L("pgm", 18 * k, 18, 1, a, b)]) for k in range(2) for a, b in ((0, 96 - 16 * k), (96 - 16 * k, 128))], 2700.0)
+    dmas([("y", T.x0[:, :], T.x[:, :], [], [W("x0")])], 5000.0)
+    dmas([("y", T.ut[:, :], T.u[:, :], [], [W("ut")])], 5400.0)
     loads = len(ops)
 
     P = lambda j: L("pi", j, 1)
-    nq = [14]
+    nq = [15]
 
     def Q():
         nq[0] += 1
@@ -241,122 +264,113 @@ def rank_program(g, core, T, topo):
         else:
             ts(L(name, lo, n, st), steps, add, A.add, most, A.min)
 
-    iota(L("pi", 0, 2), [[-64, 2]], 64, 1)
-    ts(P(7), P(1), 15, A.bitwise_and)
-    cast(L("pf", 1, 1), P(7))
-    for j in range(1, 6):
-        ts(P(1 + j), P(1), 2 ** j, A.mult) if j % 2 else iota(P(1 + j), [[0, 1]], 0, 2 ** j)
-    ts(L("pi", 8, 5), L("pi", 1, 5), 4, A.arith_shift_right, 1, A.bitwise_and)
-    ts(L("pi", 13, 7), L("pi", 0, 7), 5, A.arith_shift_right, 3, A.bitwise_and)
-    cast(L("pf", 2, 5), L("pi", 8, 5))
-    cast(L("pf", 7, 7), L("pi", 13, 7))
-    I, S, HI, K4, B1, B0, M2, M = [L("pf", j, 1) for j in range(1, 9)]
-    I4, MI, K1 = [L("pf", j, 1) for j in range(11, 14)]
+    twos = lambda j: L("rank0", 8 - j, 1)
+    ts(P(7), twos(0), 15, A.bitwise_and)
+    cast(L("pf", 0, 1), P(7))
+    for j in range(1, 5):
+        ts(twos(j), twos(0), 2 ** j, A.mult) if j % 2 else iota(twos(j), [[0, 1]], 0, 2 ** j)
+    ts(L("pi", 8, 5), L("rank0", 4, 5), 4, A.arith_shift_right, 1, A.bitwise_and)
+    ts(L("pi", 13, 9), L("rank0", 4, 9), 5, A.arith_shift_right, 3, A.bitwise_and)
+    cast(L("pf", 1, 5), L("pi", 8, 5))
+    cast(L("pf", 6, 9), L("pi", 13, 9))
+    I, B0, B1, K4, HI, S, MI, I4 = [L("pf", j, 1) for j in range(8)]
+    M = L("pf", 10, 1)
     I7 = mix(I, (HI, -8))
-    iota(L("wli", 1, 18), [[1, 18]], 0)
-    iota(L("wli", 0, 2, 19), [[0, 2]], 0)
-    listed("wl", 0, 20, W("wli"), mix(0, (I, 18)))
-    iota(W("ix"), [[1, 320]], -16)
-    iota(W("bi"), [[1, 16]], 0)
-    ts(L("ab", 0, 16), W("bi"), I, A.is_equal)
+    iota(W("bi"), [[1, 20]], 0)
+    listed("wl", 0, 20, W("bi"), mix(-1, (I, 18)), 287)
+    ts(L("ab", 0, 16), L("bi", 0, 16), I, A.is_equal, UP, A.mult)
     top, far = L("ab", 0, 1), Q()
     act(far, I, AF.Relu, 1, -13)
-    aff(W("idm"), W("ix"), top, mix(-144, (far, OUT)))
-    X3, X2, X1, X0 = Q(), Q(), Q(), Q()
-    ts(L("pf", nq[0] - 4, 4), L("pf", 3, 4), S, A.not_equal)
-    SET2, SET = Q(), Q()
-    ts(L("pf", nq[0] - 2, 2), L("pf", 7, 2), 2, A.min)
+    GR = mix(S, (M, 2))
+    lose = mix(mix(-144, (far, OUT)), (GR, mix(0, (top, -16.0 / UP))))
+    X0, X1, X2, X3 = Q(), Q(), Q(), Q()
+    ts(L("pf", nq[0] - 4, 4), L("pf", 1, 4), S, A.not_equal)
+    SET, SET2 = Q(), Q()
+    ts(L("pf", nq[0] - 2, 2), L("pf", 10, 2, 4), 2, A.min)
     iota(L("col", 0, 8), [[16, 8]], 0)
-    iota(L("col", 8, 8), [[128, 2], [2, 4]], 0)
-    iota(L("col", 16, 4), [[1, 2], [1, 2]], 0)
     iota(L("col", 20, 4), [[96, 2], [82, 2]], 14)
     own = q = mix(I, (SET, 96))
     ts(L("ol_", 0, 3), L("col", 0, 3, 2), mix(q, (HI, 8), (K4, 12), (X3, 304), (S, -16)), A.add, 9, A.add)
     ts(W("j0"), L("col", 0, 6), q, A.add, -144, A.add)
-    iota(L("pi", 20, 4), [[16, 4]], 0, 1)
-    ts(L("pi", 24, 4), L("pi", 20, 4), 4, A.arith_shift_right, 7, A.bitwise_and)
+    ts(L("pi", 24, 4), L("rank0", 8, 4), 4, A.arith_shift_right, 7, A.bitwise_and)
     ts(W("bias"), L("pi", 24, 4), mix(-1, (I, 1)), A.is_equal, LOW, A.mult)
-    GR = mix(S, (M, 2))
     less = mix(144, (GR, -288))
     tt(L("ab", 16, 8), L("ab", 2, 8), L("ab", 1, 8), A.subtract)
-    aff(L("ab", 16, 8), L("ab", 16, 8), UP, 0)
-    aff(L("ab", 24, 8), L("ab", 16, 8), 1, mix(0, (L("ab", 14, 1), -UP), (top, OUT)))
+    aff(L("ab", 24, 8), L("ab", 16, 8), 1, mix(0, (L("ab", 14, 1), -1), (top, OUT // UP)))
     for f in range(8):
         aff(L("dtab", 8 * f, 8), L("ab", 24, 8), 1, L("ab", 16 + f, 1))
     aff(L("dtab", 64, 8), L("ab", 24, 8))
-    iota(W("two8"), [[0, 32], [8, 2]], 0)
+    for k in range(2):
+        fill(L("two8", k, 40, 2), 8 * k)
     fill(W("anew"), 0)
-    fill(L("anew", 0, 32, 8), -4 * OUT)
-    fill(L("cw", 0, 288), 0)
-    fill(L("cw", 480, 160), 0)
+    fill(L("anew", 0, 24, 8), 8 * FAR)
+    fill(L("cs", 608, 96), 0)
     fill(L("o", 48, 48), 0)
     fill(L("rr", 0, 16), 0)
     fill(L("rr", 208, 16), 0)
-    iota(L("rt", 0, 16), [[-1, 2], [0, 8]], 1)
+    fill(L("rt", 0, 8), 1)
+    fill(L("rt", 8, 8), 0)
     fill(L("rt", 432, 32), 0)
-    fill(L("cs", 896, 32), 0)
     fill(L("co", 0, 16), 0)
     fill(L("co", 48, 80), 0)
-    fill(L("bw", 12, 4), 0)
     ST = lambda name, lo, n: L("st", LISTS[name] + lo, n)
-    fill(W("st"), 0)
+    fill(L("bw", 12, 56), 0)
     twice = ST("ld", 0, 1)
     aff(twice, S, 1, mix(I, (B0, -1)))
     q = mix(15, (twice, 16))
     ts(L("ls", 0, 1), q, 95, A.min)
     ts(L("ls", 2, 1), q, -8, A.add, 183, A.min)
     aff(L("nf", 0, 2), L("col", 0, 2), 1, I)
-    ts(L("nf", 2, 2), L("nf", 0, 2), -2.5, A.add, 1.0 / 6, A.mult)
+    aff(L("nf", 2, 2), L("nf", 0, 2), 1.0 / 6, -2.5 / 6)
     cast(W("ni"), L("nf", 2, 2))
-    aff(L("nf", 2, 2), W("ni"), -6, 0)
-    tt(L("nf", 2, 2), L("nf", 2, 2), L("nf", 0, 2), A.add)
+    aff(L("nf", 2, 2), L("nf", 0, 2), 8, 0)
+    for c in range(2):
+        aff(L("nf", 6 + c, 1), L("ni", c, 1), -48, L("nf", 2 + c, 1))
     aff(L("nf", 4, 2), W("ni"), 2, mix(1, (S, 8), (B0, -8)))
-    aff(L("nf", 6, 2), L("nf", 2, 2), 8, 0)
     tt(ST("lu", 0, 2), L("nf", 4, 2), L("nf", 6, 2), A.add)
     ts(L("nf", 8, 2), W("ni"), SET, A.is_equal, 2, A.mult)
-    ts(L("nf", 10, 2), W("ni"), SET2, A.is_equal, mix(5, (M, 64)), A.add)
-    tt(L("nf", 8, 2), L("nf", 8, 2), L("nf", 10, 2), A.add)
-    tt(ST("lf", 0, 2), L("nf", 8, 2), L("nf", 6, 2), A.add)
+    ts(L("nf", 10, 2), W("ni"), SET2, A.is_equal, mix(5, (M, 48)), A.add)
+    plus(L("nf", 8, 2), L("nf", 8, 2), L("nf", 10, 2))
+    plus(ST("lf", 0, 2), L("nf", 8, 2), L("nf", 6, 2))
     hot = L("ab", 32, 8)
     ts(hot, L("bi", 0, 8), I7, A.is_equal)
     H = lambda k: L("ab", 32 + k, 1)
     aff(ST("lb", 0, 3), L("col", 1, 3, 2), 1, mix(0, (B0, 16), (H(5), 80), (H(2), -1000), (H(6), -1000)))
     aff(ST("lb", 4, 3), L("col", 1, 3, 2), H(4), mix(0, (H(0), 8), (H(3), 8)))
     q = mix(16, (S, -16), (B0, 16))
-    aff(ST("lm", 0, 1), MI, 32, 128)
-    aff(ST("lm", 1, 2), L("col", 0, 2, 4), 1, mix(q, (HI, 32), (B1, 96), (K4, 16), (X2, 208)))
-    aff(ST("lm", 3, 1), X0, 208, mix(q, (MI, 32)))
-    aff(ST("lc", 0, 3), L("col", 8, 3), 1, mix(S, (I7, 8)))
+    ts(ST("lm", 0, 1), MI, 2, A.min, 32, A.mult)
+    aff(ST("lm", 2, 2), L("col", 0, 2, 4), 1, mix(q, (HI, 32), (B1, 96), (K4, 16), (X2, 208)))
+    aff(ST("lm", 4, 1), X0, 208, mix(q, (MI, 32)))
+    aff(ST("lc", 0, 3), L("bi", 0, 3), 2, mix(S, (I7, 8)))
     later = Q()
     ts(later, I, 6, A.is_ge)
-    aff(ST("lo", 0, 4), L("col", 16, 4), 1, mix(0, (I, 8), (later, -44), (S, 2)))
-    aff(ST("ly", 0, 2), L("col", 6, 2), 1, I)
-    aff(ST("ly", 1, 1), mix(0, (S, later)), mix(-193, (I, 15)), ST("ly", 1, 1))
-    q = mix(0, (I, 16), (later, 96), (S, 96))
-    aff(ST("la", 0, 4), L("col", 20, 4), 1, q)
-    aff(ST("la", 4, 2), L("col", 21, 2), 1, q)
+    aff(ST("lo", 0, 2), L("bi", 0, 2), 1, mix(0, (I, 8), (later, -44), (S, 2)))
+    aff(ST("lq", 0, 1), ST("lo", 1, 1))
+    pair = q = mix(0, (I, 16), (later, 96), (S, 96))
+    ts(ST("la", 0, 4), L("col", 20, 4), q, A.add, 478, A.min)
+    ts(ST("l0", 0, 2), L("col", 21, 2), q, A.add, 478, A.min)
     if REDO:
-        listed("l6", 0, 2, L("col", 21, 2), q, 383)
-    q = Q()
-    ts(q, I7, 5, A.min, 16, A.mult)
-    aff(ST("lk", 0, 2), L("col", 16, 2), 0, q)
-    aff(ST("lk", 2, 2), ST("lk", 0, 2), 1, 14)
-    aff(ST("lk", 4, 2), L("bi", 1, 2, 4), 1, mix(q, (S, 1), (HI, 2)))
-    aff(W("gc"), L("col", 8, 4), -2048, mix(0, (S, -2048)))
+        listed("l6", 0, 2, L("col", 21, 2), q, 382)
+    aff(ST("lk", 0, 2), L("nf", 6, 2), 2, 0)
+    aff(L("nf", 12, 2), W("ni"), 2, mix(1, (S, 1)))
+    plus(ST("lk", 2, 2), ST("lk", 0, 2), L("nf", 12, 2))
+    ts(W("cap"), L("bi", 2 * LATE, 2), I7, A.is_gt, 9000, A.mult)
+    iota(L("col", 24, 3), [[32, 3]], 82)
+    q = mix(14, (MI, 96), (HI, 16))
+    ts(ST("lv", 0, 3), L("col", 24, 3), mix(q, (B0, 14)), A.add, L("cap", 0, 1), A.min)
+    ts(ST("lw", 0, 3), L("col", 0, 3, 2), mix(q, (B0, 82)), A.add, L("cap", 1, 1), A.min)
+    aff(W("gc"), L("bi", 0, 4), -2 * FAR, mix(512, (S, -FAR)))
     aff(ST("lz", 0, 2), L("col", 0, 2, 2), 1, mix(I, (HI, 8), (S, 8)))
-    aff(ST("il", 0, 2), L("nf", 0, 2), 16, mix(1, (GR, 1), (X0, 304)))
-    if FREE:
-        aff(ST("l0", 0, 1), later, -47, mix(0, (twice, 8)))
-        q = mix(own, (S, -16))
-        aff(L("st", LISTS["lw"], 3, 2), L("col", 0, 3, 2), 1, mix(q, (S, 304)))
-        aff(L("st", LISTS["lw"] + 1, 3, 2), L("col", 1, 3, 2), 1, mix(304, (q, 1), (S, -304)))
-    for c, n in ((0, 4), (4, 12), (16, 16), (32, 12), (44, 8))[:4 + FREE]:
+    ts(L("nf", 16, 2), L("nf", 0, 2), 17, A.min, 16, A.mult)
+    aff(ST("il", 0, 2), L("nf", 16, 2), 1, mix(1, (GR, 1), (X0, 304)))
+    for c, n in ((0, 4), (4, 4), (8, 18), (26, 10), (36, 14)):
         cast(L("li", c, n), L("st", c, n))
     fill(L("gb", 0, 16), 0)
     fill(L("gb", 304, 16), 0)
-    fill(L("tb", 608, 208), 0)
     cast(L("pl", 0, 36), W("pgn"))
-    for m in range(4):
+    if FOUR:
+        cast(L("pl", 36, 36), W("pgm"))
+    for m in range(0 if FOUR else 4):
         cast(L("pl", 36, 36, 1, 32 * m, 32 * m + 32), L("pgn", 0, 36, 1, 32 * ((m + 1) % 4), 32 * ((m + 1) % 4) + 32))
     for c in range(4):
         iota(L("sw", 576 * c, 576), [[0, 576]], 0)
@@ -364,8 +378,31 @@ def rank_program(g, core, T, topo):
     do("g", lambda: g.affine_select(ap(W("et")), ap(W("one")), [[-1, 520]], A.is_equal, 0.0, 3, 4), [W("one")], [W("et")], 200 + 2.1 * 520)
     for b in range(4):
         quant("e", 128 * b, 128, "et", 3 - b)
-    q = mix(0, (B0, -8), (I, 8))
+    q = mix(0, (I, 8))
+    q = mix(q, (mix(0, (I4, 16), (B1, 64), (I, -8)), B0))
     listed("ul", 0, 10, L("bi", 0, 10), q, q)
+    iota(W("wt"), [[0, 72]], 8)
+    for d in range(-7, 8):
+        f0, n = max(0, -d), 8 - abs(d)
+        if d % 4:
+            a, b = VIEW[d % 8], VIEW[-d % 8]
+            iota(L("wt", 9 * f0 + d, n, 9), [[2, n]], 144 + 2 * f0 - SHIFT[a] + 256 * a + 1024 * b, -1)
+        elif d:
+            iota(L("wt", 9 * f0 + d, n, 9), [[4, n]], 145 + (1024 if d > 0 else 256), -1)
+    ts(L("wi", 0, 72), W("wt"), 15, A.bitwise_and)
+    ts(L("wf", 0, 72), L("wi", 0, 72), 0, A.is_equal, -8, A.mult)
+    ts(L("wf", 72, 72), L("wi", 0, 72), 15, A.is_equal, 2, A.mult)
+    tt(W("mtab"), L("wf", 0, 72), L("wf", 72, 72), A.add)
+    ts(L("wi", 72, 64), L("wt", 0, 64), 8, A.arith_shift_right, 3, A.bitwise_and)
+    ts(L("wi", 136, 64), L("wt", 0, 64), 10, A.arith_shift_right)
+    tt(L("nf", 14, 2), L("ab", 10, 2, 2), L("ab", 11, 2, 2), A.subtract)
+    aff(L("nf", 14, 2), L("nf", 14, 2), 288.0 / UP)
+    for k in range(2):
+        aff(L("wf", 144 + 64 * k, 64), L("wi", 72 + 64 * k, 64), L("nf", 14 + k, 1))
+    ends, keep = mix(0, (L("ab", 15, 1), -2.0 / UP)), mix(1, (L("ab", 15, 1), -1.0 / UP))
+    ts(L("l2", 0, 10), ST("lm", 0, 10), 15, A.add)
+    listed("l2", 10, 4, ST("lb", 4, 4), mix(0, (H(4), 15)))
+    listed("l2", 14, 2, L("bi", 10, 2, 2), pair, 383)
     quant("u", 0, 128, "ut")
     ul = L("ul", 0, 9)
     views = do("v", lambda: g.vector.tensor_copy(ap(W("Cr")).bitcast(dt.uint32), ap(W("Cu")).bitcast(dt.uint32).indirect(ap(ul))),
@@ -376,30 +413,38 @@ def rank_program(g, core, T, topo):
         x = "x%d" % t
         for c0, n in RUNS if t else ((0, 288),):
             quant(x, c0, n, x)
-            for i in range(8 if t else 0):
-                bank = (i + (8 if c0 else 0)) % (8 - STAY[t - 1])
-                mm(bank, n, "r", 2 * i, x, c0)
-                aff(L("sw", 288 * i + c0, n), PS(bank, 0, n), spread=True)
+            for i in range(3 if t else 0):
+                bank = (i + (3 if c0 else 0)) % (8 - STAY[t - 1])
+                mm(bank, n, "r", SHIFT[i], x, c0)
+                aff(L("sw", 288 * i + c0, n), PS(bank, 0, n), keep)
         if not t:
             mm(0, 288, "u", 0, x)
             aff(W("yt"), PS(0, 0, 288))
-            dmas([("y", T.sw[16 * h:16 * h + 1, :], T.yt[0:128:16, :], [W("yt")], [L("sw", 0, 2304, 1, 16 * h, 16 * h + 1)])
+            dmas([(LAYS[h], T.sw[16 * h:16 * h + 1, :], T.yt[0:128:16, :], [W("yt")], [L("sw", 0, 2304, 1, 16 * h, 16 * h + 1)])
                   for h in range(8)], 2400.0)
         dst = T.cores[rank ^ STEP[t]]
-        send(dst, [(W("Cp%d" % t), W("C" + x), u8), (W("Sp%d" % t), W("S" + x), ap)], "ca%d" % t, "cb%d" % t,
-             CODES + (0 if t else FIRST), 0 if t else FIRST)
+        c0 = RUNS[1][0] if t else 0
+        if t:
+            send(dst, [(L("Cp%d" % t, 0, c0), L("C" + x, 0, c0), u8)], "ce%d" % t, "cf%d" % t, CODES - 400.0)
+        send(dst, [(L("Cp%d" % t, c0, 288 - c0), L("C" + x, c0, 288 - c0), u8), (W("Sp%d" % t), W("S" + x), ap)], "ca%d" % t, "cb%d" % t,
+             CODES - AHEAD if t else CODES + FIRST, 0 if t else FIRST)
         for b in range(4):
             if b < 4 - STAY[t]:
                 mm(1 + b, 288, "e", 128 * b, x)
                 aff(W("f%d" % b), PS(1 + b, 0, 288))
             else:
                 mm(4 + b, 288, "e", 128 * b, x)
+                for c0, n in RUNS:
+                    if (t, b, c0) in PART:
+                        aff(L("f%d" % b, c0, n), PS(4 + b, c0, n))
 
     O = lambda name, k: L(name, k, 6, 8)
     run = lambda name, lo, n=6: L(name, lo, n, 16)
     at = lambda n: 96 * n + (96 if n < 4 else 256)
     R = lambda n, slot=None: L("cw", at(n), 96) if slot is None else run("cw", at(n) + slot)
-    SC = lambda n: L("cs", 480 + 96 * n, 96)
+    SC = lambda n, slot=None: L("cs", 96 + 96 * n, 96) if slot is None else run("cs", 96 + 96 * n + slot)
+    W1, W0, X10, X01, X11 = 512, 608, 704, 800, 896
+    step = lambda t, k: SC((k + 2 - t % 2) // 2 - 1, 14 * ((k + t) % 2))
 
     def blocks(out, o, a, b):
         ts(a, o, GR, A.is_lt, 2304, A.mult)
@@ -407,95 +452,93 @@ def rank_program(g, core, T, topo):
         tt(out, a, b, A.add)
 
     def prepare(t):
-        par, n, da = t % 2, 4 - t // 2, "da%d" % (t % 2)
+        par, n, da = t % 2, 4, "da%d" % (t % 2)
         blocks(L("ob", 0, 48), L("o", 0, 48), L("oa", 0, 48), L("oa", 48, 48))
         tt(L("co", 16, 32), L("o", par + 1, 32, 2), L("o", par, 32, 2), A.subtract)
-        sums(W("cp"), W("two8"), L("o", par, 64))
+        sums(W("cp"), W("two8"), L("o", par, 80))
         if par:
             fill(L("co", 19, 8, 4), 0)
             aff(O("cp", 7), O("o", 7), 1, 64)
-            aff(R(-1, 14), R(0, 0))
+            aff(SC(-1, 14), SC(0, 0))
         cast(W("uc"), W("cp"), W("lu"))
-        for a, b in ((0, 1), (1, n)) if t or not FREE else ((1, 2), (2, n)):
+        for a, b in ((0, 1), (1, n)):
             aff(L("ra", 96 * a, 96 * (b - a)), W("dtab"), idx=L("uc", 6 * a, 6 * (b - a)))
             turn(L(da, 96 * a, 96 * (b - a)), L("ra", 96 * a, 96 * (b - a)))
-        if t or not FREE:
-            for w in range(2):
-                tt(L("bw", 6 * w, 6), R(-1, 14) if par else W("j0"), O("ob", par + w), A.add)
-            cast(W("ub"), W("bw"), L("ld", 0, 1))
-            aff(run(da, 15), O("ob", 2 + par))
-        else:
-            ts(W("u3"), W("o"), 64, A.add, idx=L("l0", 0, 1))
-            aff(L("g4", 0, 192), W("dtab"), idx=L("u3", 0, 12))
-            turn(L("da1", 0, 192), L("g4", 0, 192))
-            aff(W("g1"), W("tw"), idx=L("lw", 0, 6))
-            for w in range(2):
-                scan(L("cs", 96 * w, 96), L("da1", 96 * w, 96), W("g1"))
-            ts(W("ub"), L("cs", 8, 184), 144, A.add, idx=L("ls", 2, 1))
-            for w in range(2):
-                aff(run("da1", 15 + 96 * w), O("ob", 2))
+        for w in range(t > 0, 2):
+            tt(L("bw", 6 * w, 6), SC(0, 0) if par else W("j0"), O("ob", par + w), A.add)
+        cast(W("ub"), W("bw"), L("ld", 0, 1))
+        aff(run(da, 15), O("ob", 2 + par))
         aff(run(da, 111), O("ob", 4 + par))
-        if t < 2:
-            aff(run(da, 303), O("o288", 7))
-        for w in range(2):
-            aff(L("g0", 96 * w, 96), W("tab") if t or not FREE else L("tab", 2304, 288), idx=L("ub", 6 * w, 6))
+        for w in range(t > 0, 2):
+            aff(L("g0", 96 * w, 96), W("tab"), idx=L("ub", 6 * w, 6))
             turn(R(4 + w), L("g0", 96 * w, 96))
-            scan(L("cs", 96 * w, 96), L(da, 0, 96) if t or not FREE else L("da1", 96 - 96 * w, 96), R(4 + w))
+            scan(L("cs", W1, 96) if w else SC(0), L(da, 0, 96), R(4 + w))
         if not t:
-            cast(W("u1"), L("cs", 0, 96), L("ls", 0, 1))
+            cast(W("u1"), SC(0), L("ls", 0, 1))
+            pick(L("g4", 0, 96), W("tab"), L("u1", 0, 6), CUT0)
+            turn(R(6), L("g4", 0, 96))
+            scan(SC(1), L(da, 96, 96), R(6))
         K = lambda k: L("co", 48 + 8 * k, 6)
+        was = lambda k: step(max(t - 1, 0), par + k)
         tt(K(2), O("ob", 3 + par), O("ob", 2 + par), A.subtract)
         tt(K(6), O("ob", 5 + par), O("ob", 4 + par), A.subtract)
-        for w in range(2):
-            tt(run("cs", 96 * w + 7), run("cs", 96 * w + 15), K(2), A.add)
-        for v in range(2):
-            cast(L("ue", 16 * v, 16), L("cs", 8 - 8 * v, 184), L("ls", 2, 1))
-            for a, b in ((0, 2),) if t or v else ((0, 1), (1, 2)):
-                c, n = 192 * v + 96 * a, 96 * (b - a)
-                pick(L("g4", c, n), W("tab"), L("ue", 16 * v + 6 * a, n // 16) if t + v + a else L("u1", 0, 6), 0 if t + v + a else CUT0)
-                turn(L("cw", at(6) + c, n), L("g4", c, n))
-            for w in range(2):
-                scan(L("cs", 192 + 192 * v + 96 * w, 96), L(da, 96, 96), R(6 + 2 * v + w))
-        X = lambda w, v: run("cs", 207 + 192 * v + 96 * w)
-        tt(K(0), R(5, 0), R(4, 0), A.subtract)
-        tt(K(1), run("cs", 111), run("cs", 15), A.subtract)
-        aff(K(3), run("cs", 15))
-        tt(K(5), X(1, 0), X(0, 0), A.subtract)
-        tt(L("co", 112, 12), run("cs", 399, 12), run("cs", 207, 12), A.subtract)
+        tt(run("cs", W0 + 7), was(1), O("ob", 3 + par), A.add)
+        tt(run("cs", W1 + 7), run("cs", W1 + 15), K(2), A.add)
+        cast(L("ue", 0, 16), L("cs", W1, 96), L("ls", 0, 1))
+        cast(L("ue", 16, 16), L("cs", W1, 184), L("ls", 2, 1))
+        for c, n, lo in ((96, 96, 0), (192, 192, 16)):
+            aff(L("g4", c, n), W("tab"), idx=L("ue", lo, n // 16))
+            turn(L("cw", at(6) + c, n), L("g4", c, n))
+        for n, c in ((7, X10), (8, X11), (9, X01)):
+            scan(L("cs", c, 96), L(da, 96, 96), R(n))
+        tt(K(0), run("cs", W1), was(0), A.subtract)
+        tt(K(1), run("cs", W1 + 14), was(1), A.subtract)
+        if t:
+            tt(K(3), was(1), O("ob", 2 + par), A.add)
+            tt(run("cs", W0 + 15), was(3), O("ob", 4 + par), A.add)
+        else:
+            aff(K(3), SC(0, 15))
+            aff(run("cs", W0 + 15), SC(1, 15))
+        tt(K(5), run("cs", X10 + 15), run("cs", W0 + 15), A.subtract)
+        tt(L("co", 112, 12), run("cs", X01 + 15, 12), run("cs", W0 + 15, 12), A.subtract)
         tt(K(4), L("co", 118, 6), K(8), A.subtract)
-        aff(K(7), X(0, 0))
+        aff(K(7), run("cs", W0 + 15) if t else SC(1, 15))
         aff(W("cf"), L("co", 56, 64), idx=L("lc", 0, 3))
         if par:
             fill(run(da, 207), 288 * 8 + 144)
         else:
             tt(L("co", 0, 6), O("ob", 7), O("ob", 6), A.subtract)
 
-    def look(n, par, more_=True):
-        pick(W("g%d" % n), W("tab"), L("u%d" % n, 0, 6), CUT if n > 1 else 0)
+    def look(n, par, more_=True, cut=0):
+        pick(W("g%d" % n), W("tab"), L("u%d" % n, 0, 6), cut if n > 1 else 0)
         turn(R(n), W("g%d" % n))
         if more_:
             scan(SC(n), L("da%d" % par, 96 * n, 96), R(n))
         if n == 2:
             cast(W("u3"), SC(n), L("ls", 0, 1))
 
-    def score_lists(t, which):
-        for n in which:
-            aff(R(n, 14), run("cs", 494 + 96 * n))
-        aff(W("sg"), W("o288"), idx=L("lo", 2 * (t % 2), 2))
-        if not t and REDO:
-            tt(W("sa"), L("cw", 0, 384), W("sg"), A.add, idx=W("l6"))
-            cast(W("s0"), W("sa"))
-        tt(L("cs", 864, 32), L("cw", 0, 640), W("sg"), A.add, idx=L("la", (4, 2, 0)[t], 2))
-        if t == 1:
-            cast(W("so"), L("cs", 864, 32))
+    def score_lists(t):
+        if t:
+            aff(SC(3, 0), R(3, 0) if t == 1 else SC(3, 14))
+        if t:
+            aff(W("sg"), W("da%d" % (t % 2)), 1, 144, idx=L("l2", 14, 2))
+            cast(W("um"), W("cp"), L("lq", 0, 1))
+            aff(W("mp"), W("mtab"), 1, ends, idx=L("um", 0, 12))
+            turn(W("pm"), W("mp"))
         else:
-            cast(W("so"), L("cs", 768, 160), W("ly"))
+            aff(W("sg"), W("o"), 288, 144, idx=L("lo", 0, 2))
+        if not t and REDO:
+            tt(W("sa"), L("cs", 0, 384), W("sg"), A.add, idx=W("l6"))
+            cast(W("s0"), W("sa"))
+        tt(L("cs", 480, 32), L("cs", 0, 480), W("sg"), A.add, idx=L("la", 4 - 2 * t, 2) if t else W("l0"))
+        cast(W("so"), L("cs", 480, 32))
 
     early = len(ops)
     products(0)
-    rows = tt(L("tab", 2288, 320), W("raw"), W("idm"), A.add, idx=W("wl"))
-    if RAW < 8:
-        cast(L("tab", 2288, 320, 1, 64, 128), L("tab", 2288, 320, 1, 0, 64))
+    for c in (0, 160):
+        aff(L("tab", 2288 + c, 160), W("raw"), 1, lose, idx=L("wl", c // 16, 10))
+        if RAW < 8:
+            aff(L("tab", 2288 + c, 160, 1, 64, 128), L("tab", 2288 + c, 160, 1, 0, 64))
     dmas([("y", u8(W("Cw")), T.wc[:, :], [], [W("Cw")]), ("y", T.Sw[:, :], T.ws[:, :], [], [W("Sw")]),
           ("y", T.vt[:, :], T.v[:, :], [], [W("vt")])], 5000.0, range(early + 3, early + 11))
     turn(L("tw", 0, 288), L("tab", 2304, 288))
@@ -503,72 +546,82 @@ def rank_program(g, core, T, topo):
     aff(L("o", 0, 48), W("tw"), 1, 144, idx=L("ol_", 0, 3))
     for r in range(4):
         aff(L("tab", 288 * r, 288), L("tab", 2304, 288), 1, L("bias", r, 1), idx=L("pl", 18 * r, 18))
-        for h in (0, 64):
-            aff(L("tab", 288 * (4 + r), 288, 1, h, h + 64), L("tab", 288 * r, 288, 1, 64 - h, 128 - h))
-    aff(W("o288"), W("o"), 288, 144)
+        halves = [(L("tab", 288 * (4 + r), 288, 1, h, h + 64), L("tab", 288 * r, 288, 1, 64 - h, 128 - h)) for h in (0, 64)]
+        if r < SWAP:
+            dmas([("y", ap(to), ap(of), [of], [to]) for to, of in halves], 2500.0)
+        for to, of in halves if r >= SWAP else ():
+            aff(to, of)
     prepare(0)
     aff(run("da0", 207), O("ob", 6))
-    cast(W("u2"), L("cs", 192, 96), L("ls", 0, 1))
-    for n, c in ((0, 0), (1, 192)):
-        aff(R(n, 0), R(4 + 2 * n, 0))
-        aff(R(n, 14), run("cs", c + 14))
+    cast(W("u2"), SC(1), L("ls", 0, 1))
     for n in (2, 3):
         look(n, 0)
-    score_lists(0, (2,))
+    score_lists(0)
     quant("v", 0, 128, "vt")
 
     for t in range(3):
         dst, par = T.cores[rank ^ STEP[t]], t % 2
         def compare(c, so):
-            aff(L("eb", 16 * c, 96), W("sw"), idx=L(so, 16 + c, 6))
-            tt(L("rr", 16 + 16 * c, 96), W("sw"), L("eb", 16 * c, 96), A.is_gt, idx=L(so, c, 6))
+            sw = L("sw", 0, 864 if t else 2304)
+            aff(L("eb", 16 * c, 96), sw, idx=L(so, 16 + c, 6))
+            tt(L("rr", 16 + 16 * c, 96), sw, L("eb", 16 * c, 96), A.is_gt, idx=L(so, c, 6))
 
         for c in (0, 6):
             compare(c, "so" if t or not REDO else "s0")
         for c, n in ((16, 96), (112, 96)) if TWO else ((16, 192),):
-            turn(L("rt", c, n), L("rr", c, n))
-        tt(W("s3"), L("rt", 0, 208), W("cf"), A.mult, idx=L("lb", 0, 3))
-        aff(W("k4"), L("rt", 0, 208), idx=L("lb", 4, 3))
+            turn(L("rq" if t else "rt", c, n), L("rr", c, n))
+            if t:
+                scan(L("rt", c, n), L("pm", c - 16, n), L("rq", c, n))
+        lm, lb = ("l2", lambda c: L("l2", 6 + c, 3)) if t else ("lm", lambda c: L("lb", c, 3))
+        tt(W("s3"), L("rt", 0, 208), W("cf"), A.mult, idx=lb(0))
+        aff(W("k4"), L("rt", 0, 208), idx=lb(4))
         if not t and REDO:
             compare(6, "so")
             turn(L("rt", 112, 96), L("rr", 112, 96))
+        if t:
+            turn(L("rr", 16, 192), L("rt", 16, 192))
         turn(L("rt", 208, 224), W("rr"))
         sums(W("s3o"), W("k4"), W("s3"))
         cast(L("u2", 0, 6), L("s3o", 7, 6, 8))
         cast(L("u1", 0, 6), L("s3o", 2, 6, 8))
-        tt(W("mm"), W("rt"), L("co", 0, 64), A.mult, idx=L("lm", 0, 4))
+        tt(L("mm", 16, 48), W("rt"), L("co", 16, 48), A.mult, idx=L(lm, 2, 3))
         if not par:
+            tt(L("mm", 0, 16), L("rt", 128, 80), L("co", 0, 16), A.mult, idx=L(lm, 0, 1))
             tt(run("da0", 207), L("mm", 0, 6), O("ob", 6), A.add)
         first, second = L("o", par, 32, 2), L("o", par + 1, 32, 2)
         tt(first, first, L("mm", 16, 32), A.add)
         tt(second, second, L("mm", 16, 32), A.subtract)
-        tt(R(0, 0), L("mm", 48, 6), R(4, 0), A.add)
-        tt(R(0, 14), L("mm", 56, 6), run("cs", 14), A.add)
-        for c in range(4):
-            act(L("mk", 64 * c, 64), L("o", 0, 64), AF.Abs, 2048, L("gc", c, 1))
-        for k in range(8):
+        for e in (1, 0) if t == 2 else (0, 1):
+            tt(SC(0, 14 * e), L("mm", 48 + 8 * e, 6), step(max(t - 1, 0), par + e), A.add)
+        aff(W("ok"), L("o", 0, 48), FAR)
+        for n in (1, 2, 3):
+            look(n, par, n < 3 or t == 1, CUT * (t > 0 and n in CUTS))
+            if n == LATE - 1:
+                tt(W("vk"), L("cs", 0, 96 * LATE + 96), W("ok"), A.add, idx=L("lw" if par else "lv", 0, 3))
+                for c in range(4):
+                    act(L("mk", 48 * c, 48), W("vk"), AF.Abs, 1, L("gc", c, 1))
+        for k in range(2 * LATE + par, 8):
             n, e = (k + 2 - par) // 2 - 1, (k + par) % 2
-            if n > 0 and not e:
-                look(n, par, n == 2 or t == 1 or t + n == 1)
-            which = 2 if k == 7 or (n > 0 and e) else e
-            tt(L("mk", k, 32, 8), R(n), L("mk", k, 32, 8), A.add, idx=L("lk", 2 * which, 2))
-        scan(W("fin"), W("anew"), W("mk"), A.add, A.min)
+            tt(L("mk", k, 32, 8), R(n), L("mk", k, 32, 8), A.add, idx=L("lk", 2 if k == 7 or e else 0, 2))
+        scan(W("fin"), W("anew"), L("mk", 0, 192), A.add, A.min)
         for to, of, n, slot in ((64, 0, 64, 6), (0, 64, 64, 6), (0, 32, 32, 5), (32, 0, 32, 5), (64, 32, 32, 5), (96, 0, 32, 5)):
-            aff(L("fin", slot, 32, 8, to, to + n), L("fin", 7, 32, 8, of, of + n))
+            aff(L("fin", slot, 24, 8, to, to + n), L("fin", 7, 24, 8, of, of + n))
         al, bl, ll = "al%d" % t, "bl%d" % t, "ll%d" % t
-        ts(W(al), W("fin"), 144, A.add, idx=W("lf"))
+        ts(W(al), W("fin"), 144 - 512, A.add, idx=W("lf"))
         send(dst, [(W(ll), L(al, 0, 18), ap)], "la%d" % t, "lb%d" % t)
         aff(L("gb", 16, 288), L("tab", 2304, 288), idx=L(al, 0, 18))
         turn(L("tb", 0, 288), L("gb", 16, 288))
         turn(L("tb", 288, 320), W("gb"))
         ts(W(bl), W("tb"), 144, A.add, idx=W("il"))
         for b in range(4):
-            mm(2 + b, 288, "e", 128 * b, "p%d" % t)
-            aff(W("d%d" % b), PS(2 + b, 0, 288))
+            bank = b + min(2, 4 - STAY[t])
+            mm(bank, 288, "e", 128 * b, "p%d" % t)
+            aff(W("d%d" % b), PS(bank, 0, 288))
         if t < 2:
-            aff(W("o288"), W("o"), 288, 144)
-            score_lists(t + 1, (1, 2))
+            for k in range(0 if t else 2):
+                tt(L("dtab", 0, 64), L("dtab", 0, 64), L("wf", 144 + 64 * k, 64), A.add)
             prepare(t + 1)
+            score_lists(t + 1)
         else:
             aff(W("ou"), L("o", 0, 64), idx=W("lz"))
             turn(W("ot"), W("ou"))
@@ -580,13 +633,13 @@ def rank_program(g, core, T, topo):
                 aff(L(z, 4 * c0 + b, n, 4), W("d%d" % b), idx=L(ll, c0 // 16, n // 16))
             quant(z, c0, n, z)
             for b in range(4):
-                bank = (1 + b, ((5, 6, 0, 1) if STAY[t] == 1 else (5, 0, 1, 2))[b])[h]
+                bank = (1 + b + 4 * h) % (8 - STAY[t])
                 mm(bank, n, "w", 128 * b, z, c0)
                 aff(L("r%d" % b, c0, n), PS(bank, 0, n), 0.03125)
         for c0, n in RUNS:
             i = L(bl, c0 // 16, n // 16)
             for b in range(4):
-                if b < 4 - STAY[t]:
+                if b < 4 - STAY[t] or (t, b, c0) in PART:
                     tt(L(x, 4 * c0 + b, n, 4), W("r%d" % b), L("f%d" % b, c0, n), A.add, idx=i)
                 else:
                     aff(L("r4", 288 * (3 - b) + c0, n), W("r%d" % b), idx=i)
@@ -673,9 +726,9 @@ def rank_program(g, core, T, topo):
                     last[q] = i
                     at, dur = max(at, free.get(q, 0.0)), o["dur"][q] if o["q"] == "f" else o["dur"]
                     if o["lat"]:
-                        free[q], done[i] = at + dur, at + (way if o["lat"] == LIST else o["lat"])
+                        free[q], done[i] = at + dur, at + (way if o["lat"] == LIST else o["lat"] * each)
                     else:
-                        free[q] = done[i] = at + dur * slow + each
+                        free[q] = done[i] = at + dur * slow
                 both += max(done)
                 i = done.index(max(done))
                 while i != -1:
@@ -699,40 +752,49 @@ def rank_program(g, core, T, topo):
             favour[:] = [float(other[i]) if near[i] and abs(shake[i]) < 50.0 else f for i, f in enumerate(kept[3])]
         order, on = sorted(range(N), key=lambda i: (kept[0][i], i)), kept[2]
         hold = [{q: [((o["dur"][q] if o["q"] == "f" else o["dur"]) if o["lat"] or not q else
-                      (o["dur"][q] if o["q"] == "f" else o["dur"]) * slow + each) if o["q"] == q or (o["q"] == "f" and q in o["dur"]) else 0.0
+                      (o["dur"][q] if o["q"] == "f" else o["dur"]) * slow) if o["q"] == q or (o["q"] == "f" and q in o["dur"]) else 0.0
                      for o in ops] for q in list(queue) + [None]} for wake, slow, each, way in CASES]
-        late = [[(way if o["lat"] == LIST else o["lat"]) if o["q"] else 0.0 for o in ops] for wake, slow, each, way in CASES]
+        late = [[(way if o["lat"] == LIST else o["lat"] * each) if o["q"] else 0.0 for o in ops] for wake, slow, each, way in CASES]
 
         can = [sorted(o["dur"]) if o["q"] == "f" else [o["q"]] for o in ops]
 
-        def inside(part, on, c, done, free, out, outq):
-            wake, why, last, free, end, at_end, all_ = CASES[c][0], {}, {}, dict(free), 0.0, -1, 0.0
-            for i in part:
-                q, at, by = on[i], 0.0, -1
-                for m in pre[i]:
-                    if done[m] + wake > at:
-                        at, by = done[m] + wake, m
-                if q is None:
-                    d = at - wake
-                else:
-                    if free[q] > at:
-                        at, by = free[q], -2 - last.get(q, -1)
-                    last[q] = i
-                    free[q] = at + hold[c][q][i]
-                    d = at + late[c][i] if late[c][i] else free[q]
-                done[i], why[i] = d, by
-                all_ += d
-                if d + out[i] > end:
-                    end, at_end = d + out[i], i
+        def inside(part, on, c, a, limit, done, why, marks, out, outq, least):
+            wake, hold_, late_, a = CASES[c][0], hold[c], late[c], a // 8
+            done, why, marks = done[:], dict(why), marks[:a + 1]
+            free, last, end, at_end, all_ = marks[a]
+            free, last = dict(free), dict(last)
+            for n in range(8 * a, len(part), 8):
+                for i in part[n:n + 8]:
+                    q, at, by = on[i], -1e9, -1
+                    for m in pre[i]:
+                        if done[m] > at:
+                            at, by = done[m], m
+                    if q is None:
+                        d = at
+                    else:
+                        at += wake
+                        if free[q] > at:
+                            at, by = free[q], -2 - last[q]
+                        last[q] = i
+                        d = free[q] = at + hold_[q][i]
+                        if late_[i]:
+                            d = at + late_[i]
+                    if d + least[i] > limit:
+                        return None
+                    done[i], why[i] = d, by
+                    all_ += d
+                    if d + out[i] > end:
+                        end, at_end = d + out[i], i
+                marks.append((dict(free), dict(last), end, at_end, all_))
             for q in free:
                 if free[q] + outq[q] > end:
-                    end, at_end = free[q] + outq[q], last.get(q, -1)
+                    end, at_end = free[q] + outq[q], last[q]
             tight, i = [], at_end
             while i in why:
                 if why[i] < -1:
                     tight.append((i, -2 - why[i]))
                 i = why[i] if why[i] >= -1 else -2 - why[i]
-            return end + EARLY * all_ / len(part), tight
+            return end + EARLY * all_ / len(part), tight, end, done, why, marks
 
         for WIDE, ANEW, POLISH in SWEEPS:
             for c0 in range(0, N - WIDE // 2, WIDE // 2):
@@ -752,14 +814,27 @@ def rank_program(g, core, T, topo):
                         tail[i] = after - wake if q is None else max((late[c][i] or hold[c][q][i]) + after, hold[c][q][i] + outq[q])
                         if q:
                             outq[q] = tail[i]
-                    state.append((done, free, {i: max([0.0] + [wake + tail[k] for k in nxt[i] if k in tail]) for i in part}, outq))
+                    out, least = {i: max([0.0] + [wake + tail[k] for k in nxt[i] if k in tail]) for i in part}, {}
+                    for i in reversed(part):
+                        least[i] = max([out[i]] + [least[k] + (wake + (late[c][k] or min(hold[c][q][k] for q in can[k])) if on[k] else 0.0)
+                                                   for k in nxt[i] if k in least])
+                    state.append([done, {}, [(free, {q: -1 for q in queue}, 0.0, -1, 0.0)], out, outq, least, 1e18])
 
-                def both(part, on):
-                    got = [inside(part, on, c, *state[c]) for c in range(len(CASES))]
+                def both(part, on, a, most):
+                    got, room = [], most - took + ROOM
+                    for c in range(len(CASES)):
+                        got.append(inside(part, on, c, a, state[c][6] + room, *state[c][:6]))
+                        if got[-1] is None:
+                            return None
+                    if sum(x[0] for x in got) > most:
+                        return None
+                    for c, x in enumerate(got):
+                        state[c][:3], state[c][6] = x[3:], x[2]
                     return sum(x[0] for x in got), [p for x in got for p in x[1]]
 
-                took, tight = both(part, on)
-                done, free, out, outq = state[0]
+                took = 0.0
+                took, tight = both(part, on, 0, 1e18)
+                done, free, out, outq = state[0][0], state[0][2][0][0], state[0][3], state[0][4]
                 wake, here, way = CASES[0][0], set(part), {}
                 for i in reversed(part):
                     way[i] = (late[0][i] or hold[0][on[i]][i]) + max([out[i], outq.get(on[i], 0.0)] + [wake + way[k] for k in nxt[i] if k in here])
@@ -767,7 +842,7 @@ def rank_program(g, core, T, topo):
                 inner = [{i: [m for m in x[i] if m in here] for i in part} for x in (pre, nxt)]
 
                 def lay(key, to, lean, back):
-                    before, after, from_, busy = inner[back], inner[1 - back], (into, out)[back], {q: [(0.0, (free, outq)[back][q]), (1e18, 1e18)] for q in queue}
+                    before, after, from_, gaps = inner[back], inner[1 - back], (into, out)[back], {q: [((free, outq)[back][q], 1e18)] for q in queue}
                     left, start, end = {i: len(before[i]) for i in part}, {}, {}
                     ready = [(key[i], i) for i in part if not left[i]]
                     while ready:
@@ -783,16 +858,20 @@ def rank_program(g, core, T, topo):
                             for q in (can[i] if lean is not None else [to[i]]):
                                 dur = hold[0][q][i]
                                 at = at0 + (late[0][i] - dur if back and late[0][i] else 0.0)
-                                for c, (a, b) in enumerate(busy[q]):
-                                    if b > at:
-                                        if a >= at + dur:
-                                            break
-                                        at = b
+                                gap = gaps[q]
+                                c = len(gap) - 1
+                                while c and gap[c - 1][1] >= at + dur:
+                                    c -= 1
+                                while gap[c][1] - gap[c][0] < dur:
+                                    c += 1
+                                if gap[c][0] > at:
+                                    at = gap[c][0]
                                 worth = at + dur + (lean[i] if q == "v" and lean is not None else 0.0)
                                 if pick_ is None or worth < pick_[0]:
                                     pick_ = (worth, at, dur, q, c)
                             worth, at, dur, to[i], c = pick_
-                            busy[to[i]].insert(c, (at, at + dur))
+                            a, b = gaps[to[i]][c]
+                            gaps[to[i]][c:c + 1] = [x for x in ((a, at), (at + dur, b)) if x[1] - x[0] >= 59.0]
                             start[i], end[i] = at, at + (dur if back else late[0][i] or dur)
                         for k in after[i]:
                             left[k] -= 1
@@ -807,11 +886,11 @@ def rank_program(g, core, T, topo):
                     for again in range(2):
                         start, end = lay(key, to, lean if n % 3 or not again else None, 0)
                         new = sorted(part, key=lambda i: (start[i], i))
-                        t2, w2 = both(new, to)
+                        got = both(new, to, 0, took)
                         key = lay({i: -end[i] for i in part}, dict(to), None, 1)[1]
                         key = {i: i - 1e9 if i < loads else -key[i] for i in part}
-                        if t2 <= took:
-                            part, on, took, tight, seed = new, dict(to), t2, w2, key
+                        if got:
+                            part, on, took, tight, seed = new, dict(to), got[0], got[1], key
                 where, best, M_ = {m: n for n, m in enumerate(part)}, (took, part, on), len(part)
                 for n in range(POLISH):
                     luck = dice.rand(6)
@@ -822,7 +901,9 @@ def rank_program(g, core, T, topo):
                         i, k = tight[int(luck[1] * len(tight))]
                     new, to, how = part, on, int(luck[3] * 3)
                     if how == 0 and ops[k]["q"] == "f":
-                        to = dict(on)
+                        if k not in where:
+                            continue
+                        to, a = dict(on), where[k]
                         to[k] = sorted(ops[k]["dur"])[int(luck[4] * len(ops[k]["dur"]))]
                     else:
                         up, far = how == 1, (0, 0, 3, 10, 30)[int(luck[4] * 5)]
@@ -835,9 +916,9 @@ def rank_program(g, core, T, topo):
                         if todo or (i in move and k in move) or min(move) < loads:
                             continue
                         new = part[:a] + [m for m in part[a:b + 1] if (m in move) == up] + [m for m in part[a:b + 1] if (m in move) != up] + part[b + 1:]
-                    t2, w2 = both(new, to)
-                    if t2 <= took - HEAT * (1.0 - n / POLISH) * math.log(1.0 - luck[5]):
-                        part, on, took, tight = new, to, t2, w2
+                    got = both(new, to, a, took - HEAT * (1.0 - n / POLISH) * math.log(1.0 - luck[5]))
+                    if got:
+                        part, on, took, tight = new, to, got[0], got[1]
                         where = {m: c for c, m in enumerate(part)}
                         if took <= best[0]:
                             best = (took, part, on)

import math
import numpy
from concourse.mybir import dt, AluOpType, ActivationFunctionType

STEP = (4, 1, 2)
HALF = ((0, 160), (160, 128))
RUNS = HALF
LAST, YW, OW, REDO, RAW, CUT, TWO = 4, 1, 1, 1, 4, 4, 1
CUTS = ()
CUT0, ENDS, SWAP, FOUR = 0, 0, 0, 0
LAYS = "yysyysyy"
LATE = 3
SHIFT = (0, 2, 6)
VIEW = (0, 0, 1, 0, 0, 2, 2, 1)
FAR = 4096
PART = ((0, 1, 0), (1, 1, 0), (2, 1, 0))
STAY = (3, 3, 3)
UP, LOW, OUT = 1024, -768, -4096

BF, F32, I32, U16 = "bfloat16", "float32", "int32", "uint16"
SCRATCH, PLACE = {}, {}
for _d, _names in (
        (BF, "one 520 et 520 ut 512 vt 512 tab 2608 tw 608 dtab 72 ra 384 da0 384 da1 384 tb 608 anew 192 "
             "g0 192 g1 96 g2 96 g3 96 g4 384 cw 1216 gb 320 rr 224 rt 464 rq 208 mp 192 pm 192 mtab 72 o 96 cp 80 two8 80 "
             "f0 288 f1 288 f2 288 f3 288 d0 288 d1 288 d2 288 d3 288 x0 1152 x1 1152 x2 1152 x3 1152 z0 1152 z1 1152 z2 1152"),
        (F32, "pf 96 bias 4 ob 48 oa 96 sa 32 mm 64 j0 6 bw 16 st 52 co 128 cf 48 mk 192 s3 48 k4 48 s3o 48 sg 32 cs 992 gc 4 ou 32 "
              "sw 2304 eb 256 ot 32 yt 288 r0 288 r1 288 r2 288 r3 288 r4 1152 ab 40 nf 18 bi 20 col 32 "
              "fin 192 ok 48 vk 48 cap 2 wf 272"),
        (I32, "pi 28 raw 288 rank0 26 pgn 36 pgm 36 ni 2 wt 72 wi 200"),
        (U16, "l2 16 um 16 wl 20 pl 72 ol_ 4 ul 10 uc 32 ub 16 ue 32 u1 16 u2 16 u3 16 so 32 s0 32 li 52 l6 2 "
              "ls 4 al0 32 al1 32 al2 32 bl0 32 bl1 32 bl2 32 ll0 18 ll1 18 ll2 18")):
    _w = _names.split()
    for _n, _c in zip(_w[0::2], _w[1::2]):
        if _d != BF and _n[:2] not in ("ra", "pg", "ll", "al", "sw", "eb", "ot", "yt", "r0", "r1", "r2", "r3", "r4"):
            _at = SCRATCH.get("all" + _d, ("", [0, 0]))[1][1]
            SCRATCH["all" + _d] = ("sbuf", [128, _at + (int(_c) + 15) // 16 * 16], _d)
            PLACE[_n] = ("all" + _d, _at, int(_c))
        else:
            SCRATCH[_n] = ("sbuf", [128, int(_c)], _d)
LISTS = dict(ld=0, lu=2, lo=4, l0=6, lm=8, lb=14, lc=22, lk=26, lf=30, lv=32, lw=36, la=40, lq=44, lz=46, il=48)
for _n, _c in LISTS.items():
    PLACE[_n] = (PLACE["li"][0], PLACE["li"][1] + _c, 2)
for _n, _c in (("e", 512), ("u", 128), ("r", 144), ("v", 128), ("w", 512)) + tuple(
        (_m, 288) for _m in ("x0", "x1", "x2", "x3", "p0", "p1", "p2", "z0", "z1", "z2")):
    SCRATCH["C" + _n], SCRATCH["S" + _n] = ("sbuf", [128, _c], "float8_e4m3fn_x4"), ("sbuf", [128, _c], "uint8")
SCRATCH["ps"] = ("psum", [128, 4096], F32)
SEMAPHORES = ["vq_", "sq_", "tq_", "gq_"] + ["dm%d" % i for i in range(24)] + [
    n + str(t) for t in range(3) for n in ("ca", "cb", "ce", "cf", "la", "lb")]
AHEAD = 1000.0
ORDER = []
INFO = {}
CASES = ((155.0, 1.0, 1.0, 2500.0), (150.0, 1.2, 1.15, 2700.0), (200.0, 0.95, 1.1, 2900.0))
LOOSE, EARLY, HEAT, ROOM = 0.2, 0.03, 15.0, 60.0
SWEEPS = ((330, 150, 800), (200, 150, 1500), (140, 100, 1500), (260, 100, 1500), (100, 80, 1500), (180, 100, 1500), (70, 60, 1200),
          (130, 60, 1500))
TRIES, SEED = 12, 7
WAKE = 140.0
CODES, LIST, COLUMN = 6200.0, 2800.0, 0.75
FIRST, ISSUE = 1000.0, 200.0
FAVOUR = 100.0


def rank_program(g, core, T, topo):
    rank = T.rank_of(core)
    if rank is None:
        return
    A, AF = AluOpType, ActivationFunctionType
    queue = {"v": g.vector, "s": g.scalar, "t": g.tensor, "g": g, "y": g.sync}
    ops, recs = [], {}

    def L(name, lo, n, st=1, p0=0, p1=128):
        name, at = PLACE.get(name, (name, 0))[:2]
        return (name, at + lo, at + lo + st * (n - 1) + 1, st, p0, p1)

    def W(name):
        return L(name, 0, PLACE[name][2] if name in PLACE else SCRATCH[name][1][1])

    def PS(bank, lo, n, st=1):
        return L("ps", 512 * bank + lo, n, st)

    def ap(v, idx=None):
        name, lo, hi, st, p0, p1 = v
        a = T[name][p0:p1, lo:hi] if st == 1 else T[name][p0:p1, lo:hi:st]
        return a.indirect(ap(idx)) if idx else a

    def u8(v):
        return ap(v).bitcast(dt.uint8)

    def clash(a, b):
        if a[0] == "ps":
            return a[1] // 512 == b[1] // 512
        if a[1] >= b[2] or b[1] >= a[2] or a[4] >= b[5] or b[4] >= a[5]:
            return False
        return (a[1] - b[1]) % math.gcd(a[3], b[3]) == 0

    def rec(q, call, reads, writes, dur, sem, inc=1, lat=0.0, group=None):
        n, wait = len(ops), set()
        for acc, w in [(r, False) for r in reads] + [(r, True) for r in writes]:
            for m, w2, acc2 in recs.get(acc[0], []):
                bank = acc[0] == "ps" and (ops[m]["q"] != q or q == "f")
                if m != n and not (group and ops[m]["group"] == group) and (w or w2 or bank) and clash(acc, acc2):
                    wait.update(ops[m]["mates"])
        for acc in writes:
            recs[acc[0]] = [r for r in recs.get(acc[0], []) for b in [r[2]] if not (
                clash(acc, b) if acc[0] == "ps" else
                acc[1] <= b[1] and b[2] <= acc[2] and acc[4] <= b[4] and b[5] <= acc[5]
                and (acc[3] == 1 or (b[3] % acc[3] == 0 and (acc[1] - b[1]) % acc[3] == 0)))]
        for acc, w in [(r, False) for r in reads] + [(r, True) for r in writes]:
            recs.setdefault(acc[0], []).append((n, w, acc))
        ops.append(dict(q=q, call=call, dur=dur, lat=lat, wait=wait, sem=sem, inc=inc, group=group, mates=[n],
                        what=named((writes or reads)[0])))
        return n

    def named(v):
        for k, (b, at, n) in PLACE.items():
            if b == v[0] and at <= v[1] < at + n:
                return k, v[1] - at
        return v[:2]

    def size(v):
        return (v[2] - v[1] - 1) // v[3] + 1

    def cost(q, out, ins, idx, two=False):
        n = size(out)
        if idx:
            return (50 if q == "v" else 65) + 1.6 * size(idx) * 16
        two_byte = all(SCRATCH[v[0]][2] in (BF, "float16", U16) for v in [out] + ins)
        psum = any(v[0] == "ps" for v in ins)
        return 1.04 * max(64, n * (2 if two and not psum else 0.5 if two_byte and q == "v" and not two else 1))

    def do(q, call, reads, writes, dur):
        return rec(q, lambda: call().then_inc(T.sem[q + "q_"], 1), reads, writes, dur, q + "q_")

    nd = [0]

    def dmas(jobs, lat=2200.0, after=()):
        sem = "dm%d" % nd[0]
        nd[0] += 1
        ids = [rec(e, lambda e=e, o=o, i=i: queue[e].dma_start(o, i).then_inc(T.sem[sem], 16), rd, wr, 60.0, sem, 16 * len(jobs), lat, sem)
               for e, o, i, rd, wr in jobs]
        for i in ids:
            ops[i]["mates"] = ids
            ops[i]["wait"].update(after)

    def send(dst, jobs, arr, loc, lat=LIST, more_=0.0):
        rid, pid = topo.addr(dst, core)
        n = len(topo.engines(core, dst)) * len(jobs)
        s = rec("g", lambda: [g.remote_dma(f(out), f(in_), T.sem[arr], T.sem[loc], pid, rid, topo.mask(core, dst)) for out, in_, f in jobs],
                [j[1] for j in jobs], [], ISSUE * len(jobs) + more_, loc, n, lat)
        r = rec(None, None, [], [j[0] for j in jobs], 0.0, arr, n, lat)
        ops[r]["wait"].add(s)

    def more(*vs):
        return [v for v in vs if isinstance(v, tuple)]

    def tt(out, a, b, op, idx=None):
        return do("v", lambda: g.vector.tensor_tensor(ap(out), ap(a, idx), ap(b), op), [a, b] + more(idx), [out],
                  cost("v", out, [a, b], idx, True))

    def ts(out, a, s1, op0, s2=None, op1=None, idx=None):
        c = [ap(s) if isinstance(s, tuple) else s for s in (s1, s2)]
        o2 = (op0,) if op1 is None else (op0, op1)
        do("v", lambda: g.vector.tensor_scalar(ap(out), ap(a, idx), c[0], c[1], *o2), [a] + more(s1, s2, idx), [out], cost("v", out, [a], idx))

    def cast(out, a, idx=None):
        do("v", lambda: g.vector.tensor_copy(ap(out), ap(a, idx)), [a] + more(idx), [out], cost("v", out, [a], idx))

    def scan(out, d0, d1, op0=A.add, op1=A.max):
        do("v", lambda: g.vector.tensor_tensor_scan(ap(out), ap(d0), ap(d1), 0.0, op0, op1), [d0, d1], [out], cost("v", out, [d0, d1], None))

    def sums(out, keep, d1):
        scan(out, keep, d1, A.mult, A.add)

    def turn(out, a):
        do("v", lambda: g.vector.transpose(ap(out), ap(a)), [a], [out], cost("v", out, [a], None))

    def act(out, a, func, scale=None, bias=0, idx=None):
        kw = {} if scale is None else {k: ap(s) if isinstance(s, tuple) else float(s) for k, s in (("scale", scale), ("bias", bias))}
        do("s", lambda: g.scalar.activation(ap(out), ap(a, idx), func, **kw), [a] + more(idx, scale, bias), [out], cost("s", out, [a], idx))

    def same(out, a, minus, k=1):
        act(out, a, AF.Abs, 1, minus)
        act(out, out, AF.Relu, -k, k)

    def aff(out, a, scale=1, bias=0, idx=None, spread=False):
        k, c = [ap(s) if isinstance(s, tuple) else float(s) for s in (scale, bias)]
        plain = scale == 1 and bias == 0
        calls = {"v": lambda: g.vector.tensor_copy(ap(out), ap(a, idx)) if plain else g.vector.tensor_scalar(ap(out), ap(a, idx), k, c, A.mult, A.add),
                 "s": lambda: g.scalar.activation(ap(out), ap(a, idx), AF.Copy) if plain else
                 g.scalar.activation(ap(out), ap(a, idx), AF.Identity, bias=c, scale=k)}
        dur = {q: cost(q, out, [a], idx) for q in "vs"}
        if spread:
            calls["g"], dur["g"] = lambda: g.partition_broadcast(ap(out), ap(a[:5] + (1,)), 128), 180 + 4.2 * size(out)
        elif plain and not idx and size(out) <= 80 and SCRATCH[out[0]][2] == SCRATCH[a[0]][2] and out[4:] == (0, 128):
            calls["g"] = lambda: g.affine_select(ap(out), ap(a), [[0, size(out)]], A.is_ge, 0.0, 0, 0)
            dur["g"] = 210 + 2.1 * size(out)
        rec("f", calls, [a] + more(scale, bias, idx), [out], dur, None)

    def fill(v, k):
        calls = {"v": lambda: g.vector.memset(ap(v), float(k)),
                 "g": lambda: g.iota(ap(v), [[0, size(v)]], k, 0, allow_small_or_imprecise_dtypes=True)}
        dur, none = {"g": 160 + 2.1 * size(v), "v": cost("v", v, [], None)}, L("cs", 0, min(96, size(v)))
        if size(v) <= 96 and v != none:
            calls["s"], dur["s"] = lambda: g.scalar.activation(ap(v), ap(none), AF.Identity, bias=float(k), scale=1.0), cost("s", v, [], None)
        rec("f", calls, [none] if "s" in dur else [], [v], dur, None)

    def plus(out, a, b):
        for c in range(size(out)):
            aff(out[:1] + (out[1] + c, out[1] + c + 1) + out[3:], a[:1] + (a[1] + c, a[1] + c + 1) + a[3:], 1, b[:1] + (b[1] + c, b[1] + c + 1) + b[3:])

    def quant(name, c0, n, x, x0=None):
        q, s, v = L("C" + name, c0, n), L("S" + name, c0, n), L(x, 4 * c0 if x0 is None else x0, 4 * n)
        do("v", lambda: g.vector.quantize_mx(ap(q), ap(s), ap(v)), [v], [q, s], 15 + 1.1 * n)

    def mm(bank, n, w, w0, x, x0=0):
        a, b, c, d = L("C" + w, w0, 128), L("S" + w, w0, 128), L("C" + x, x0, n), L("S" + x, x0, n)
        o = PS(bank, 0, n)
        do("t", lambda: g.tensor.matmul_mx(ap(o), ap(a), ap(b), ap(c), ap(d), True, True), [a, b, c, d], [o], COLUMN * (n + 16))

    def iota(v, pattern, base, cm=0):
        small = SCRATCH[v[0]][2] != I32
        do("g", lambda: g.iota(ap(v), pattern, base, cm, allow_small_or_imprecise_dtypes=True) if small else g.iota(ap(v), pattern, base, cm),
           [], [v], 160 + 2.1 * size(v))

    def pick(out, win, idx, cut):
        for a, b in ((0, cut), (cut, size(idx))):
            if b > a:
                aff(L(out[0], out[1] + 16 * a, 16 * (b - a)), win, idx=L(idx[0], idx[1] + a, b - a))

    iota(L("rank0", 8, 18), [[16, 18]], 0, 1)
    do("v", lambda: g.vector.memset(ap(L("cs", 0, 96)), 0.0), [], [L("cs", 0, 96)], 100.0)
    do("v", lambda: g.vector.memset(ap(L("raw", 0, 288, 1, 64, 128)), 0), [], [L("raw", 0, 288, 1, 64, 128)], 300.0)
    rows = [(h, 1, 9, T.pg[:, :]) for h in range(4)] + [(h, 9, 16, T.og[0:112, :]) for h in (0, 2)] + [
        (h, a, b, of) for h in (1, 3) for a, b, of in ((9, 13, T.og[64:128, :]), (13, 16, T.og[0:48, :]))]
    dmas([("ys"[n % 2], T.raw[16 * h + a:16 * h + b, :], of, [], [L("raw", 0, 288, 1, 16 * h + a, 16 * h + b)]) for n, (h, a, b, of) in enumerate(rows)]
         + [("y", T.raw[0:64:16, :], T.rank0[0:64, 8:26], [L("rank0", 8, 18)], [L("raw", 0, 288, 1, 0, 64)])], 2350.0)
    dmas([("y", T.pgn[:, 0:18], T.pg[:, :], [], [L("pgn", 0, 18)]),
          ("y", T.pgn[0:112, 18:36], T.pg[16:128, :], [], [L("pgn", 18, 18, 1, 0, 112)]),
          ("y", T.pgn[112:128, 18:36], T.pg[0:16, :], [], [L("pgn", 18, 18, 1, 112, 128)])], 2700.0)
    if FOUR:
        dmas([("y", T.pgm[a:b, 18 * k:18 * k + 18], T.pg[(a + 32 + 16 * k) % 128:(b + 31 + 16 * k) % 128 + 1, :], [],
               [L("pgm", 18 * k, 18, 1, a, b)]) for k in range(2) for a, b in ((0, 96 - 16 * k), (96 - 16 * k, 128))], 2700.0)
    dmas([("y", T.x0[:, :], T.x[:, :], [], [W("x0")])], 5000.0)
    dmas([("y", T.ut[:, :], T.u[:, :], [], [W("ut")])], 5400.0)
    loads = len(ops)

    P = lambda j: L("pi", j, 1)
    nq = [15]

    def Q():
        nq[0] += 1
        return L("pf", nq[0] - 1, 1)

    def mix(first, *terms):
        out = Q()
        for a, k in terms:
            aff(out, a, k, first)
            first = out
        return out

    def listed(name, lo, n, steps, add, most=None, st=1):
        if most is None:
            ts(L(name, lo, n, st), steps, add, A.add)
        else:
            ts(L(name, lo, n, st), steps, add, A.add, most, A.min)

    twos = lambda j: L("rank0", 8 - j, 1)
    ts(P(7), twos(0), 15, A.bitwise_and)
    cast(L("pf", 0, 1), P(7))
    for j in range(1, 5):
        ts(twos(j), twos(0), 2 ** j, A.mult) if j % 2 else iota(twos(j), [[0, 1]], 0, 2 ** j)
    ts(L("pi", 8, 5), L("rank0", 4, 5), 4, A.arith_shift_right, 1, A.bitwise_and)
    ts(L("pi", 13, 9), L("rank0", 4, 9), 5, A.arith_shift_right, 3, A.bitwise_and)
    cast(L("pf", 1, 5), L("pi", 8, 5))
    cast(L("pf", 6, 9), L("pi", 13, 9))
    I, B0, B1, K4, HI, S, MI, I4 = [L("pf", j, 1) for j in range(8)]
    M = L("pf", 10, 1)
    I7 = mix(I, (HI, -8))
    iota(W("bi"), [[1, 20]], 0)
    listed("wl", 0, 20, W("bi"), mix(-1, (I, 18)), 287)
    ts(L("ab", 0, 16), L("bi", 0, 16), I, A.is_equal, UP, A.mult)
    top, far = L("ab", 0, 1), Q()
    act(far, I, AF.Relu, 1, -13)
    GR = mix(S, (M, 2))
    lose = mix(mix(-144, (far, OUT)), (GR, mix(0, (top, -16.0 / UP))))
    X0, X1, X2, X3 = Q(), Q(), Q(), Q()
    ts(L("pf", nq[0] - 4, 4), L("pf", 1, 4), S, A.not_equal)
    SET, SET2 = Q(), Q()
    ts(L("pf", nq[0] - 2, 2), L("pf", 10, 2, 4), 2, A.min)
    iota(L("col", 0, 8), [[16, 8]], 0)
    iota(L("col", 20, 4), [[96, 2], [82, 2]], 14)
    own = q = mix(I, (SET, 96))
    ts(L("ol_", 0, 3), L("col", 0, 3, 2), mix(q, (HI, 8), (K4, 12), (X3, 304), (S, -16)), A.add, 9, A.add)
    ts(W("j0"), L("col", 0, 6), q, A.add, -144, A.add)
    ts(L("pi", 24, 4), L("rank0", 8, 4), 4, A.arith_shift_right, 7, A.bitwise_and)
    ts(W("bias"), L("pi", 24, 4), mix(-1, (I, 1)), A.is_equal, LOW, A.mult)
    less = mix(144, (GR, -288))
    tt(L("ab", 16, 8), L("ab", 2, 8), L("ab", 1, 8), A.subtract)
    aff(L("ab", 24, 8), L("ab", 16, 8), 1, mix(0, (L("ab", 14, 1), -1), (top, OUT // UP)))
    for f in range(8):
        aff(L("dtab", 8 * f, 8), L("ab", 24, 8), 1, L("ab", 16 + f, 1))
    aff(L("dtab", 64, 8), L("ab", 24, 8))
    for k in range(2):
        fill(L("two8", k, 40, 2), 8 * k)
    fill(W("anew"), 0)
    fill(L("anew", 0, 24, 8), 8 * FAR)
    fill(L("cs", 608, 96), 0)
    fill(L("o", 48, 48), 0)
    fill(L("rr", 0, 16), 0)
    fill(L("rr", 208, 16), 0)
    fill(L("rt", 0, 8), 1)
    fill(L("rt", 8, 8), 0)
    fill(L("rt", 432, 32), 0)
    fill(L("co", 0, 16), 0)
    fill(L("co", 48, 80), 0)
    ST = lambda name, lo, n: L("st", LISTS[name] + lo, n)
    fill(L("bw", 12, 56), 0)
    twice = ST("ld", 0, 1)
    aff(twice, S, 1, mix(I, (B0, -1)))
    q = mix(15, (twice, 16))
    ts(L("ls", 0, 1), q, 95, A.min)
    ts(L("ls", 2, 1), q, -8, A.add, 183, A.min)
    aff(L("nf", 0, 2), L("col", 0, 2), 1, I)
    aff(L("nf", 2, 2), L("nf", 0, 2), 1.0 / 6, -2.5 / 6)
    cast(W("ni"), L("nf", 2, 2))
    aff(L("nf", 2, 2), L("nf", 0, 2), 8, 0)
    for c in range(2):
        aff(L("nf", 6 + c, 1), L("ni", c, 1), -48, L("nf", 2 + c, 1))
    aff(L("nf", 4, 2), W("ni"), 2, mix(1, (S, 8), (B0, -8)))
    tt(ST("lu", 0, 2), L("nf", 4, 2), L("nf", 6, 2), A.add)
    ts(L("nf", 8, 2), W("ni"), SET, A.is_equal, 2, A.mult)
    ts(L("nf", 10, 2), W("ni"), SET2, A.is_equal, mix(5, (M, 48)), A.add)
    plus(L("nf", 8, 2), L("nf", 8, 2), L("nf", 10, 2))
    plus(ST("lf", 0, 2), L("nf", 8, 2), L("nf", 6, 2))
    hot = L("ab", 32, 8)
    ts(hot, L("bi", 0, 8), I7, A.is_equal)
    H = lambda k: L("ab", 32 + k, 1)
    aff(ST("lb", 0, 3), L("col", 1, 3, 2), 1, mix(0, (B0, 16), (H(5), 80), (H(2), -1000), (H(6), -1000)))
    aff(ST("lb", 4, 3), L("col", 1, 3, 2), H(4), mix(0, (H(0), 8), (H(3), 8)))
    q = mix(16, (S, -16), (B0, 16))
    ts(ST("lm", 0, 1), MI, 2, A.min, 32, A.mult)
    aff(ST("lm", 2, 2), L("col", 0, 2, 4), 1, mix(q, (HI, 32), (B1, 96), (K4, 16), (X2, 208)))
    aff(ST("lm", 4, 1), X0, 208, mix(q, (MI, 32)))
    aff(ST("lc", 0, 3), L("bi", 0, 3), 2, mix(S, (I7, 8)))
    later = Q()
    ts(later, I, 6, A.is_ge)
    aff(ST("lo", 0, 2), L("bi", 0, 2), 1, mix(0, (I, 8), (later, -44), (S, 2)))
    aff(ST("lq", 0, 1), ST("lo", 1, 1))
    pair = q = mix(0, (I, 16), (later, 96), (S, 96))
    ts(ST("la", 0, 4), L("col", 20, 4), q, A.add, 478, A.min)
    ts(ST("l0", 0, 2), L("col", 21, 2), q, A.add, 478, A.min)
    if REDO:
        listed("l6", 0, 2, L("col", 21, 2), q, 382)
    aff(ST("lk", 0, 2), L("nf", 6, 2), 2, 0)
    aff(L("nf", 12, 2), W("ni"), 2, mix(1, (S, 1)))
    plus(ST("lk", 2, 2), ST("lk", 0, 2), L("nf", 12, 2))
    ts(W("cap"), L("bi", 2 * LATE, 2), I7, A.is_gt, 9000, A.mult)
    iota(L("col", 24, 3), [[32, 3]], 82)
    q = mix(14, (MI, 96), (HI, 16))
    ts(ST("lv", 0, 3), L("col", 24, 3), mix(q, (B0, 14)), A.add, L("cap", 0, 1), A.min)
    ts(ST("lw", 0, 3), L("col", 0, 3, 2), mix(q, (B0, 82)), A.add, L("cap", 1, 1), A.min)
    aff(W("gc"), L("bi", 0, 4), -2 * FAR, mix(512, (S, -FAR)))
    aff(ST("lz", 0, 2), L("col", 0, 2, 2), 1, mix(I, (HI, 8), (S, 8)))
    ts(L("nf", 16, 2), L("nf", 0, 2), 17, A.min, 16, A.mult)
    aff(ST("il", 0, 2), L("nf", 16, 2), 1, mix(1, (GR, 1), (X0, 304)))
    for c, n in ((0, 4), (4, 4), (8, 18), (26, 10), (36, 14)):
        cast(L("li", c, n), L("st", c, n))
    fill(L("gb", 0, 16), 0)
    fill(L("gb", 304, 16), 0)
    cast(L("pl", 0, 36), W("pgn"))
    if FOUR:
        cast(L("pl", 36, 36), W("pgm"))
    for m in range(0 if FOUR else 4):
        cast(L("pl", 36, 36, 1, 32 * m, 32 * m + 32), L("pgn", 0, 36, 1, 32 * ((m + 1) % 4), 32 * ((m + 1) % 4) + 32))
    for c in range(4):
        iota(L("sw", 576 * c, 576), [[0, 576]], 0)
    fill(W("one"), 1)
    do("g", lambda: g.affine_select(ap(W("et")), ap(W("one")), [[-1, 520]], A.is_equal, 0.0, 3, 4), [W("one")], [W("et")], 200 + 2.1 * 520)
    for b in range(4):
        quant("e", 128 * b, 128, "et", 3 - b)
    q = mix(0, (I, 8))
    q = mix(q, (mix(0, (I4, 16), (B1, 64), (I, -8)), B0))
    listed("ul", 0, 10, L("bi", 0, 10), q, q)
    iota(W("wt"), [[0, 72]], 8)
    for d in range(-7, 8):
        f0, n = max(0, -d), 8 - abs(d)
        if d % 4:
            a, b = VIEW[d % 8], VIEW[-d % 8]
            iota(L("wt", 9 * f0 + d, n, 9), [[2, n]], 144 + 2 * f0 - SHIFT[a] + 256 * a + 1024 * b, -1)
        elif d:
            iota(L("wt", 9 * f0 + d, n, 9), [[4, n]], 145 + (1024 if d > 0 else 256), -1)
    ts(L("wi", 0, 72), W("wt"), 15, A.bitwise_and)
    ts(L("wf", 0, 72), L("wi", 0, 72), 0, A.is_equal, -8, A.mult)
    ts(L("wf", 72, 72), L("wi", 0, 72), 15, A.is_equal, 2, A.mult)
    tt(W("mtab"), L("wf", 0, 72), L("wf", 72, 72), A.add)
    ts(L("wi", 72, 64), L("wt", 0, 64), 8, A.arith_shift_right, 3, A.bitwise_and)
    ts(L("wi", 136, 64), L("wt", 0, 64), 10, A.arith_shift_right)
    tt(L("nf", 14, 2), L("ab", 10, 2, 2), L("ab", 11, 2, 2), A.subtract)
    aff(L("nf", 14, 2), L("nf", 14, 2), 288.0 / UP)
    for k in range(2):
        aff(L("wf", 144 + 64 * k, 64), L("wi", 72 + 64 * k, 64), L("nf", 14 + k, 1))
    ends, keep = mix(0, (L("ab", 15, 1), -2.0 / UP)), mix(1, (L("ab", 15, 1), -1.0 / UP))
    ts(L("l2", 0, 10), ST("lm", 0, 10), 15, A.add)
    listed("l2", 10, 4, ST("lb", 4, 4), mix(0, (H(4), 15)))
    listed("l2", 14, 2, L("bi", 10, 2, 2), pair, 383)
    quant("u", 0, 128, "ut")
    ul = L("ul", 0, 9)
    views = do("v", lambda: g.vector.tensor_copy(ap(W("Cr")).bitcast(dt.uint32), ap(W("Cu")).bitcast(dt.uint32).indirect(ap(ul))),
               [W("Cu"), ul], [W("Cr")], 280.0)
    act(W("Sr"), W("Su"), AF.Copy, idx=ul)

    def products(t):
        x = "x%d" % t
        for c0, n in RUNS if t else ((0, 288),):
            quant(x, c0, n, x)
            for i in range(3 if t else 0):
                bank = (i + (3 if c0 else 0)) % (8 - STAY[t - 1])
                mm(bank, n, "r", SHIFT[i], x, c0)
                aff(L("sw", 288 * i + c0, n), PS(bank, 0, n), keep)
        if not t:
            mm(0, 288, "u", 0, x)
            aff(W("yt"), PS(0, 0, 288))
            dmas([(LAYS[h], T.sw[16 * h:16 * h + 1, :], T.yt[0:128:16, :], [W("yt")], [L("sw", 0, 2304, 1, 16 * h, 16 * h + 1)])
                  for h in range(8)], 2400.0)
        dst = T.cores[rank ^ STEP[t]]
        c0 = RUNS[1][0] if t else 0
        if t:
            send(dst, [(L("Cp%d" % t, 0, c0), L("C" + x, 0, c0), u8)], "ce%d" % t, "cf%d" % t, CODES - 400.0)
        send(dst, [(L("Cp%d" % t, c0, 288 - c0), L("C" + x, c0, 288 - c0), u8), (W("Sp%d" % t), W("S" + x), ap)], "ca%d" % t, "cb%d" % t,
             CODES - AHEAD if t else CODES + FIRST, 0 if t else FIRST)
        for b in range(4):
            if b < 4 - STAY[t]:
                mm(1 + b, 288, "e", 128 * b, x)
                aff(W("f%d" % b), PS(1 + b, 0, 288))
            else:
                mm(4 + b, 288, "e", 128 * b, x)
                for c0, n in RUNS:
                    if (t, b, c0) in PART:
                        aff(L("f%d" % b, c0, n), PS(4 + b, c0, n))

    O = lambda name, k: L(name, k, 6, 8)
    run = lambda name, lo, n=6: L(name, lo, n, 16)
    at = lambda n: 96 * n + (96 if n < 4 else 256)
    R = lambda n, slot=None: L("cw", at(n), 96) if slot is None else run("cw", at(n) + slot)
    SC = lambda n, slot=None: L("cs", 96 + 96 * n, 96) if slot is None else run("cs", 96 + 96 * n + slot)
    W1, W0, X10, X01, X11 = 512, 608, 704, 800, 896
    step = lambda t, k: SC((k + 2 - t % 2) // 2 - 1, 14 * ((k + t) % 2))

    def blocks(out, o, a, b):
        ts(a, o, GR, A.is_lt, 2304, A.mult)
        aff(b, o, 288, less)
        tt(out, a, b, A.add)

    def prepare(t):
        par, n, da = t % 2, 4, "da%d" % (t % 2)
        blocks(L("ob", 0, 48), L("o", 0, 48), L("oa", 0, 48), L("oa", 48, 48))
        tt(L("co", 16, 32), L("o", par + 1, 32, 2), L("o", par, 32, 2), A.subtract)
        sums(W("cp"), W("two8"), L("o", par, 80))
        if par:
            fill(L("co", 19, 8, 4), 0)
            aff(O("cp", 7), O("o", 7), 1, 64)
            aff(SC(-1, 14), SC(0, 0))
        cast(W("uc"), W("cp"), W("lu"))
        for a, b in ((0, 1), (1, n)):
            aff(L("ra", 96 * a, 96 * (b - a)), W("dtab"), idx=L("uc", 6 * a, 6 * (b - a)))
            turn(L(da, 96 * a, 96 * (b - a)), L("ra", 96 * a, 96 * (b - a)))
        for w in range(t > 0, 2):
            tt(L("bw", 6 * w, 6), SC(0, 0) if par else W("j0"), O("ob", par + w), A.add)
        cast(W("ub"), W("bw"), L("ld", 0, 1))
        aff(run(da, 15), O("ob", 2 + par))
        aff(run(da, 111), O("ob", 4 + par))
        for w in range(t > 0, 2):
            aff(L("g0", 96 * w, 96), W("tab"), idx=L("ub", 6 * w, 6))
            turn(R(4 + w), L("g0", 96 * w, 96))
            scan(L("cs", W1, 96) if w else SC(0), L(da, 0, 96), R(4 + w))
        if not t:
            cast(W("u1"), SC(0), L("ls", 0, 1))
            pick(L("g4", 0, 96), W("tab"), L("u1", 0, 6), CUT0)
            turn(R(6), L("g4", 0, 96))
            scan(SC(1), L(da, 96, 96), R(6))
        K = lambda k: L("co", 48 + 8 * k, 6)
        was = lambda k: step(max(t - 1, 0), par + k)
        tt(K(2), O("ob", 3 + par), O("ob", 2 + par), A.subtract)
        tt(K(6), O("ob", 5 + par), O("ob", 4 + par), A.subtract)
        tt(run("cs", W0 + 7), was(1), O("ob", 3 + par), A.add)
        tt(run("cs", W1 + 7), run("cs", W1 + 15), K(2), A.add)
        cast(L("ue", 0, 16), L("cs", W1, 96), L("ls", 0, 1))
        cast(L("ue", 16, 16), L("cs", W1, 184), L("ls", 2, 1))
        for c, n, lo in ((96, 96, 0), (192, 192, 16)):
            aff(L("g4", c, n), W("tab"), idx=L("ue", lo, n // 16))
            turn(L("cw", at(6) + c, n), L("g4", c, n))
        for n, c in ((7, X10), (8, X11), (9, X01)):
            scan(L("cs", c, 96), L(da, 96, 96), R(n))
        tt(K(0), run("cs", W1), was(0), A.subtract)
        tt(K(1), run("cs", W1 + 14), was(1), A.subtract)
        if t:
            tt(K(3), was(1), O("ob", 2 + par), A.add)
            tt(run("cs", W0 + 15), was(3), O("ob", 4 + par), A.add)
        else:
            aff(K(3), SC(0, 15))
            aff(run("cs", W0 + 15), SC(1, 15))
        tt(K(5), run("cs", X10 + 15), run("cs", W0 + 15), A.subtract)
        tt(L("co", 112, 12), run("cs", X01 + 15, 12), run("cs", W0 + 15, 12), A.subtract)
        tt(K(4), L("co", 118, 6), K(8), A.subtract)
        aff(K(7), run("cs", W0 + 15) if t else SC(1, 15))
        aff(W("cf"), L("co", 56, 64), idx=L("lc", 0, 3))
        if par:
            fill(run(da, 207), 288 * 8 + 144)
        else:
            tt(L("co", 0, 6), O("ob", 7), O("ob", 6), A.subtract)

    def look(n, par, more_=True, cut=0):
        pick(W("g%d" % n), W("tab"), L("u%d" % n, 0, 6), cut if n > 1 else 0)
        turn(R(n), W("g%d" % n))
        if more_:
            scan(SC(n), L("da%d" % par, 96 * n, 96), R(n))
        if n == 2:
            cast(W("u3"), SC(n), L("ls", 0, 1))

    def score_lists(t):
        if t:
            aff(SC(3, 0), R(3, 0) if t == 1 else SC(3, 14))
        if t:
            aff(W("sg"), W("da%d" % (t % 2)), 1, 144, idx=L("l2", 14, 2))
            cast(W("um"), W("cp"), L("lq", 0, 1))
            aff(W("mp"), W("mtab"), 1, ends, idx=L("um", 0, 12))
            turn(W("pm"), W("mp"))
        else:
            aff(W("sg"), W("o"), 288, 144, idx=L("lo", 0, 2))
        if not t and REDO:
            tt(W("sa"), L("cs", 0, 384), W("sg"), A.add, idx=W("l6"))
            cast(W("s0"), W("sa"))
        tt(L("cs", 480, 32), L("cs", 0, 480), W("sg"), A.add, idx=L("la", 4 - 2 * t, 2) if t else W("l0"))
        cast(W("so"), L("cs", 480, 32))

    early = len(ops)
    products(0)
    for c in (0, 160):
        aff(L("tab", 2288 + c, 160), W("raw"), 1, lose, idx=L("wl", c // 16, 10))
        if RAW < 8:
            aff(L("tab", 2288 + c, 160, 1, 64, 128), L("tab", 2288 + c, 160, 1, 0, 64))
    dmas([("y", u8(W("Cw")), T.wc[:, :], [], [W("Cw")]), ("y", T.Sw[:, :], T.ws[:, :], [], [W("Sw")]),
          ("y", T.vt[:, :], T.v[:, :], [], [W("vt")])], 5000.0, range(early + 3, early + 11))
    turn(L("tw", 0, 288), L("tab", 2304, 288))
    turn(L("tw", 288, 320), L("tab", 2288, 320))
    aff(L("o", 0, 48), W("tw"), 1, 144, idx=L("ol_", 0, 3))
    for r in range(4):
        aff(L("tab", 288 * r, 288), L("tab", 2304, 288), 1, L("bias", r, 1), idx=L("pl", 18 * r, 18))
        halves = [(L("tab", 288 * (4 + r), 288, 1, h, h + 64), L("tab", 288 * r, 288, 1, 64 - h, 128 - h)) for h in (0, 64)]
        if r < SWAP:
            dmas([("y", ap(to), ap(of), [of], [to]) for to, of in halves], 2500.0)
        for to, of in halves if r >= SWAP else ():
            aff(to, of)
    prepare(0)
    aff(run("da0", 207), O("ob", 6))
    cast(W("u2"), SC(1), L("ls", 0, 1))
    for n in (2, 3):
        look(n, 0)
    score_lists(0)
    quant("v", 0, 128, "vt")

    for t in range(3):
        dst, par = T.cores[rank ^ STEP[t]], t % 2
        def compare(c, so):
            sw = L("sw", 0, 864 if t else 2304)
            aff(L("eb", 16 * c, 96), sw, idx=L(so, 16 + c, 6))
            tt(L("rr", 16 + 16 * c, 96), sw, L("eb", 16 * c, 96), A.is_gt, idx=L(so, c, 6))

        for c in (0, 6):
            compare(c, "so" if t or not REDO else "s0")
        for c, n in ((16, 96), (112, 96)) if TWO else ((16, 192),):
            turn(L("rq" if t else "rt", c, n), L("rr", c, n))
            if t:
                scan(L("rt", c, n), L("pm", c - 16, n), L("rq", c, n))
        lm, lb = ("l2", lambda c: L("l2", 6 + c, 3)) if t else ("lm", lambda c: L("lb", c, 3))
        tt(W("s3"), L("rt", 0, 208), W("cf"), A.mult, idx=lb(0))
        aff(W("k4"), L("rt", 0, 208), idx=lb(4))
        if not t and REDO:
            compare(6, "so")
            turn(L("rt", 112, 96), L("rr", 112, 96))
        if t:
            turn(L("rr", 16, 192), L("rt", 16, 192))
        turn(L("rt", 208, 224), W("rr"))
        sums(W("s3o"), W("k4"), W("s3"))
        cast(L("u2", 0, 6), L("s3o", 7, 6, 8))
        cast(L("u1", 0, 6), L("s3o", 2, 6, 8))
        tt(L("mm", 16, 48), W("rt"), L("co", 16, 48), A.mult, idx=L(lm, 2, 3))
        if not par:
            tt(L("mm", 0, 16), L("rt", 128, 80), L("co", 0, 16), A.mult, idx=L(lm, 0, 1))
            tt(run("da0", 207), L("mm", 0, 6), O("ob", 6), A.add)
        first, second = L("o", par, 32, 2), L("o", par + 1, 32, 2)
        tt(first, first, L("mm", 16, 32), A.add)
        tt(second, second, L("mm", 16, 32), A.subtract)
        for e in (1, 0) if t == 2 else (0, 1):
            tt(SC(0, 14 * e), L("mm", 48 + 8 * e, 6), step(max(t - 1, 0), par + e), A.add)
        aff(W("ok"), L("o", 0, 48), FAR)
        for n in (1, 2, 3):
            look(n, par, n < 3 or t == 1, CUT * (t > 0 and n in CUTS))
            if n == LATE - 1:
                tt(W("vk"), L("cs", 0, 96 * LATE + 96), W("ok"), A.add, idx=L("lw" if par else "lv", 0, 3))
                for c in range(4):
                    act(L("mk", 48 * c, 48), W("vk"), AF.Abs, 1, L("gc", c, 1))
        for k in range(2 * LATE + par, 8):
            n, e = (k + 2 - par) // 2 - 1, (k + par) % 2
            tt(L("mk", k, 32, 8), R(n), L("mk", k, 32, 8), A.add, idx=L("lk", 2 if k == 7 or e else 0, 2))
        scan(W("fin"), W("anew"), L("mk", 0, 192), A.add, A.min)
        for to, of, n, slot in ((64, 0, 64, 6), (0, 64, 64, 6), (0, 32, 32, 5), (32, 0, 32, 5), (64, 32, 32, 5), (96, 0, 32, 5)):
            aff(L("fin", slot, 24, 8, to, to + n), L("fin", 7, 24, 8, of, of + n))
        al, bl, ll = "al%d" % t, "bl%d" % t, "ll%d" % t
        ts(W(al), W("fin"), 144 - 512, A.add, idx=W("lf"))
        send(dst, [(W(ll), L(al, 0, 18), ap)], "la%d" % t, "lb%d" % t)
        aff(L("gb", 16, 288), L("tab", 2304, 288), idx=L(al, 0, 18))
        turn(L("tb", 0, 288), L("gb", 16, 288))
        turn(L("tb", 288, 320), W("gb"))
        ts(W(bl), W("tb"), 144, A.add, idx=W("il"))
        for b in range(4):
            bank = b + min(2, 4 - STAY[t])
            mm(bank, 288, "e", 128 * b, "p%d" % t)
            aff(W("d%d" % b), PS(bank, 0, 288))
        if t < 2:
            for k in range(0 if t else 2):
                tt(L("dtab", 0, 64), L("dtab", 0, 64), L("wf", 144 + 64 * k, 64), A.add)
            prepare(t + 1)
            score_lists(t + 1)
        else:
            aff(W("ou"), L("o", 0, 64), idx=W("lz"))
            turn(W("ot"), W("ou"))
            dmas([("y", T.ol[:, 32 * c:32 * c + 32], T.ot[32 * (c // 3) + 8 * (c % 3):32 * (c // 3) + 8 * (c % 3) + 8, :], [W("ot")], [])
                  for c in range(9)])
        z, x = "z%d" % t, "x%d" % (t + 1)
        for h, (c0, n) in enumerate(HALF):
            for b in range(4):
                aff(L(z, 4 * c0 + b, n, 4), W("d%d" % b), idx=L(ll, c0 // 16, n // 16))
            quant(z, c0, n, z)
            for b in range(4):
                bank = (1 + b + 4 * h) % (8 - STAY[t])
                mm(bank, n, "w", 128 * b, z, c0)
                aff(L("r%d" % b, c0, n), PS(bank, 0, n), 0.03125)
        for c0, n in RUNS:
            i = L(bl, c0 // 16, n // 16)
            for b in range(4):
                if b < 4 - STAY[t] or (t, b, c0) in PART:
                    tt(L(x, 4 * c0 + b, n, 4), W("r%d" % b), L("f%d" % b, c0, n), A.add, idx=i)
                else:
                    aff(L("r4", 288 * (3 - b) + c0, n), W("r%d" % b), idx=i)
                    tt(L(x, 4 * c0 + b, n, 4), PS(4 + b, c0, n), L("r4", 288 * (3 - b) + c0, n), A.add)
                if t == 2 and c0 and b >= LAST:
                    ops[-1]["wait"].add(stored)
            if t == 2:
                stored = len(ops)
                quant(x, c0, n, x)
        if t < 2:
            products(t + 1)

    for h, (c0, n) in enumerate(RUNS):
        mm(4 + h, n, "v", 0, "x3", c0)
        aff(L("yt", c0, n), PS(4 + h, 0, n))
        if h and ENDS:
            ops[-1]["dur"] = {"v": ops[-1]["dur"]["v"]}
    for c0, n in RUNS if YW else ((0, 288),):
        dmas([("y", T.y[:, c0:c0 + n], T.yt[:, c0:c0 + n], [L("yt", c0, n)], [])], 2150.0 if c0 else 2900.0)
    for c0, n in RUNS if OW else ((0, 288),):
        dmas([("s", T.oc[:, 4 * c0:4 * c0 + 4 * n], u8(L("Cx3", c0, n)), [L("Cx3", c0, n)], [])], 2500.0 if c0 else 3300.0)
    dmas([("ys"[k % 2 * ENDS], T.osc[4 * k:4 * k + 4, :], T.Sx3[32 * k:32 * k + 4, 0:288], [W("Sx3")], []) for k in range(4)], 2000.0)

    if not ORDER:
        N = len(ops)
        nxt, prio, favour = [[] for _ in ops], [0.0] * N, [FAVOUR] * N
        for i, o in enumerate(ops):
            for m in o["wait"]:
                nxt[m].append(i)
        span = lambda o: o["dur"]["v"] if o["q"] == "f" else (o["lat"] if o["q"] else 0.0) or o["dur"]
        for i in reversed(range(N)):
            prio[i] = span(ops[i]) + max([0.0] + [WAKE + prio[k] for k in nxt[i]])

        def place(key, before, after, on, back):
            left, start, end, on = [len(b) for b in before], [0.0] * N, [0.0] * N, dict(on)
            busy = {q: [] for q in queue}
            ready = [(key[i], i) for i in range(N) if not left[i]]
            while ready:
                ready.sort(reverse=True)
                i = ready.pop()[1]
                o = ops[i]
                at0 = max([0.0] + [end[m] + WAKE for m in before[i]])
                best = None
                for q in ([on[i]] if back or o["q"] != "f" else sorted(o["dur"])):
                    dur = o["dur"][q] if o["q"] == "f" else o["dur"]
                    lat = o["lat"] if q and o["lat"] else dur
                    at, n = at0 + (lat - dur if back else 0.0), 0
                    for n, (a, b) in enumerate(busy.get(q, []) + [(1e18, 1e18)]):
                        if b > at:
                            if a >= at + dur:
                                break
                            at = b
                    if best is None or at + dur + (favour[i] if q == "v" else 0.0) < best[0] + best[1] - (2 * favour[i] if best[3] == "g" else 0.0):
                        best = (at, dur, lat, q, n)
                at, dur, lat, q, n = best
                if q:
                    busy[q].insert(n, (at, at + dur))
                    start[i], end[i] = at, at + (dur if back else lat)
                else:
                    start[i], end[i] = at0, at0 - WAKE
                on[i] = q
                for k in after[i]:
                    left[k] -= 1
                    if not left[k]:
                        ready.append((key[k], k))
            return start, end, on

        pre = [sorted(o["wait"]) for o in ops]
        key, on, kept = [-p for p in prio], {i: o["q"] for i, o in enumerate(ops)}, None
        dice = numpy.random.RandomState(SEED)

        def lasts(order, on):
            both, tight = 0.0, []
            for wake, slow, each, way in CASES:
                free, done, why, last = {}, [0.0] * N, [None] * N, {}
                for i in order:
                    o, q = ops[i], on[i]
                    at, why[i] = max([(0.0, -1)] + [(done[m] + wake, m) for m in pre[i]])
                    if q is None:
                        done[i] = at - wake
                        continue
                    if free.get(q, 0.0) > at:
                        why[i] = -2 - last[q]
                    last[q] = i
                    at, dur = max(at, free.get(q, 0.0)), o["dur"][q] if o["q"] == "f" else o["dur"]
                    if o["lat"]:
                        free[q], done[i] = at + dur, at + (way if o["lat"] == LIST else o["lat"] * each)
                    else:
                        free[q] = done[i] = at + dur * slow
                both += max(done)
                i = done.index(max(done))
                while i != -1:
                    if why[i] < -1:
                        tight.append((i, -2 - why[i]))
                    i = why[i] if why[i] >= -1 else -2 - why[i]
            return both, tight

        for n in range(TRIES):
            start, end, on = place([i - 1e9 if i < loads else k for i, k in enumerate(key)], pre, nxt, on, False)
            took = lasts(sorted(range(N), key=lambda i: (start[i], i)), on)[0]
            if kept is None or took <= kept[4]:
                kept = (start, end, on, list(favour), took)
                base = key = [-e for e in place([-e for e in end], nxt, pre, on, True)[1]]
                if n % 2:
                    continue
            lo = float(dice.rand()) * max(kept[1])
            shake, other = dice.normal(0.0, float(dice.choice((60.0, 200.0, 500.0))), N), dice.choice((-100.0, 0.0, 100.0, 300.0), N)
            near = [lo <= s < lo + 2500.0 for s in kept[0]]
            key = [k + float(shake[i]) if near[i] else k for i, k in enumerate(base)]
            favour[:] = [float(other[i]) if near[i] and abs(shake[i]) < 50.0 else f for i, f in enumerate(kept[3])]
        order, on = sorted(range(N), key=lambda i: (kept[0][i], i)), kept[2]
        hold = [{q: [((o["dur"][q] if o["q"] == "f" else o["dur"]) if o["lat"] or not q else
                      (o["dur"][q] if o["q"] == "f" else o["dur"]) * slow) if o["q"] == q or (o["q"] == "f" and q in o["dur"]) else 0.0
                     for o in ops] for q in list(queue) + [None]} for wake, slow, each, way in CASES]
        late = [[(way if o["lat"] == LIST else o["lat"] * each) if o["q"] else 0.0 for o in ops] for wake, slow, each, way in CASES]

        can = [sorted(o["dur"]) if o["q"] == "f" else [o["q"]] for o in ops]

        def inside(part, on, c, a, limit, done, why, marks, out, outq, least):
            wake, hold_, late_, a = CASES[c][0], hold[c], late[c], a // 8
            done, why, marks = done[:], dict(why), marks[:a + 1]
            free, last, end, at_end, all_ = marks[a]
            free, last = dict(free), dict(last)
            for n in range(8 * a, len(part), 8):
                for i in part[n:n + 8]:
                    q, at, by = on[i], -1e9, -1
                    for m in pre[i]:
                        if done[m] > at:
                            at, by = done[m], m
                    if q is None:
                        d = at
                    else:
                        at += wake
                        if free[q] > at:
                            at, by = free[q], -2 - last[q]
                        last[q] = i
                        d = free[q] = at + hold_[q][i]
                        if late_[i]:
                            d = at + late_[i]
                    if d + least[i] > limit:
                        return None
                    done[i], why[i] = d, by
                    all_ += d
                    if d + out[i] > end:
                        end, at_end = d + out[i], i
                marks.append((dict(free), dict(last), end, at_end, all_))
            for q in free:
                if free[q] + outq[q] > end:
                    end, at_end = free[q] + outq[q], last[q]
            tight, i = [], at_end
            while i in why:
                if why[i] < -1:
                    tight.append((i, -2 - why[i]))
                i = why[i] if why[i] >= -1 else -2 - why[i]
            return end + EARLY * all_ / len(part), tight, end, done, why, marks

        for WIDE, ANEW, POLISH in SWEEPS:
            for c0 in range(0, N - WIDE // 2, WIDE // 2):
                part, rest, state = order[c0:c0 + WIDE], order[c0 + WIDE:], []
                for c in range(len(CASES)):
                    wake, done, free, tail, outq = CASES[c][0], [0.0] * N, {q: 0.0 for q in queue}, {}, {q: 0.0 for q in queue}
                    for i in order[:c0]:
                        q, at = on[i], max([0.0] + [done[m] + wake for m in pre[i]])
                        if q is None:
                            done[i] = at - wake
                        else:
                            at = max(at, free[q])
                            free[q] = at + hold[c][q][i]
                            done[i] = at + late[c][i] if late[c][i] else free[q]
                    for i in reversed(rest):
                        q, after = on[i], max([0.0] + [wake + tail[k] for k in nxt[i]])
                        tail[i] = after - wake if q is None else max((late[c][i] or hold[c][q][i]) + after, hold[c][q][i] + outq[q])
                        if q:
                            outq[q] = tail[i]
                    out, least = {i: max([0.0] + [wake + tail[k] for k in nxt[i] if k in tail]) for i in part}, {}
                    for i in reversed(part):
                        least[i] = max([out[i]] + [least[k] + (wake + (late[c][k] or min(hold[c][q][k] for q in can[k])) if on[k] else 0.0)
                                                   for k in nxt[i] if k in least])
                    state.append([done, {}, [(free, {q: -1 for q in queue}, 0.0, -1, 0.0)], out, outq, least, 1e18])

                def both(part, on, a, most):
                    got, room = [], most - took + ROOM
                    for c in range(len(CASES)):
                        got.append(inside(part, on, c, a, state[c][6] + room, *state[c][:6]))
                        if got[-1] is None:
                            return None
                    if sum(x[0] for x in got) > most:
                        return None
                    for c, x in enumerate(got):
                        state[c][:3], state[c][6] = x[3:], x[2]
                    return sum(x[0] for x in got), [p for x in got for p in x[1]]

                took = 0.0
                took, tight = both(part, on, 0, 1e18)
                done, free, out, outq = state[0][0], state[0][2][0][0], state[0][3], state[0][4]
                wake, here, way = CASES[0][0], set(part), {}
                for i in reversed(part):
                    way[i] = (late[0][i] or hold[0][on[i]][i]) + max([out[i], outq.get(on[i], 0.0)] + [wake + way[k] for k in nxt[i] if k in here])
                into = {i: max([0.0] + [done[m] + wake for m in pre[i] if m not in here]) for i in part}
                inner = [{i: [m for m in x[i] if m in here] for i in part} for x in (pre, nxt)]

                def lay(key, to, lean, back):
                    before, after, from_, gaps = inner[back], inner[1 - back], (into, out)[back], {q: [((free, outq)[back][q], 1e18)] for q in queue}
                    left, start, end = {i: len(before[i]) for i in part}, {}, {}
                    ready = [(key[i], i) for i in part if not left[i]]
                    while ready:
                        ready.sort(reverse=True)
                        i = ready.pop()[1]
                        at0, pick_ = from_[i], None
                        for m in before[i]:
                            if end[m] + wake > at0:
                                at0 = end[m] + wake
                        if to[i] is None:
                            start[i] = end[i] = at0 - wake
                        else:
                            for q in (can[i] if lean is not None else [to[i]]):
                                dur = hold[0][q][i]
                                at = at0 + (late[0][i] - dur if back and late[0][i] else 0.0)
                                gap = gaps[q]
                                c = len(gap) - 1
                                while c and gap[c - 1][1] >= at + dur:
                                    c -= 1
                                while gap[c][1] - gap[c][0] < dur:
                                    c += 1
                                if gap[c][0] > at:
                                    at = gap[c][0]
                                worth = at + dur + (lean[i] if q == "v" and lean is not None else 0.0)
                                if pick_ is None or worth < pick_[0]:
                                    pick_ = (worth, at, dur, q, c)
                            worth, at, dur, to[i], c = pick_
                            a, b = gaps[to[i]][c]
                            gaps[to[i]][c:c + 1] = [x for x in ((a, at), (at + dur, b)) if x[1] - x[0] >= 59.0]
                            start[i], end[i] = at, at + (dur if back else late[0][i] or dur)
                        for k in after[i]:
                            left[k] -= 1
                            if not left[k]:
                                ready.append((key[k], k))
                    return start, end

                seed = {i: -way[i] for i in part}
                for n in range(ANEW):
                    noise, lean = dice.normal(0.0, (30.0, 80.0, 200.0, 500.0)[n % 4], N), dice.normal(FAVOUR / 2, FAVOUR, N)
                    to, key = dict(on), {i: i - 1e9 if i < loads else seed[i] + noise[i] for i in part}
                    for again in range(2):
                        start, end = lay(key, to, lean if n % 3 or not again else None, 0)
                        new = sorted(part, key=lambda i: (start[i], i))
                        got = both(new, to, 0, took)
                        key = lay({i: -end[i] for i in part}, dict(to), None, 1)[1]
                        key = {i: i - 1e9 if i < loads else -key[i] for i in part}
                        if got:
                            part, on, took, tight, seed = new, dict(to), got[0], got[1], key
                where, best, M_ = {m: n for n, m in enumerate(part)}, (took, part, on), len(part)
                for n in range(POLISH):
                    luck = dice.rand(6)
                    if luck[0] < LOOSE or not tight:
                        b = 1 + int(luck[1] * (M_ - 1))
                        i, k = part[b], part[max(0, b - 1 - int(luck[2] * 40))]
                    else:
                        i, k = tight[int(luck[1] * len(tight))]
                    new, to, how = part, on, int(luck[3] * 3)
                    if how == 0 and ops[k]["q"] == "f":
                        if k not in where:
                            continue
                        to, a = dict(on), where[k]
                        to[k] = sorted(ops[k]["dur"])[int(luck[4] * len(ops[k]["dur"]))]
                    else:
                        up, far = how == 1, (0, 0, 3, 10, 30)[int(luck[4] * 5)]
                        a, b = (max(0, where[k] - far), where[i]) if up else (where[k], min(M_ - 1, where[i] + far))
                        move, todo = set(), [i if up else k]
                        while todo and len(move) < 12:
                            m = todo.pop()
                            move.add(m)
                            todo += [x for x in (pre if up else nxt)[m] if a <= where.get(x, -1) <= b and x not in move]
                        if todo or (i in move and k in move) or min(move) < loads:
                            continue
                        new = part[:a] + [m for m in part[a:b + 1] if (m in move) == up] + [m for m in part[a:b + 1] if (m in move) != up] + part[b + 1:]
                    got = both(new, to, a, took - HEAT * (1.0 - n / POLISH) * math.log(1.0 - luck[5]))
                    if got:
                        part, on, took, tight = new, to, got[0], got[1]
                        where = {m: c for c, m in enumerate(part)}
                        if took <= best[0]:
                            best = (took, part, on)
                order, on = order[:c0] + best[1] + rest, best[2]
        took = lasts(order, on)[0]
        ORDER.extend((i, on[i]) for i in order)
        INFO.update(ops=ops, start=kept[0], done=kept[1], on=kept[2], took=took)

    known, total, waited, snap, token = {q: {} for q in queue}, {}, {}, {}, {}
    for i, q in ORDER:
        o = ops[i]
        sem = o["sem"]
        if o["q"] == "f":
            sem = q + "q_"
            o["call"] = lambda o=o, c=o["call"][q], sem=sem: c().then_inc(T.sem[sem], 1)
        if q is None:
            total[sem], token[i] = o["inc"], (sem, o["inc"])
            continue
        want = {}
        for m in o["wait"]:
            s, v = token[m]
            want[s] = max(want.get(s, 0), v)
        for s, v in sorted(want.items(), key=lambda kv: -kv[1]):
            if known[q].get(s, 0) >= v:
                continue
            queue[q].wait_ge(T.sem[s], v)
            waited[s] = max(waited.get(s, 0), v)
            known[q][s] = v
            for s2, v2 in snap.get((s, v), {}).items():
                known[q][s2] = max(known[q].get(s2, 0), v2)
        o["call"]()
        total[sem] = total.get(sem, 0) + 1 if not o["lat"] else o["inc"]
        token[i] = (sem, total[sem])
        seen = snap.setdefault(token[i], {})
        for s2, v2 in known[q].items():
            seen[s2] = max(seen.get(s2, 0), v2)
    for sem in sorted(total):
        if waited.get(sem, 0) < total[sem]:
            g.sync.wait_ge(T.sem[sem], total[sem])
